import numpy as np, ml_dtypes
CORES = [1,5,17,21,33,37,49,53]
N = 8
BF = ml_dtypes.bfloat16
W, V, L, F, B, TH, S, RO, SV = 3072, 1536, 256, 2, 4, 8, 4, 3, 6
def parts(rng):
    x = np.clip(rng.integers(0, 256, (N, 8, 1, W)) + rng.integers(-70, 71, (N, 8, 16, W)), 0, 255)
    q = np.clip(rng.integers(0, 200, (N, 8, 1, L)) + rng.integers(-70, 71, (N, 8, 16, L)), 0, 255)
    return x, q, rng.integers(0, W, (N, 8, W)), rng.integers(0, W, (N, 8, W)), rng.integers(0, V, (N, 8, W)), rng.integers(0, W, (N, 8, 16, V))
def pack(x, q, nx, pv, rc, u):
    return {"xd": np.ascontiguousarray(x.reshape(N, 128, W)).astype(np.float32).astype(BF), "nx": nx.astype(np.int32), "pv": pv.astype(np.int32), "rc": rc.astype(np.int32),
            "ul": np.ascontiguousarray(u.reshape(N, 128, V)).astype(np.int32), "mv": np.ascontiguousarray(q.reshape(N, 128, L)).astype(np.float32).astype(BF)}
def some(rng, n):
    return 255 * (np.argsort(rng.random((N, 8, 16, L)), axis=2) < n[:, :, None, :])
def setup_inputs(rng):
    return pack(*parts(rng))
def setup_inputs_corners(rng):
    x, q, nx, pv, rc, u = parts(rng); c = np.arange(W); sh = int(rng.integers(0, 8))
    x[..., ::64] = 255; x[..., 63::64] = 0; q[..., :8] = 0; q[..., L - 8:] = 255
    for r in range(N):
        for g in range(8):
            k = (g + 3 * r + sh) % 8
            if k == 0: nx[r, g] = c; pv[r, g] = c; rc[r, g] = c % V
            elif k == 1: nx[r, g] = np.minimum(c + 1, W - 1); pv[r, g] = np.maximum(c - 1, 0); rc[r, g] = V - 1 - c % V
            elif k == 2: nx[r, g] = (c + 1) % W; pv[r, g] = (c + W - 1) % W
            elif k == 3: nx[r, g] = 0; pv[r, g] = W - 1; rc[r, g] = V - 1
            elif k == 4: nx[r, g] = W - 1; pv[r, g] = 0; rc[r, g] = 0
            elif k == 5: u[r, g] = u[r, g, :1] + np.zeros((16, 1), np.int64)
            elif k == 6: u[r, g] = rng.choice(np.array([0, W - 1, W // 2]), (16, V))
            else: nx[r, g] = c ^ 1; pv[r, g] = c ^ 1
            if (g + r) % 2 == 0:
                z, p, e, t1, t2, t3 = [int(b) for b in 1 + rng.permutation(W - 2)[:6]]; xb, ub, i = x[r, g], u[r, g], int(rng.integers(0, 16))
                xb[:, [z, p]] = 0; xb[i, p] = 1; xb[:, [e, t1, t2, t3]] = 255; xb[i, e] = 254
                nx[r, g, [z, p, t1, t2, t3]] = z; pv[r, g, [z, t1, t3]] = t1; pv[r, g, [p, e, t2]] = t2
                ub[:, (L - 1) * SV] = p; ub[15, (L - 1) * SV] = z
                ub[:, (L - 2) * SV] = t3
                ub[:, SV] = t1; ub[15, SV] = e
    return pack(x, q, nx, pv, rc, u)
def setup_inputs_counts(rng):
    x, q, nx, pv, rc, u = parts(rng); x = np.clip(x, 1, 254)
    much = rng.permutation(np.array((256, 511, 1024, 8 * L - 1, 255, 257, 8 * L, 0)[:N]))
    hit = (np.argsort(rng.random((N, 8 * L)), axis=1) < much[:, None]).reshape(N, 8, L)
    n = np.where(hit, rng.integers(TH, 17, (N, 8, L)), rng.integers(0, TH, (N, 8, L)))
    return pack(x, some(rng, n), nx, pv, rc, u)
def setup_inputs_ends(rng):
    x = 255 * rng.integers(0, 2, (N, 8, 16, W)); m = rng.random((N, 8, 1, W)); x = np.where(m < 0.3, 0, np.where(m < 0.6, 255, x))
    fl = rng.integers(0, 2, (N, 8)); fl[0] = 0; fl[N - 1] = 0; f2 = rng.integers(0, 2, (N, 8))
    x[:, :, :, 0] = 255 * fl[:, :, None]; x[:, :, :, W - 1] = 255 * (1 - fl)[:, :, None]
    odd = (np.arange(8) % 2 == 1)[None, :, None]
    def far(hi, n):
        a = hi * rng.integers(0, 2, (N, 8, n))
        return np.where((rng.random((N, 8, n)) < 0.35) & odd, rng.integers(0, hi + 1, (N, 8, n)), a)
    nx = far(W - 1, W); pv = far(W - 1, W); rc = far(V - 1, W); u = far(W - 1, 16 * V).reshape(N, 8, 16, V)
    u[N - 1] = (W - 1) * rng.integers(0, 2, (8, 16, V)); nx[N - 1, :, 0] = 0; nx[N - 1, :, W - 1] = 0
    rc[:, :, 0] = (V - 1) * f2; rc[:, :, W - 1] = (V - 1) * (1 - f2)
    n = rng.choice(np.array([0, TH - 1, TH, 16]), (N, 8, L))
    n[0] = rng.choice(np.array([0, TH - 1, TH // 2]), (8, L)); n[N - 1] = rng.choice(np.array([16, TH]), (8, L))
    z = (L - 1) * SV; n[0, 7, L - 2:] = 0; n[N - 1, 7, L - 1] = 16
    u[0, 7, :, z] = W - 1; u[0, 7, :, z - SV] = W - 1; u[0, 7, 15, z - SV] = 0
    u[N - 1, 7, :, z] = W - 1; u[N - 1, 7, 15, z] = 0
    n[1, 7, L - 1] = 16; x[1, 7, :, 0] = 0; x[1, 7, :, 1] = 255; x[1, 7, :, 2] = 0; x[1, 7, :, W - 1] = 255
    nx[1, 7, 0] = W - 1; nx[1, 7, W - 1] = W - 1; nx[1, 7, 1] = 2; u[1, 7, :15, z] = 1; u[1, 7, 15, z] = 0
    return pack(x, some(rng, n), nx, pv, rc, u)
def setup_inputs_near(rng):
    x, q, nx, pv, rc, u = parts(rng); b = rng.integers(0, 255, (N, 8, 1, 1)); b[0, 0] = 0; b[1, 1] = 254
    x = b + (rng.random((N, 8, 16, W)) < rng.choice(np.array([0.2, 0.5, 0.8]), (N, 8, 1, W)))
    q = b + (rng.random((N, 8, 16, L)) < rng.choice(np.array([0.2, 0.5, 0.8, 1.0]), (N, 8, 1, L)))
    few = rng.integers(0, W, (N, 8, 64)); u = np.take_along_axis(few, rng.integers(0, 64, (N, 8, 16 * V)), 2).reshape(N, 8, 16, V)
    return pack(x, q, nx, pv, rc, u)
def setup_inputs_spread(rng):
    x = (np.exp2(8 * rng.random((N, 8, 1, W))) * rng.random((N, 8, 16, W))).astype(np.int64)
    q = (np.exp2(8 * rng.random((N, 8, 1, L))) * rng.random((N, 8, 16, L))).astype(np.int64)
    def skew(hi, n):
        return np.minimum((hi * rng.random((N, 8, n)) ** rng.choice(np.array([1, 2, 4]), (N, 8, 1))).astype(np.int64), hi - 1)
    return pack(np.minimum(x, 255), np.minimum(q, 255), skew(W, W), skew(W, W), skew(V, W), skew(W, 16 * V).reshape(N, 8, 16, V))
def check_inputs(d):
    bad = []
    for k, lo, hi in (("xd", 0, 255), ("nx", 0, W - 1), ("pv", 0, W - 1), ("rc", 0, V - 1), ("ul", 0, W - 1), ("mv", 0, 255)):
        a = np.asarray(d[k]).astype(np.float64)
        if not (np.min(a) >= lo and np.max(a) <= hi): bad.append("range of " + k)
        elif np.any(a != np.floor(a)): bad.append("whole numbers in " + k)
    return bad
def lowest(n):
    same = n[:, :, :, None] == n[:, :, None, :]
    return ~np.any(same & np.tril(np.ones((L, L), bool), -1), axis=3)
def reference(xd, nx, pv, rc, ul, mv):
    X = np.ascontiguousarray(xd.astype(np.float32).astype(np.int32).reshape(N, 8, 16, W).transpose(0, 1, 3, 2))
    q = np.ascontiguousarray(mv.astype(np.float32).astype(np.int32).reshape(N, 8, 16, L).transpose(0, 1, 3, 2))
    nxt, pre, rec = nx.astype(np.int64), pv.astype(np.int64), rc.astype(np.int64)
    U = ul.astype(np.int64).reshape(N, 8, 16, V); v = np.zeros((N, 8, L), np.int64) + SV * np.arange(L)
    R3, G3 = np.arange(N)[:, None, None], np.arange(8)[None, :, None]; R4, G4 = R3[..., None], G3[..., None]
    for t in range(RO):
        d = np.take_along_axis(U, v[:, :, None, :], 3)
        score = np.add.reduce(np.abs(X[R4, G4, d] - q[:, :, None]), axis=4)
        cleared = np.zeros(d.shape, bool); c = d
        for f in range(F):
            c = nxt[R4, G4, c]
            cleared = cleared | (np.add.reduce((X[R4, G4, c] < q[:, :, None]).astype(np.int32), axis=4) >= TH)
        none = np.all(cleared, axis=2)
        k = np.where(none, np.argmax(score, axis=2), np.argmin(np.where(cleared, 2 ** 20, score), axis=2))
        a = np.take_along_axis(d, k[:, :, None, :], 2)[:, :, 0]; go = np.ones(a.shape, bool)
        for s in range(B):
            b = pre[R3, G3, a]
            go = go & (np.add.reduce((X[R3, G3, b] < q).astype(np.int32), axis=3) < TH)
            a = np.where(go, b, a)
        w = rec[R3, G3, a]
        A = np.add.reduce(none.reshape(N, -1).astype(np.int32), axis=1) & 255
        z = (q + A[:, None, None, None]) >> 1
        xn = (X[R3, G3, a] + q + 1) >> 1; nn = nxt[R3, G3, nxt[R3, G3, a]]
        r, g, i = np.nonzero(lowest(v)); U[r, g, k[r, g, i], v[r, g, i]] = a[r, g, i]
        r, g, i = np.nonzero(lowest(a)); X[r, g, a[r, g, i]] = xn[r, g, i]; nxt[r, g, a[r, g, i]] = nn[r, g, i]
        v = w + 0; q = z + 0
        for h in range(1, S):
            s = 1 + (t + h - 1) % (N - 1)
            v[:, :, h::S] = np.roll(w, s, axis=0)[:, :, h::S]; q[:, :, h::S] = np.roll(z, s, axis=0)[:, :, h::S]
    return {"yu": U.reshape(N, 128, V).astype(np.float32), "yx": np.ascontiguousarray(X.transpose(0, 1, 3, 2)).reshape(N, 128, W).astype(np.float32).astype(BF),
            "yv": v.astype(np.float32), "yq": np.ascontiguousarray(q.transpose(0, 1, 3, 2)).reshape(N, 128, L).astype(np.float32).astype(BF)}

@@ -1,0 +1,497 @@
+from concourse.mybir import AluOpType, AxisListType, ActivationFunctionType
+
+OP, AF = AluOpType, ActivationFunctionType
+NR = 3
+BIG = 131072.0
+SHARE = ((3, 0), (3, 1))
+SBANK = ("P4", "P5", "P3", "P6")
+
+SCRATCH = {}
+
+
+def _buf(dtype, **names):
+    for k, n in names.items():
+        SCRATCH[k] = ("sbuf", [128, n], dtype)
+
+
+_buf("bfloat16", X=3328, X1=3072, X2=3072, TT=15360, ZZ=3072, NXR=3328, BHB=768, BLB=768, Q16=4096, QW=1024,
+     DF=4096, AB=4096, L1=4096, L2=4096, LW=1024, XG=2048, EA=2176, EV=2176, EW=2176, NFB=16, E16=16)
+_buf("int32", ULI=1536, B4=768, BHI=768, BLI=768, KI=16, I192=192, I16=16, IJL=16, I32=32, I64=64, IQ4=64)
+_buf("uint16", NXL=192, PVL=192, C64=64, Q4L=64, DL=256, BLU=64)
+_buf("float16", DI=256, OHD=256, OHA=256, AR16=256, UH=144, IDH=128, IDMH=128)
+_buf("float32", ULF=1792, IN144=144, IG16=128)
+for _t in range(NR + 1):
+    SCRATCH["QJ%d" % _t] = ("sbuf", [128, 256], "bfloat16")
+    SCRATCH["VL%d" % _t] = ("sbuf", [128, 32], "uint16")
+    if _t < NR:
+        SCRATCH["ZB%d" % _t] = ("sbuf", [128, 256], "bfloat16")
+        SCRATCH["MW%d" % _t] = ("sbuf", [128, 32], "uint16")
+for _k in range(8):
+    SCRATCH["P%d" % _k] = ("psum", [128, 512], "float32")
+_PACK, _WIDTH = {}, {}
+for _w, _names, _dt, _n, _u in (
+        ("sm", "IP P16 G16 F2 R4 RM G15 G12 C192 C96 C16 CQ WA WW WP W3 T1 T2 NRED AM NP", "float32", 8, 1),
+        ("ci", "IPI PI F2I R4I RMI NI", "int32", 8, 1),
+        ("lu", "QIL IJU KU AU O2 AU2 OFA OFV VPU N1U", "uint16", 16, 16),
+        ("lf", "DUA DUV IDU IDV A0F AC A2F OM NV VF OMV YV", "float32", 16, 16),
+        ("mat", "U U16 UC UA UW UP U3", "bfloat16", 144, 144),
+        ("sq", "BB BB4 TR RA ONE CB CZ IDP IDM CM4", "bfloat16", 128, 128),
+        ("ff", "K16 KB2 DB D0 MK KB W1 W2 KEY CM CS CMV CSV UV", "float32", 256, 256),
+        ("bb", "QM QI1 QI2 FB GB VJ VG N1B NNB ON KPB", "bfloat16", 256, 256),
+        ("ii", "RI ZI XI XS", "int32", 256, 256),
+        ("fs", "IS64 DW DS N5 S1 S2", "float32", 64, 64)):
+    for _j, _nm in enumerate(_names.split()):
+        _PACK[_nm] = (_w, _j * _n)
+        _WIDTH[_nm] = _u
+    SCRATCH[_w] = ("sbuf", [128, _n * len(_names.split())], _dt)
+
+NDMA = 40
+SEMAPHORES = ["qV", "qS", "qP", "qG", "sent"] + ["d%d" % _k for _k in range(NDMA)]
+for _t in range(NR):
+    for _h in range(1, 4):
+        SEMAPHORES += ["z%d%d" % (_t, _h), "w%d%d" % (_t, _h)]
+
+
+def shift(t, h):
+    return 1 + (t + h - 1) % 7
+
+
+def rank_program(g, core, T, topo):
+    me = T.rank_of(core)
+    if me is None:
+        return
+    N = len(T.cores)
+    ENG = {"V": g.vector, "S": g.scalar, "P": g.tensor, "G": g, "sync": g.sync, "act": g.scalar}
+    cnt = {"V": 0, "S": 0, "P": 0, "G": 0}
+    know = {"V": {}, "S": {}, "P": {}, "G": {}, "sync": {}}
+    snap = {}
+    unit = {"V": 1, "S": 1, "P": 1, "G": 1}
+    total = {}
+    log = {}
+    nd = [0]
+    sent = [0]
+
+    def v(name, lo=0, hi=None, step=1):
+        w, b = _PACK.get(name, (name, 0))
+        if hi is None: hi = _WIDTH[name] if name in _PACK else T[w].shape[1]
+        lo, hi = lo + b, hi + b
+        ap = T[w][:, lo:hi:step] if step != 1 else T[w][:, lo:hi]
+        return (ap, [(w, lo, hi, step, None)], [])
+
+    def rows(name, f, lo, hi):
+        return (T[name][f:128:16, lo:hi], [(name, lo, hi, 1, f)], [])
+
+    def ind(win, off):
+        return (win[0].indirect(off[0]), win[1], off[1])
+
+    def order(q, w, r):
+        need = {}
+        def dep(tok):
+            if tok[0] == q == "P": return
+            if know[q].get(tok[0], 0) < tok[1]: need[tok[0]] = max(need.get(tok[0], 0), tok[1])
+        for keys, wr in ((w, True), (r, False)):
+            for (nm, lo, hi, stp, prt) in keys:
+                ps = nm[0] == "P" and nm[1:].isdigit()
+                for (l2, h2, kind, tok, s2, p2) in log.get(nm, []):
+                    if ps:
+                        if tok[0] != q or (kind == "w" and not wr): dep(tok)
+                    elif l2 < hi and lo < h2 and (kind == "w" or wr):
+                        if prt is not None and p2 is not None and prt != p2: continue
+                        if stp == s2 and stp > 1 and (lo - l2) % stp: continue
+                        dep(tok)
+        for a in sorted(need):
+            if any(b != a and snap.get((b, need[b]), {}).get(a, 0) >= need[a] for b in need): continue
+            ENG[q].wait_ge(T.sem["q" + a if a in cnt else a], need[a] * unit[a])
+        for a in need:
+            for b, n in snap.get((a, need[a]), {}).items(): know[q][b] = max(know[q].get(b, 0), n)
+            know[q][a] = max(know[q].get(a, 0), need[a])
+
+    def note(tok, w, r):
+        for keys, kind in ((w, "w"), (r, "r")):
+            for (nm, lo, hi, stp, prt) in keys:
+                ps = nm[0] == "P" and nm[1:].isdigit()
+                if ps: lo, hi = 0, 512
+                L = log.setdefault(nm, [])
+                if ps and kind == "r":
+                    L[:] = [e for e in L if e[2] == "w" and e[3][0] == "P"][-1:] + [(lo, hi, "r", tok, 1, None)]
+                else:
+                    if kind == "w" and stp == 1 and prt is None: L[:] = [e for e in L if not (lo <= e[0] and e[1] <= hi)]
+                    L.append((lo, hi, kind, tok, stp, prt))
+
+    def emit(q, fn, outs, ins):
+        w, r = [], []
+        for o in outs: w += o[1]; r += o[2]
+        for i in ins: r += i[1] + i[2]
+        order(q, w, r)
+        cnt[q] += 1
+        fn().then_inc(T.sem["q" + q], 1)
+        now = dict(know[q]); now[q] = cnt[q]
+        snap[(q, cnt[q])] = now
+        note((q, cnt[q]), w, r)
+
+    def dma(out, in_, q="sync"):
+        qk = {"sync": "sync", "act": "S"}[q]
+        w = out[1] if isinstance(out, tuple) else []
+        r = in_[1] if isinstance(in_, tuple) else []
+        order(qk, w, r)
+        nm = "d%d" % nd[0]; nd[0] += 1
+        o = out[0] if isinstance(out, tuple) else out
+        i = in_[0] if isinstance(in_, tuple) else in_
+        ENG[q].dma_start(o, i).then_inc(T.sem[nm], 16)
+        unit[nm] = 16; total[nm] = 1
+        snap[(nm, 1)] = dict(know[qk])
+        note((nm, 1), w, r)
+
+    def remote(kind, t, h, dst_view, src_view):
+        d = T.cores[(me + shift(t, h)) % N]
+        order("G", [], src_view[1])
+        rid, pid, _s = topo.addr(d)
+        es = topo.engines(core, d)[:8]
+        nm = "%s%d%d" % (kind, t, h)
+        g.remote_dma(dst_view[0], src_view[0], T.sem[nm], T.sem.sent, pid, rid, sum(1 << e for e in es))
+        sent[0] += len(es)
+        src = T.cores[(me - shift(t, h)) % N]
+        unit[nm] = len(topo.engines(src, core)[:8]); total[nm] = 1
+        snap[(nm, 1)] = {}
+        note((nm, 1), dst_view[1], [])
+
+    def cp(o, i): emit("V", lambda: g.vector.tensor_copy(o[0], i[0]), [o], [i])
+    def tt(o, a, b, op): emit("V", lambda: g.vector.tensor_tensor(o[0], a[0], b[0], op), [o], [a, b])
+    def ts(o, a, s1, op0, s2=None, op1=None):
+        ex = [s for s in (s1, s2) if isinstance(s, tuple)]
+        x1 = s1[0] if isinstance(s1, tuple) else s1
+        x2 = s2[0] if isinstance(s2, tuple) else s2
+        if op1 is None: emit("V", lambda: g.vector.tensor_scalar(o[0], a[0], x1, None, op0), [o], [a] + ex)
+        else: emit("V", lambda: g.vector.tensor_scalar(o[0], a[0], x1, x2, op0, op1), [o], [a] + ex)
+    def scan(o, d0, d1, init, op0, op1): emit("V", lambda: g.vector.tensor_tensor_scan(o[0], d0[0], d1[0], init, op0, op1), [o], [d0, d1])
+    def rsum(o, i): emit("V", lambda: g.vector.tensor_reduce(o[0], i[0], AxisListType.X, OP.add), [o], [i])
+    def fill(o, c): emit("V", lambda: g.vector.memset(o[0], c), [o], [])
+    def act(o, i, f=AF.Identity, bias=0.0, scale=1.0):
+        ex = [s for s in (bias, scale) if isinstance(s, tuple)]
+        b = bias[0] if isinstance(bias, tuple) else bias
+        s = scale[0] if isinstance(scale, tuple) else scale
+        emit("S", lambda: g.scalar.activation(o[0], i[0], f, bias=b, scale=s), [o], [i] + ex)
+    def mm(o, l, r, start, stop): emit("P", lambda: g.tensor.matmul(o[0], l[0], r[0], start, stop), [o], [l, r])
+    def iota(o, pat, base=0, cm=0, small=True):
+        if small: emit("G", lambda: g.iota(o[0], pat, base, cm, allow_small_or_imprecise_dtypes=True), [o], [])
+        else: emit("G", lambda: g.iota(o[0], pat, base, cm), [o], [])
+    def keep(o, i, pat, op, base, cm): emit("G", lambda: g.affine_select(o[0], i[0], pat, op, 0.0, base, cm), [o], [i])
+    def usl(name, r): return v(name, 15 - r, 143 - r)
+
+    def diag(bank, mat, src, n):
+        for r in range(16):
+            mm(v(bank, 0, n), usl(mat, r), v(src, r, 16 * n, 16), r == 0, r == 15)
+
+    dma(v("B4", 576, 768), T.nx[:])
+    dma(v("B4", 384, 576), T.pv[:], "act")
+    dma(v("QM"), T.mv[:])
+    dma(v("ULI"), T.ul[:])
+    dma(v("X", 0, 3072), T.xd[:], "act")
+    dma(v("B4", 192, 384), T.rc[:])
+
+    fill(v("NXR", 0, 3072), 0.0)
+    fill(v("ON"), 1.0)
+    iota(v("IPI"), [[1, 1]], 0, 1, False)
+    iota(v("IP"), [[1, 1]], 0, 1)
+    iota(v("IN144"), [[1, 144]])
+    iota(v("IJL"), [[1, 4], [4, 4]], 0, 0, False)
+    iota(v("I64"), [[1, 64]], 0, 0, False)
+    iota(v("I32"), [[6, 4], [24, 8]], 0, 0, False)
+    iota(v("I192"), [[1, 192]], 0, 0, False)
+    iota(v("K16"), [[0, 16], [1, 16]])
+    iota(v("IG16"), [[16, 8], [0, 16]])
+    iota(v("I16"), [[1, 16]], 0, 0, False)
+    iota(v("IQ4"), [[16, 4], [64, 4], [4, 4]], 0, 0, False)
+    iota(v("IDU"), [[16, 16]], 3072, 0)
+    iota(v("IDV"), [[16, 16]], 1536, 0)
+    iota(v("IS64"), [[0, 16], [1, 4]])
+    keep(v("IDP"), v("ON", 0, 128), [[-1, 128]], OP.is_equal, 0, 1)
+    iota(v("ZZ"), [[0, 3072]])
+
+    def halves(lo, hi):
+        ts(v("BHI", lo, hi), v("B4", lo, hi), 6, OP.arith_shift_right)
+        ts(v("BLI", lo, hi), v("B4", lo, hi), 63, OP.bitwise_and)
+        cp(v("BHB", lo, hi), v("BHI", lo, hi))
+        cp(v("BLB", lo, hi), v("BLI", lo, hi))
+
+    def weights(nm, k):
+        ts(v("T1"), v("P16"), k, OP.is_equal, 64.0, OP.mult)
+        ts(v("T2"), v("P16"), k + 1, OP.is_equal)
+        tt(v(nm), v("T1"), v("T2"), OP.add)
+
+    def spread(t, hs):
+        for h in hs:
+            act(v("Q16", 1024 * h, 1024 * h + 1024), ind(v("QJ%d" % t, 64 * h, 64 * h + 64), v("C64")))
+
+    ts(v("PI"), v("IPI"), 15, OP.bitwise_and)
+    cp(v("P16"), v("PI"))
+    ts(v("C16"), v("P16"), 16.0, OP.mult)
+    ts(v("IJU"), v("IJL"), v("C16"), OP.add)
+    cp(v("C64"), v("I64"))
+    halves(576, 768)
+    dma(rows("NXR", 0, 0, 3072), v("BHB", 576, 768))
+    dma(rows("NXR", 1, 0, 3072), v("BLB", 576, 768))
+    weights("WA", 0.0)
+    tt(v("G16"), v("IP"), v("P16"), OP.subtract)
+    ts(v("G15"), v("G16"), 15.0, OP.add)
+    ts(v("U"), v("IN144"), v("G15"), OP.is_equal)
+    act(v("QJ0"), ind(v("QM"), v("IJU")))
+    act(v("UA"), v("U"), scale=v("WA"))
+    ts(v("C96"), v("P16"), 96.0, OP.mult)
+    ts(v("VL0"), v("I32"), v("C96"), OP.add)
+    fill(v("TT", 0, 3072), 0.0)
+    halves(384, 576)
+    dma(rows("TT", 4, 0, 3072), v("BHB", 384, 576))
+    dma(rows("TT", 5, 0, 3072), v("BLB", 384, 576))
+    weights("WP", 4.0)
+    spread(0, range(1))
+    act(v("UP"), v("U"), scale=v("WP"))
+    spread(0, range(1, 3))
+    diag("P3", "UA", "NXR", 192)
+    diag("P7", "UP", "TT", 192)
+
+    def consts2():
+        ts(v("C192"), v("P16"), 192.0, OP.mult)
+        ts(v("B4", 0, 192), v("I192"), v("C192"), OP.add)
+        halves(0, 384)
+        for k in range(2):
+            dma(rows("TT", 2 * k, 0, 3072), v("BHB", 192 * k, 192 * k + 192))
+            dma(rows("TT", 2 * k + 1, 0, 3072), v("BLB", 192 * k, 192 * k + 192))
+        weights("WW", 2.0)
+        ts(v("NP"), v("P16"), -1.0, OP.mult)
+        ts(v("IDM"), v("IDP"), -1.0, OP.mult)
+        act(v("U16"), v("U"), scale=16.0)
+        act(v("UC"), v("U"), scale=1048576.0)
+        act(v("KPB"), v("K16"))
+        fill(v("CB"), -61440.0)
+        cp(v("PVL"), v("P7", 0, 192))
+
+    def late_consts():
+        act(v("UW"), v("U"), scale=v("WW"))
+        act(v("D0"), v("K16"), AF.Sign)
+        act(v("DB"), v("D0"), scale=-524288.0, bias=524288.0)
+        act(v("KB2"), v("K16"), scale=2.0, bias=BIG)
+        act(v("MK"), v("K16"), AF.Square, bias=v("NP"))
+        act(v("MK"), v("MK"), AF.Relu, scale=-1.0, bias=1.0)
+        act(v("DS"), v("IS64"), AF.Sign)
+        act(v("DW"), v("DS"), scale=-3072.0, bias=3072.0)
+        act(v("DUA"), v("IDU"), bias=v("P16"))
+        act(v("DUV"), v("IDV"), bias=v("P16"))
+        ts(v("R4I"), v("PI"), 2, OP.arith_shift_right)
+        ts(v("F2I"), v("PI"), 1, OP.arith_shift_right)
+        ts(v("RMI"), v("PI"), 3, OP.bitwise_and)
+        cp(v("R4"), v("R4I"))
+        cp(v("F2"), v("F2I"))
+        cp(v("RM"), v("RMI"))
+        cp(v("UH"), v("U"))
+        cp(v("IDH"), v("IDP"))
+        ts(v("IDMH"), v("IDP"), -1.0, OP.mult)
+        ts(v("T1"), v("F2"), -2.0, OP.mult, v("P16"), OP.add)
+        ts(v("T1"), v("T1"), -63.0, OP.mult, 64.0, OP.add)
+        ts(v("W3"), v("P16"), 8.0, OP.is_lt, v("T1"), OP.mult)
+        tt(v("G12"), v("G16"), v("F2"), OP.add)
+        ts(v("G12"), v("G12"), 12.0, OP.add)
+        ts(v("U3"), v("IN144"), v("G12"), OP.is_equal, v("W3"), OP.mult)
+        ts(v("BB"), v("IG16"), v("G16"), OP.is_equal)
+        act(v("BB4"), v("BB"), scale=4096.0)
+        act(v("RA"), v("BB"), scale=v("WA"))
+        keep(v("TR"), v("BB4"), [[1, 128]], OP.is_gt, 0, -1)
+        fill(v("ONE"), 1.0)
+        fill(v("CZ"), 0.0)
+        fill(v("CM4"), -1.0 / 4096)
+        ts(v("E16"), v("IN144", 0, 16), v("P16"), OP.is_equal)
+        ts(v("Q4L"), v("IQ4"), v("R4"), OP.add)
+        ts(v("CQ"), v("RM"), 64.0, OP.mult)
+        ts(v("T1"), v("R4"), 16.0, OP.mult)
+        tt(v("CQ"), v("CQ"), v("T1"), OP.add)
+        ts(v("QIL"), v("I16"), v("CQ"), OP.add)
+
+    def table(q, m):
+        o, w = v("TT", 3072 * m, 3072 * m + 3072), v("TT", 3072 * m - 3072, 3072 * m)
+        if q == "V": cp(o, ind(w, v("PVL")))
+        else: act(o, ind(w, v("PVL")))
+        for f in range(2):
+            dma(rows("ZZ", 2 * m - 2 + f, 0, 3072), rows("TT", f, 3072 * m, 3072 * m + 3072))
+
+    def lane_q(t):
+        act(v("QW"), ind(v("QJ%d" % t), v("Q4L")))
+        act(v("QI%d" % (1 + t % 2)), ind(v("QJ%d" % t), v("QIL")), bias=1.0)
+
+    def eo(p): return 256 * p - 8 * p * (p - 1)
+
+    def dedupe_mm(bank, e, ps):
+        for p in ps:
+            if p == 0: mm(v(bank, 0, 256), v("CZ"), v("ON"), True, False)
+            if p < 15: mm(v(bank, 16 * p + 16, 256), v("BB4"), v(e, eo(p) + 16, eo(p + 1)), False, False)
+            mm(v(bank, 16 * p, 16 * p + 16), v("TR"), v(e, eo(p), eo(p) + 16), False, p == 15)
+
+    def dedupe_off(bank, cm, cs, om, dump, num, off):
+        tt(v(cm), v(bank, 0, 256), v("MK"), OP.mult)
+        scan(v(cs), v("D0"), v(cm), 0.0, OP.mult, OP.add)
+        tt(v(om), v(cs, 15, 256, 16), v(dump), OP.min)
+        tt(v(off), v(om), v(num), OP.max)
+
+    def test(x, out, h, op, n=1024):
+        tt(v(out, 1024 * h, 1024 * h + n), ind(v(x, 0, 3072), v("DL", 64 * h, 64 * h + n // 16)), v("Q16", 1024 * h, 1024 * h + n), op)
+
+    def sums(bank, mat, src, h, last):
+        for c in range(4):
+            mm(v(bank, 0, 256), usl(mat, 4 * c + h), v(src, 1024 * h + 256 * c, 1024 * h + 256 * c + 256), False, last and c == 3)
+
+    for t in range(NR):
+        Q, Qn, VLt, Vn = "QJ%d" % t, "QJ%d" % (t + 1), "VL%d" % t, "VL%d" % (t + 1)
+        first, lastr = t == 0, t == NR - 1
+        UT = v("ULI") if first else v("ULF", 0, 1536)
+
+        def places(h): cp(v("DL", 64 * h, 64 * h + 64), ind(UT, v(VLt, 8 * h, 8 * h + 4)))
+        places(0)
+        test("X", "DF", 0, OP.subtract)
+        if first: cp(v("NXL"), v("P3", 0, 192))
+        act(v("X1"), ind(v("X", 0, 3072), v("NXL")))
+        if first: spread(0, range(3, 4))
+        act(v("X2"), ind(v("X1"), v("NXL")))
+        for h in range(1, 4):
+            places(h)
+            n = 1024 - 512 * len([1 for x in SHARE if x[0] == h])
+            if n: test("X", "DF", h, OP.subtract, n)
+        if first:
+            consts2()
+            late_consts()
+            table("V", 1)
+            table("V", 2)
+        for h in range(4):
+            act(v("VJ", 64 * h, 64 * h + 64), ind(v("TT", 0, 3072), v(VLt, 8 * h, 8 * h + 4)))
+        for r in [4 * c + k for k in range(4) for c in range(4)]:
+            b = 64 * (r % 4) + 16 * (r // 4)
+            mm(v("P7", 0, 16), usl("UA", r), v("VJ", b, b + 16), r == 0, r == 15)
+        for j, (h, k) in enumerate(SHARE):
+            act(v("XG", 512 * j, 512 * j + 512), ind(v("X", 0, 3072), v("DL", 64 * h + 32 * k, 64 * h + 32 * k + 32)))
+        for h in range(4):
+            n = 1024 - 512 * len([1 for x in SHARE if x[0] == h])
+            if n: act(v("AB", 1024 * h, 1024 * h + n), v("DF", 1024 * h, 1024 * h + n), AF.Abs)
+        mm(v("P1", 0, 256), v("CB"), v("ON"), True, False)
+        mm(v("P2", 0, 256), v("CB"), v("ON"), True, False)
+        mm(v("P0", 0, 256), v("IDP"), v("KPB"), True, False)
+        for h in range(4):
+            test("X1", "L1", h, OP.is_lt)
+            sums("P1", "UC", "L1", h, h == 3)
+            if h == 1:
+                for j, (hs, k) in enumerate(SHARE):
+                    mm(v(SBANK[j]), v("IDP"), v("XG", 512 * j, 512 * j + 512), True, False)
+                    mm(v(SBANK[j]), v("IDM"), v("Q16", 1024 * hs + 512 * k, 1024 * hs + 512 * k + 512), False, True)
+                for j, (hs, k) in enumerate(SHARE):
+                    act(v("AB", 1024 * hs + 512 * k, 1024 * hs + 512 * k + 512), v(SBANK[j]), AF.Abs)
+        cp(v("VPU"), v("P7", 0, 16))
+        act(v("VF"), v("P7", 0, 16))
+        act(v("NV"), v("P7", 0, 16), scale=-1.0)
+        act(v("VG"), ind(v("TT", 0, 3072), v("VPU")))
+        for h in range(4):
+            sums("P0", "U16", "AB", h, h == 3)
+        mm(v("P6", 0, 256), v("RA"), v("VG"), True, True)
+        if first:
+            lane_q(0)
+            table("S", 3)
+            table("S", 4)
+        for h in range(2):
+            test("X2", "L2", h, OP.is_lt)
+            sums("P2", "UC", "L2", h, False)
+        test("X2", "L2", 2, OP.is_lt)
+        sums("P2", "UC", "L2", 2, False)
+        for p in range(16):
+            act(v("EV", eo(p), eo(p + 1)), v("P6", 16 * p, 256), AF.Square, bias=v("NV", p, p + 1))
+        act(v("EW"), v("EV"), AF.Relu, scale=-1.0, bias=1.0)
+        test("X2", "L2", 3, OP.is_lt)
+        sums("P2", "UC", "L2", 3, True)
+        ts(v("DI"), ind(UT, v("VPU")), -1536.0, OP.add)
+        tt(v("KB"), v("KB2"), v("P0", 0, 256), OP.subtract)
+        tt(v("W1"), v("P1", 0, 256), v("KB"), OP.min)
+        tt(v("P4", 0, 256), v("W1"), v("P0", 0, 256), OP.max)
+        tt(v("W2"), v("P2", 0, 256), v("KB"), OP.min)
+        tt(v("KEY"), v("W2"), v("P4", 0, 256), OP.max)
+        scan(v("RI"), v("DB"), v("KEY"), 1000000.0, OP.add, OP.min)
+        ts(v("KI"), v("RI", 15, 256, 16), 15, OP.bitwise_and)
+        cp(v("KU"), v("KI"))
+        tt(v("OHD"), ind(v("E16"), v("KU")), v("DI"), OP.mult)
+        diag("P3", "UH", "OHD", 16)
+        ts(v("NFB"), v("RI", 15, 256, 16), 65536.0, OP.is_ge)
+        mm(v("P1", 0, 16), v("ONE"), v("NFB"), True, False)
+        mm(v("P1", 0, 16), v("CM4"), v("ON", 0, 16), False, True)
+        if first: cp(v("ULF", 0, 1536), v("ULI"))
+        ts(v("AU"), v("P3", 0, 16), 1536.0, OP.add)
+        cp(v("FB"), ind(v("ZZ"), v("AU")))
+        for ch in range(4):
+            for r4 in range(4):
+                b = 64 * ch + 16 * r4
+                mm(v("P4", ch, 64, 4), v("U3", 12 - 4 * r4, 140 - 4 * r4), v("FB", b, b + 16), r4 == 0, r4 == 3)
+        rsum(v("NRED"), v("P1", 0, 16))
+        ts(v("NI"), v("NRED"), 1.0 / 256, OP.mult, -127.0 / 256, OP.add)
+        ts(v("AM"), v("NI"), -256.0, OP.mult, v("NRED"), OP.add)
+        ts(v("A0F"), v("P3", 0, 16), 1536.0, OP.add)
+        ts(v("ZI"), v(Q), v("AM"), OP.add, 0.5, OP.mult)
+        cp(v("BLU"), v("P4", 0, 64))
+        for k in range(2):
+            tt(v("LW", 512 * k, 512 * k + 512), ind(v("X", 0, 3072), v("BLU", 32 * k, 32 * k + 32)), v("QW", 512 * k, 512 * k + 512), OP.is_lt)
+            for r in range(8 * k, 8 * k + 8):
+                mm(v("P5", 0, 64), usl("U", r), v("LW", 64 * r, 64 * r + 64), r == 0, r == 15)
+        cp(v("ZB%d" % t), v("ZI"))
+        for h in range(1, 4):
+            remote("z", t, h, v(Qn, 64 * h, 64 * h + 64), v("ZB%d" % t, 64 * h, 64 * h + 64))
+        act(v(Qn, 0, 64), v("ZB%d" % t, 0, 64))
+        if not lastr: spread(t + 1, range(1))
+        ts(v("N5"), v("P5", 0, 64), 7.5, OP.is_lt, 3072.0, OP.mult)
+        scan(v("S1"), v("DW"), v("N5"), 0.0, OP.max, OP.min)
+        scan(v("S2"), v("DS"), v("S1"), 0.0, OP.mult, OP.add)
+        tt(v("O2"), v("S2", 3, 64, 4), v("A0F"), OP.add)
+        cp(v("GB"), ind(v("TT"), v("O2")))
+        for p in range(16):
+            mm(v("P6", 0, 16), usl("UW", p), v("GB", 16 * p, 16 * p + 16), p == 0, p == 15)
+        diag("P7", "UA", "GB", 16)
+        mm(v("P4", 0, 256), v("RA"), v("GB"), True, True)
+        for h in range(1, 4):
+            cp(v("MW%d" % t, 8 * h, 8 * h + 4), v("P6", h, 16, 4))
+            remote("w", t, h, v(Vn, 8 * h, 8 * h + 4), v("MW%d" % t, 8 * h, 8 * h + 4))
+        cp(v(Vn, 0, 4), v("P6", 0, 16, 4))
+        cp(v("AU2"), v("P7", 0, 16))
+        ts(v("AC"), v("P7", 0, 16), -1536.0, OP.add)
+        act(v("A2F"), v("P7", 0, 16))
+        ts(v("AR16"), v("P4", 0, 256), -1536.0, OP.add)
+        if not lastr:
+            act(v("N1B"), ind(v("NXR", 0, 3072), v("AU2")))
+            diag("P6", "UA", "N1B", 16)
+        for p in range(16):
+            ts(v("EA", eo(p), eo(p + 1)), v("AR16", 16 * p, 256), v("AC", p, p + 1), OP.is_equal)
+            dedupe_mm("P5", "EA", range(p, p + 1))
+            if p == 9 and not lastr:
+                cp(v("N1U"), v("P6", 0, 16))
+                act(v("NNB"), ind(v("NXR", 0, 3072), v("N1U")))
+                spread(t + 1, range(1, 4))
+        dedupe_mm("P0", "EW", range(16))
+        tt(v("XI"), ind(v("X", 0, 3072), v("AU2")), v("QI%d" % (1 + t % 2)), OP.add)
+        ts(v("XS"), v("XI"), 1, OP.arith_shift_right)
+        tt(v("OHA"), ind(v("E16"), v("KU")), v("AR16"), OP.mult)
+        mm(v("P7", 0, 256), v("IDH"), v("DI"), True, False)
+        mm(v("P7", 0, 256), v("IDMH"), v("OHD"), False, False)
+        mm(v("P7", 0, 256), v("IDH"), v("OHA"), False, True)
+        act(v("UV"), v("P7", 0, 256), bias=1536.0)
+        if not lastr: lane_q(t + 1)
+        dedupe_off("P5", "CM", "CS", "OM", "DUA", "A2F", "OFA")
+        if not lastr:
+            cp(ind(v("NXR"), v("OFA")), v("NNB"))
+            diag("P3", "UA", "NXR", 192)
+        cp(ind(v("X"), v("OFA")), v("XS"))
+        if lastr: dma(T.yx[:], v("X", 0, 3072), "act")
+        dedupe_off("P0", "CMV", "CSV", "OMV", "DUV", "VF", "OFV")
+        cp(ind(v("ULF"), v("OFV")), v("UV"))
+        if not lastr: cp(v("NXL"), v("P3", 0, 192))
+        if lastr: dma(T.yu[:], v("ULF", 0, 1536))
+    VE, QE = "VL%d" % NR, "QJ%d" % NR
+    act(v("QI1"), ind(v(QE), v("QIL")))
+    dma(T.yq[:], v("QI1"), "act")
+    for h in range(4):
+        cp(v("YV", h, 16, 4), v(VE, 8 * h, 8 * h + 4))
+    dma(T.yv[:], v("YV"))
+    for q in ("V", "S", "P", "G"):
+        g.wait_ge(T.sem["q" + q], cnt[q])
+    for nm in sorted(total):
+        g.wait_ge(T.sem[nm], unit[nm])
+    g.wait_ge(T.sem.sent, sent[0])

@@ -1,55 +1,60 @@
-from concourse.mybir import AluOpType, AxisListType, ActivationFunctionType
+from concourse.bass import DstId, RemoteDMATransfer
+from concourse.mybir import AluOpType, ActivationFunctionType
 
 OP, AF = AluOpType, ActivationFunctionType
 NR = 3
-BIG = 131072.0
-SHARE = ((3, 0), (3, 1))
-SBANK = ("P4", "P5", "P3", "P6")
+BIG = 131102.0
+OFF = 1536.0
+A = slice(None)
+H4 = slice(0, 4)
 
 SCRATCH = {}
 
 
 def _buf(dtype, **names):
     for k, n in names.items():
-        SCRATCH[k] = ("sbuf", [128, n], dtype)
+        SCRATCH[k] = ("sbuf", [128] + (list(n) if isinstance(n, tuple) else [n]), dtype)
 
 
-_buf("bfloat16", X=3328, X1=3072, X2=3072, TT=15360, ZZ=3072, NXR=3328, BHB=768, BLB=768, Q16=4096, QW=1024,
-     DF=4096, AB=4096, L1=4096, L2=4096, LW=1024, XG=2048, EA=2176, EV=2176, EW=2176, NFB=16, E16=16)
-_buf("int32", ULI=1536, B4=768, BHI=768, BLI=768, KI=16, I192=192, I16=16, IJL=16, I32=32, I64=64, IQ4=64)
-_buf("uint16", NXL=192, PVL=192, C64=64, Q4L=64, DL=256, BLU=64)
-_buf("float16", DI=256, OHD=256, OHA=256, AR16=256, UH=144, IDH=128, IDMH=128)
-_buf("float32", ULF=1792, IN144=144, IG16=128)
+_buf("bfloat16", X=3328, X1=3072, X2=3072, NXR=3328, BHB=192, BLB=192, QA=1024, QB=1024, DF=2048, AB=4096, L1=4096, L2=4096,
+     LW=1024, XG=2048, EA=2560, E16=16, SG=16, G6=96, WI=96)
+for _c in range(4):
+    for _e in ("EV", "EW"):
+        _buf("bfloat16", **{"%s%d" % (_e, _c): (4, 4, 4 - _c, 16)})
+_buf("int32", ULI=1536, PW=3072, W1=3072, NXN=192, PVN=192, P2N=192, IDN=192, BHI=192, BLI=192, KI=16, RI=256)
+_buf("uint16", NXL=192, PVL=192, P2L=192, Q4L=64, DL=256, BLU=64)
+_buf("float16", DI=256, OHD=256, FB=256, GC=512, VG=256, AR=256, AR2=256, XH=256, ZH=256, NH=384, TN=384, VH=16, NI=8,
+     TD=(4, 2, 2, 16), TF=(4, 2, 2, 16), VR=(4, 4, 16))
+_buf("float32", ULF=1792, IN160=160, IG16=128, I64=64, I192=192, DE=96, SH=96)
 for _t in range(NR + 1):
     SCRATCH["QJ%d" % _t] = ("sbuf", [128, 256], "bfloat16")
     SCRATCH["VL%d" % _t] = ("sbuf", [128, 32], "uint16")
     if _t < NR:
         SCRATCH["ZB%d" % _t] = ("sbuf", [128, 256], "bfloat16")
-        SCRATCH["MW%d" % _t] = ("sbuf", [128, 32], "uint16")
+        SCRATCH["MW%d" % _t] = ("sbuf", [128, 16], "uint16")
 for _k in range(8):
-    SCRATCH["P%d" % _k] = ("psum", [128, 512], "float32")
+    SCRATCH["P%d" % _k] = ("psum", [128, 512] if _k in (3, 4, 7) else [128, 8, 4, 16], "float32")
 _PACK, _WIDTH = {}, {}
 for _w, _names, _dt, _n, _u in (
-        ("sm", "IP P16 G16 F2 R4 RM G15 G12 C192 C96 C16 CQ WA WW WP W3 T1 T2 NRED AM NP", "float32", 8, 1),
-        ("ci", "IPI PI F2I R4I RMI NI", "int32", 8, 1),
-        ("lu", "QIL IJU KU AU O2 AU2 OFA OFV VPU N1U", "uint16", 16, 16),
-        ("lf", "DUA DUV IDU IDV A0F AC A2F OM NV VF OMV YV", "float32", 16, 16),
-        ("mat", "U U16 UC UA UW UP U3", "bfloat16", 144, 144),
-        ("sq", "BB BB4 TR RA ONE CB CZ IDP IDM CM4", "bfloat16", 128, 128),
-        ("ff", "K16 KB2 DB D0 MK KB W1 W2 KEY CM CS CMV CSV UV", "float32", 256, 256),
-        ("bb", "QM QI1 QI2 FB GB VJ VG N1B NNB ON KPB", "bfloat16", 256, 256),
-        ("ii", "RI ZI XI XS", "int32", 256, 256),
-        ("fs", "IS64 DW DS N5 S1 S2", "float32", 64, 64)):
+        ("sm", "IP P16 G16 G15 IP16 M0 M1 C192 C24 WA WB W5 T1 T2 T3 NP BC ZC", "float32", 8, 1),
+        ("ci", "IPI PI EI", "int32", 8, 1),
+        ("lu", "KU AU AU2 OFA OFV N1U", "uint16", 16, 16),
+        ("lf", "DUA DUV I16 IV NV VF YV JK", "float32", 16, 16),
+        ("mat", "U U16 UC UA", "bfloat16", 144, 144),
+        ("mh", "UH UW B0 B1 B0N B1N", "float16", 160, 160),
+        ("sh", "IDH IDMH RA", "float16", 128, 128),
+        ("sq", "BB BB4 TR TRE ONE CB C15 IDP IDM", "bfloat16", 128, 128),
+        ("ff", "K16 DB D0 MK KB W2 KEY CS DM OHA", "float32", 256, 256),
+        ("bb", "QM NNB ON MON PO C1 XA XS RV YQ", "bfloat16", 256, 256)):
     for _j, _nm in enumerate(_names.split()):
         _PACK[_nm] = (_w, _j * _n)
         _WIDTH[_nm] = _u
     SCRATCH[_w] = ("sbuf", [128, _n * len(_names.split())], _dt)
 
-NDMA = 40
+NDMA = 30
 SEMAPHORES = ["qV", "qS", "qP", "qG", "sent"] + ["d%d" % _k for _k in range(NDMA)]
 for _t in range(NR):
-    for _h in range(1, 4):
-        SEMAPHORES += ["z%d%d" % (_t, _h), "w%d%d" % (_t, _h)]
+    SEMAPHORES += ["z%d" % _t, "w%d" % _t]
 
 
 def shift(t, h):
@@ -78,6 +83,11 @@ def rank_program(g, core, T, topo):
         ap = T[w][:, lo:hi:step] if step != 1 else T[w][:, lo:hi]
         return (ap, [(w, lo, hi, step, None)], [])
 
+    def n(name, *ix):
+        f = ix[0] if ix else A
+        lo, hi = (f, f + 1) if isinstance(f, int) else (f.start or 0, f.stop or 64)
+        return (T[name][(A,) + ix], [(name, lo, hi, 1, None)], [])
+
     def rows(name, f, lo, hi):
         return (T[name][f:128:16, lo:hi], [(name, lo, hi, 1, f)], [])
 
@@ -103,7 +113,7 @@ def rank_program(g, core, T, topo):
             if any(b != a and snap.get((b, need[b]), {}).get(a, 0) >= need[a] for b in need): continue
             ENG[q].wait_ge(T.sem["q" + a if a in cnt else a], need[a] * unit[a])
         for a in need:
-            for b, n in snap.get((a, need[a]), {}).items(): know[q][b] = max(know[q].get(b, 0), n)
+            for b, m in snap.get((a, need[a]), {}).items(): know[q][b] = max(know[q].get(b, 0), m)
             know[q][a] = max(know[q].get(a, 0), need[a])
 
     def note(tok, w, r):
@@ -142,18 +152,25 @@ def rank_program(g, core, T, topo):
         snap[(nm, 1)] = dict(know[qk])
         note((nm, 1), w, r)
 
-    def remote(kind, t, h, dst_view, src_view):
-        d = T.cores[(me + shift(t, h)) % N]
-        order("G", [], src_view[1])
-        rid, pid, _s = topo.addr(d)
-        es = topo.engines(core, d)[:8]
-        nm = "%s%d%d" % (kind, t, h)
-        g.remote_dma(dst_view[0], src_view[0], T.sem[nm], T.sem.sent, pid, rid, sum(1 << e for e in es))
-        sent[0] += len(es)
-        src = T.cores[(me - shift(t, h)) % N]
-        unit[nm] = len(topo.engines(src, core)[:8]); total[nm] = 1
+    def engines(src, dst, h):
+        return topo.engines(src, dst)[2 * h - 2:2 * h]
+
+    def remote(kind, t, dst, src):
+        nm = "%s%d" % (kind, t)
+        order("G", [], [k for h in range(1, 4) for k in src(h)[1]])
+        trs = []
+        for h in range(1, 4):
+            d = T.cores[(me + shift(t, h)) % N]
+            rid, pid, _s = topo.addr(d)
+            es = engines(core, d, h)
+            trs.append(RemoteDMATransfer(dst_ids=[DstId(rid=rid, pnc=pid)], dma_engine_mask=sum(1 << e for e in es),
+                                         remote_sem=T.sem[nm], src=src(h)[0], dst=dst(h)[0]))
+            sent[0] += len(es)
+        g.remote_dma_fused(trs, local_sem=T.sem.sent)
+        unit[nm] = sum(len(engines(T.cores[(me - shift(t, h)) % N], core, h)) for h in range(1, 4))
+        total[nm] = 1
         snap[(nm, 1)] = {}
-        note((nm, 1), dst_view[1], [])
+        note((nm, 1), [k for h in range(1, 4) for k in dst(h)[1]], [])
 
     def cp(o, i): emit("V", lambda: g.vector.tensor_copy(o[0], i[0]), [o], [i])
     def tt(o, a, b, op): emit("V", lambda: g.vector.tensor_tensor(o[0], a[0], b[0], op), [o], [a, b])
@@ -164,332 +181,356 @@ def rank_program(g, core, T, topo):
         if op1 is None: emit("V", lambda: g.vector.tensor_scalar(o[0], a[0], x1, None, op0), [o], [a] + ex)
         else: emit("V", lambda: g.vector.tensor_scalar(o[0], a[0], x1, x2, op0, op1), [o], [a] + ex)
     def scan(o, d0, d1, init, op0, op1): emit("V", lambda: g.vector.tensor_tensor_scan(o[0], d0[0], d1[0], init, op0, op1), [o], [d0, d1])
-    def rsum(o, i): emit("V", lambda: g.vector.tensor_reduce(o[0], i[0], AxisListType.X, OP.add), [o], [i])
+    def turn(o, i): emit("V", lambda: g.vector.transpose(o[0], i[0]), [o], [i])
     def fill(o, c): emit("V", lambda: g.vector.memset(o[0], c), [o], [])
-    def act(o, i, f=AF.Identity, bias=0.0, scale=1.0):
+    def act(o, i, f=AF.Identity, bias=0.0, scale=1.0, acc=None):
         ex = [s for s in (bias, scale) if isinstance(s, tuple)]
         b = bias[0] if isinstance(bias, tuple) else bias
         s = scale[0] if isinstance(scale, tuple) else scale
-        emit("S", lambda: g.scalar.activation(o[0], i[0], f, bias=b, scale=s), [o], [i] + ex)
+        if acc is None: emit("S", lambda: g.scalar.activation(o[0], i[0], f, bias=b, scale=s), [o], [i] + ex)
+        else: emit("S", lambda: g.scalar.activation(o[0], i[0], f, bias=b, scale=s, accum_out=acc[0]), [o, acc], [i] + ex)
     def mm(o, l, r, start, stop): emit("P", lambda: g.tensor.matmul(o[0], l[0], r[0], start, stop), [o], [l, r])
     def iota(o, pat, base=0, cm=0, small=True):
         if small: emit("G", lambda: g.iota(o[0], pat, base, cm, allow_small_or_imprecise_dtypes=True), [o], [])
         else: emit("G", lambda: g.iota(o[0], pat, base, cm), [o], [])
-    def keep(o, i, pat, op, base, cm): emit("G", lambda: g.affine_select(o[0], i[0], pat, op, 0.0, base, cm), [o], [i])
+    def keep(o, i, pat, op, base, cm, other=0.0): emit("G", lambda: g.affine_select(o[0], i[0], pat, op, other, base, cm), [o], [i])
+    def gcp(o, i, m): keep(o, i, [[0, m]], OP.is_ge, 0, 0)
     def usl(name, r): return v(name, 15 - r, 143 - r)
+    def sel(f, e, neg=""): return v("B%d%s" % (f, neg), 16 + 16 * (f - e), 144 + 16 * (f - e))
 
-    def diag(bank, mat, src, n):
+    def diag(out, mat, src, m, last=True):
         for r in range(16):
-            mm(v(bank, 0, n), usl(mat, r), v(src, r, 16 * n, 16), r == 0, r == 15)
+            mm(out, usl(mat, r), v(src, r, 16 * m, 16), r == 0, last and r == 15)
 
-    dma(v("B4", 576, 768), T.nx[:])
-    dma(v("B4", 384, 576), T.pv[:], "act")
+    def unturn(bank, src, ks, ko, neg=None):
+        for f in range(2):
+            o = slice(f, 4, 2)
+            for e in range(2):
+                mm(n(bank, H4, o, ko), sel(f, e), n(src, A, A, e, ks), e == 0, e == 1 and neg is None)
+            if neg is not None:
+                for e in range(2):
+                    mm(n(bank, H4, o, neg[1]), sel(f, e, "N"), n(src, A, A, e, neg[0]), False, e == 1)
+
+    def to_list(nat, bank, o=0):
+        ts(v("NH", o, o + 192), v(nat), -OFF, OP.add)
+        turn(v("TN", o, o + 192), v("NH", o, o + 192))
+        for m in range(12):
+            for e in range(2):
+                b = o + 32 * (m // 2) + 16 * e
+                mm(v(bank, m, 192, 12), sel(m % 2, e), v("TN", b, b + 16), e == 0, e == 1)
+
+    dma(v("NXN"), T.nx[:])
+    dma(v("PVN"), T.pv[:], "act")
     dma(v("QM"), T.mv[:])
-    dma(v("ULI"), T.ul[:])
-    dma(v("X", 0, 3072), T.xd[:], "act")
-    dma(v("B4", 192, 384), T.rc[:])
+    dma(v("X", 0, 3072), T.xd[:])
 
-    fill(v("NXR", 0, 3072), 0.0)
-    fill(v("ON"), 1.0)
+    fill(v("PW", 0, 1024), 0)
     iota(v("IPI"), [[1, 1]], 0, 1, False)
     iota(v("IP"), [[1, 1]], 0, 1)
-    iota(v("IN144"), [[1, 144]])
-    iota(v("IJL"), [[1, 4], [4, 4]], 0, 0, False)
-    iota(v("I64"), [[1, 64]], 0, 0, False)
-    iota(v("I32"), [[6, 4], [24, 8]], 0, 0, False)
-    iota(v("I192"), [[1, 192]], 0, 0, False)
-    iota(v("K16"), [[0, 16], [1, 16]])
+    iota(v("IN160"), [[1, 160]])
+    iota(v("I64"), [[16, 16], [0, 4]])
+    iota(v("IV"), [[6, 4], [384, 4]])
     iota(v("IG16"), [[16, 8], [0, 16]])
-    iota(v("I16"), [[1, 16]], 0, 0, False)
-    iota(v("IQ4"), [[16, 4], [64, 4], [4, 4]], 0, 0, False)
-    iota(v("IDU"), [[16, 16]], 3072, 0)
-    iota(v("IDV"), [[16, 16]], 1536, 0)
-    iota(v("IS64"), [[0, 16], [1, 4]])
-    keep(v("IDP"), v("ON", 0, 128), [[-1, 128]], OP.is_equal, 0, 1)
-    iota(v("ZZ"), [[0, 3072]])
-
-    def halves(lo, hi):
-        ts(v("BHI", lo, hi), v("B4", lo, hi), 6, OP.arith_shift_right)
-        ts(v("BLI", lo, hi), v("B4", lo, hi), 63, OP.bitwise_and)
-        cp(v("BHB", lo, hi), v("BHI", lo, hi))
-        cp(v("BLB", lo, hi), v("BLI", lo, hi))
-
-    def weights(nm, k):
-        ts(v("T1"), v("P16"), k, OP.is_equal, 64.0, OP.mult)
-        ts(v("T2"), v("P16"), k + 1, OP.is_equal)
-        tt(v(nm), v("T1"), v("T2"), OP.add)
-
-    def spread(t, hs):
-        for h in hs:
-            act(v("Q16", 1024 * h, 1024 * h + 1024), ind(v("QJ%d" % t, 64 * h, 64 * h + 64), v("C64")))
-
+    iota(v("I192"), [[1, 192]])
+    for k in range(1, 3):
+        act(v("PW", 1024 * k, 1024 * k + 1024), v("PW", 0, 1024))
+    dma(rows("PW", 4, 0, 3072), T.pv[:])
+    dma(v("ULI"), T.ul[:])
+    ts(v("EI"), v("IPI"), 4, OP.arith_shift_right, 1, OP.bitwise_and)
     ts(v("PI"), v("IPI"), 15, OP.bitwise_and)
+    ts(v("IP16"), v("IP"), 16.0, OP.add)
+    cp(v("M1"), v("EI"))
     cp(v("P16"), v("PI"))
-    ts(v("C16"), v("P16"), 16.0, OP.mult)
-    ts(v("IJU"), v("IJL"), v("C16"), OP.add)
-    cp(v("C64"), v("I64"))
-    halves(576, 768)
-    dma(rows("NXR", 0, 0, 3072), v("BHB", 576, 768))
-    dma(rows("NXR", 1, 0, 3072), v("BLB", 576, 768))
-    weights("WA", 0.0)
+    ts(v("M0"), v("M1"), -1.0, OP.mult, 1.0, OP.add)
+    ts(v("B1"), v("IN160"), v("IP16"), OP.is_equal, v("M1"), OP.mult)
+    ts(v("B0"), v("IN160"), v("IP16"), OP.is_equal, v("M0"), OP.mult)
+    fill(v("ON"), 1.0)
     tt(v("G16"), v("IP"), v("P16"), OP.subtract)
+    to_list("PVN", "P4", 192)
+    to_list("NXN", "P3")
+    act(v("Q4L"), v("I64"), bias=v("P16"))
+    for h in range(4):
+        act(v("QJ0", 64 * h, 64 * h + 64), v("QM", h, 256, 4))
+    ts(v("BHI"), v("NXN"), 6, OP.arith_shift_right)
+    ts(v("BLI"), v("NXN"), 63, OP.bitwise_and)
     ts(v("G15"), v("G16"), 15.0, OP.add)
-    ts(v("U"), v("IN144"), v("G15"), OP.is_equal)
-    act(v("QJ0"), ind(v("QM"), v("IJU")))
-    act(v("UA"), v("U"), scale=v("WA"))
-    ts(v("C96"), v("P16"), 96.0, OP.mult)
-    ts(v("VL0"), v("I32"), v("C96"), OP.add)
-    fill(v("TT", 0, 3072), 0.0)
-    halves(384, 576)
-    dma(rows("TT", 4, 0, 3072), v("BHB", 384, 576))
-    dma(rows("TT", 5, 0, 3072), v("BLB", 384, 576))
-    weights("WP", 4.0)
-    spread(0, range(1))
-    act(v("UP"), v("U"), scale=v("WP"))
-    spread(0, range(1, 3))
-    diag("P3", "UA", "NXR", 192)
-    diag("P7", "UP", "TT", 192)
-
-    def consts2():
-        ts(v("C192"), v("P16"), 192.0, OP.mult)
-        ts(v("B4", 0, 192), v("I192"), v("C192"), OP.add)
-        halves(0, 384)
-        for k in range(2):
-            dma(rows("TT", 2 * k, 0, 3072), v("BHB", 192 * k, 192 * k + 192))
-            dma(rows("TT", 2 * k + 1, 0, 3072), v("BLB", 192 * k, 192 * k + 192))
-        weights("WW", 2.0)
-        ts(v("NP"), v("P16"), -1.0, OP.mult)
-        ts(v("IDM"), v("IDP"), -1.0, OP.mult)
-        act(v("U16"), v("U"), scale=16.0)
-        act(v("UC"), v("U"), scale=1048576.0)
-        act(v("KPB"), v("K16"))
-        fill(v("CB"), -61440.0)
-        cp(v("PVL"), v("P7", 0, 192))
+    cp(v("BHB"), v("BHI"))
+    cp(v("BLB"), v("BLI"))
+    ts(v("PVL"), v("P4", 0, 192), OFF, OP.add)
+    act(v("NXL"), v("P3", 0, 192), bias=OFF)
+    act(v("QA"), ind(v("QJ0"), v("Q4L")))
+    ts(v("U"), v("IN160", 0, 144), v("G15"), OP.is_equal)
+    ts(v("C24"), v("P16"), 24.0, OP.mult)
+    ts(v("C192"), v("P16"), 192.0, OP.mult)
+    ts(v("VL0", 4, 20), v("IV"), v("C24"), OP.add)
+    ts(v("IDN"), v("I192"), v("C192"), OP.add)
+    ts(v("BB"), v("IG16"), v("G16"), OP.is_equal)
+    ts(v("T1"), v("P16"), 8.0, OP.is_equal, 64.0, OP.mult)
+    ts(v("T2"), v("P16"), 9.0, OP.is_equal)
+    ts(v("T3"), v("P16"), 6.0, OP.is_equal)
+    ts(v("W5"), v("P16"), 5.0, OP.is_equal)
+    ts(v("NP"), v("P16"), -1.0, OP.mult)
+    ts(v("E16"), v("IN160", 0, 16), v("P16"), OP.is_equal)
+    ts(v("U16"), v("U"), 16.0, OP.mult)
+    ts(v("UC"), v("U"), 1048576.0, OP.mult)
+    ts(v("BB4"), v("BB"), 4096.0, OP.mult)
+    fill(v("CB"), -61440.0)
+    fill(v("C15"), 15.0 / 128)
+    fill(v("ONE"), 1.0)
+    fill(v("MON"), -1.0)
+    keep(v("IDP"), v("ON", 0, 128), [[-1, 128]], OP.is_equal, 0, 1)
+    iota(v("K16"), [[0, 16], [1, 16]])
+    iota(v("I16"), [[16, 16]])
+    keep(v("IDM"), v("MON", 0, 128), [[-1, 128]], OP.is_equal, 0, 1)
+    keep(v("IDMH"), v("MON", 0, 128), [[-1, 128]], OP.is_equal, 0, 1)
+    keep(v("TR"), v("BB4"), [[1, 128]], OP.is_gt, 0, -1)
+    keep(v("TRE"), v("BB4"), [[1, 128]], OP.is_ge, 0, -1)
+    keep(v("D0"), v("ON"), [[0, 16], [1, 16]], OP.is_gt, 0, 0)
+    keep(v("DB"), v("MON"), [[0, 16], [1, 16]], OP.is_gt, 0, 0, 524288.0)
+    iota(v("WI"), [[0, 16], [-16, 6]], 16)
+    keep(v("WI"), v("WI"), [[0, 16], [-1, 6]], OP.is_ge, 0, 0)
+    gcp(v("UH", 0, 144), v("U"), 144)
+    gcp(v("IDH"), v("IDP"), 128)
+    gcp(v("ULF", 0, 1536), v("ULI"), 1536)
+    iota(v("NXR", 0, 3072), [[0, 3072]])
+    cp(v("W1"), ind(v("PW"), v("PVL")))
+    dma(v("P2N"), rows("W1", 4, 0, 3072))
+    dma(rows("PW", 3, 0, 3072), rows("W1", 4, 0, 3072))
+    dma(rows("PW", 5, 0, 3072), v("IDN"))
+    dma(rows("PW", 6, 0, 3072), T.rc[:])
 
     def late_consts():
-        act(v("UW"), v("U"), scale=v("WW"))
-        act(v("D0"), v("K16"), AF.Sign)
-        act(v("DB"), v("D0"), scale=-524288.0, bias=524288.0)
-        act(v("KB2"), v("K16"), scale=2.0, bias=BIG)
+        act(v("B0N"), v("B0"), scale=-1.0)
+        act(v("B1N"), v("B1"), scale=-1.0)
         act(v("MK"), v("K16"), AF.Square, bias=v("NP"))
-        act(v("MK"), v("MK"), AF.Relu, scale=-1.0, bias=1.0)
-        act(v("DS"), v("IS64"), AF.Sign)
-        act(v("DW"), v("DS"), scale=-3072.0, bias=3072.0)
-        act(v("DUA"), v("IDU"), bias=v("P16"))
-        act(v("DUV"), v("IDV"), bias=v("P16"))
-        ts(v("R4I"), v("PI"), 2, OP.arith_shift_right)
-        ts(v("F2I"), v("PI"), 1, OP.arith_shift_right)
-        ts(v("RMI"), v("PI"), 3, OP.bitwise_and)
-        cp(v("R4"), v("R4I"))
-        cp(v("F2"), v("F2I"))
-        cp(v("RM"), v("RMI"))
-        cp(v("UH"), v("U"))
-        cp(v("IDH"), v("IDP"))
-        ts(v("IDMH"), v("IDP"), -1.0, OP.mult)
-        ts(v("T1"), v("F2"), -2.0, OP.mult, v("P16"), OP.add)
-        ts(v("T1"), v("T1"), -63.0, OP.mult, 64.0, OP.add)
-        ts(v("W3"), v("P16"), 8.0, OP.is_lt, v("T1"), OP.mult)
-        tt(v("G12"), v("G16"), v("F2"), OP.add)
-        ts(v("G12"), v("G12"), 12.0, OP.add)
-        ts(v("U3"), v("IN144"), v("G12"), OP.is_equal, v("W3"), OP.mult)
-        ts(v("BB"), v("IG16"), v("G16"), OP.is_equal)
-        act(v("BB4"), v("BB"), scale=4096.0)
-        act(v("RA"), v("BB"), scale=v("WA"))
-        keep(v("TR"), v("BB4"), [[1, 128]], OP.is_gt, 0, -1)
-        fill(v("ONE"), 1.0)
-        fill(v("CZ"), 0.0)
-        fill(v("CM4"), -1.0 / 4096)
-        ts(v("E16"), v("IN144", 0, 16), v("P16"), OP.is_equal)
-        ts(v("Q4L"), v("IQ4"), v("R4"), OP.add)
-        ts(v("CQ"), v("RM"), 64.0, OP.mult)
-        ts(v("T1"), v("R4"), 16.0, OP.mult)
-        tt(v("CQ"), v("CQ"), v("T1"), OP.add)
-        ts(v("QIL"), v("I16"), v("CQ"), OP.add)
+        act(v("WA"), v("T1"), bias=v("T2"))
+        act(v("MK"), v("MK"), AF.Sign)
+        act(v("WB"), v("WA"), bias=v("T3"))
+        act(v("PO"), v("MK"), scale=-4194304.0, bias=OFF)
+        act(v("RA"), v("BB"), scale=v("W5"))
+        act(v("UW", 0, 144), v("U"), scale=v("WB"))
+        act(v("UA"), v("U"), scale=v("WA"))
+        act(v("DUA"), v("I16"), bias=v("P16"))
+        act(v("DUV"), v("DUA"), bias=1536.0)
+        act(v("DUA"), v("DUA"), bias=3072.0)
 
-    def table(q, m):
-        o, w = v("TT", 3072 * m, 3072 * m + 3072), v("TT", 3072 * m - 3072, 3072 * m)
-        if q == "V": cp(o, ind(w, v("PVL")))
-        else: act(o, ind(w, v("PVL")))
-        for f in range(2):
-            dma(rows("ZZ", 2 * m - 2 + f, 0, 3072), rows("TT", f, 3072 * m, 3072 * m + 3072))
+    def test(x, out, q, op, Q4):
+        tt(v(out, 1024 * q, 1024 * q + 1024), ind(v(x, 0, 3072), v("DL", 64 * q, 64 * q + 64)), v(Q4), op)
 
-    def lane_q(t):
-        act(v("QW"), ind(v("QJ%d" % t), v("Q4L")))
-        act(v("QI%d" % (1 + t % 2)), ind(v("QJ%d" % t), v("QIL")), bias=1.0)
+    def sums(bank, mat, src, q, last):
+        for r in range(16):
+            mm(n(bank, H4, A, slice(4 * q, 4 * q + 4)), usl(mat, r), v(src, 1024 * q + r, 1024 * q + 1024, 16), False, last and r == 15)
 
-    def eo(p): return 256 * p - 8 * p * (p - 1)
-
-    def dedupe_mm(bank, e, ps):
-        for p in ps:
-            if p == 0: mm(v(bank, 0, 256), v("CZ"), v("ON"), True, False)
-            if p < 15: mm(v(bank, 16 * p + 16, 256), v("BB4"), v(e, eo(p) + 16, eo(p + 1)), False, False)
-            mm(v(bank, 16 * p, 16 * p + 16), v("TR"), v(e, eo(p), eo(p) + 16), False, p == 15)
-
-    def dedupe_off(bank, cm, cs, om, dump, num, off):
-        tt(v(cm), v(bank, 0, 256), v("MK"), OP.mult)
-        scan(v(cs), v("D0"), v(cm), 0.0, OP.mult, OP.add)
-        tt(v(om), v(cs, 15, 256, 16), v(dump), OP.min)
-        tt(v(off), v(om), v(num), OP.max)
-
-    def test(x, out, h, op, n=1024):
-        tt(v(out, 1024 * h, 1024 * h + n), ind(v(x, 0, 3072), v("DL", 64 * h, 64 * h + n // 16)), v("Q16", 1024 * h, 1024 * h + n), op)
-
-    def sums(bank, mat, src, h, last):
-        for c in range(4):
-            mm(v(bank, 0, 256), usl(mat, 4 * c + h), v(src, 1024 * h + 256 * c, 1024 * h + 256 * c + 256), False, last and c == 3)
+    HC = [(h, c) for c in range(4) for h in range(4)]
 
     for t in range(NR):
-        Q, Qn, VLt, Vn = "QJ%d" % t, "QJ%d" % (t + 1), "VL%d" % t, "VL%d" % (t + 1)
+        Q, Qn, VL, Vn = "QJ%d" % t, "QJ%d" % (t + 1), v("VL%d" % t, 4, 20), "VL%d" % (t + 1)
+        Q4, Q4n = ("QA", "QB") if t % 2 == 0 else ("QB", "QA")
         first, lastr = t == 0, t == NR - 1
         UT = v("ULI") if first else v("ULF", 0, 1536)
 
-        def places(h): cp(v("DL", 64 * h, 64 * h + 64), ind(UT, v(VLt, 8 * h, 8 * h + 4)))
-        places(0)
-        test("X", "DF", 0, OP.subtract)
-        if first: cp(v("NXL"), v("P3", 0, 192))
-        act(v("X1"), ind(v("X", 0, 3072), v("NXL")))
-        if first: spread(0, range(3, 4))
+        def share(j):
+            b = "P%d" % (3 + j % 2)
+            mm(v(b), v("IDP"), v("XG", 512 * j, 512 * j + 512), True, False)
+            mm(v(b), v("IDM"), v(Q4, 512 * (j % 2), 512 * (j % 2) + 512), False, True)
+
+        def sgather(j): act(v("XG", 512 * j, 512 * j + 512), ind(v("X", 0, 3072), v("DL", 128 + 32 * j, 160 + 32 * j)))
+        def sabs(j): act(v("AB", 2048 + 512 * j, 2560 + 512 * j), v("P%d" % (3 + j % 2)), AF.Abs)
+
+        def squares(c):
+            if first: return
+            for h in range(4):
+                act(n("EV%d" % c, h), n("VR", A, slice(c, 4)), AF.Square, bias=v("NV", 4 * h + c, 4 * h + c + 1))
+            act(n("EW%d" % c), n("EV%d" % c), AF.Relu, scale=-1.0, bias=1.0)
+
+        def equal(c):
+            if first: return
+            for h in range(4):
+                ts(n("EW%d" % c, h), n("VR", A, slice(c, 4)), v("VF", 4 * h + c, 4 * h + c + 1), OP.is_equal)
+
+        def count(c, start=False, stop=False):
+            if first: return
+            if start: mm(n("P1", H4), v("IDP"), v("PO"), True, False)
+            src = "EW%d" % c
+            for h in range(4):
+                if c < 3: mm(n("P1", H4, slice(c + 1, 4)), v("BB4"), n(src, h, A, slice(1, 4 - c)), False, False)
+                mm(n("P1", slice(0, h + 1), c), v("TR"), n(src, h, slice(0, h + 1), 0), False, stop and h == 3)
+                if h < 3: mm(n("P1", slice(h + 1, 4), c), v("TRE"), n(src, h, slice(h + 1, 4), 0), False, False)
+
+        if first: act(v("X1"), ind(v("X", 0, 3072), v("NXL")))
+        ts(v("DI"), ind(UT, VL), -OFF, OP.add)
+        turn(n("TD"), v("DI"))
+        unturn("P5", "TD", A, A)
+        mm(n("P0", H4), v("C15"), v("ON"), True, False)
+        mm(n("P1", H4), v("CB"), v("ON"), True, False)
+        mm(n("P2", H4), v("CB"), v("ON"), True, False)
+        for q in range(4):
+            ts(v("DL", 64 * q, 64 * q + 64), n("P5", H4, A, slice(4 * q, 4 * q + 4)), OFF, OP.add)
+        if not first:
+            act(v("VG"), ind(v("PW"), VL))
+            mm(n("P6", H4), v("RA"), v("VG"), True, True)
         act(v("X2"), ind(v("X1"), v("NXL")))
-        for h in range(1, 4):
-            places(h)
-            n = 1024 - 512 * len([1 for x in SHARE if x[0] == h])
-            if n: test("X", "DF", h, OP.subtract, n)
+        test("X", "DF", 0, OP.subtract, Q4)
         if first:
-            consts2()
-            late_consts()
-            table("V", 1)
-            table("V", 2)
-        for h in range(4):
-            act(v("VJ", 64 * h, 64 * h + 64), ind(v("TT", 0, 3072), v(VLt, 8 * h, 8 * h + 4)))
-        for r in [4 * c + k for k in range(4) for c in range(4)]:
-            b = 64 * (r % 4) + 16 * (r // 4)
-            mm(v("P7", 0, 16), usl("UA", r), v("VJ", b, b + 16), r == 0, r == 15)
-        for j, (h, k) in enumerate(SHARE):
-            act(v("XG", 512 * j, 512 * j + 512), ind(v("X", 0, 3072), v("DL", 64 * h + 32 * k, 64 * h + 32 * k + 32)))
-        for h in range(4):
-            n = 1024 - 512 * len([1 for x in SHARE if x[0] == h])
-            if n: act(v("AB", 1024 * h, 1024 * h + n), v("DF", 1024 * h, 1024 * h + n), AF.Abs)
-        mm(v("P1", 0, 256), v("CB"), v("ON"), True, False)
-        mm(v("P2", 0, 256), v("CB"), v("ON"), True, False)
-        mm(v("P0", 0, 256), v("IDP"), v("KPB"), True, False)
-        for h in range(4):
-            test("X1", "L1", h, OP.is_lt)
-            sums("P1", "UC", "L1", h, h == 3)
-            if h == 1:
-                for j, (hs, k) in enumerate(SHARE):
-                    mm(v(SBANK[j]), v("IDP"), v("XG", 512 * j, 512 * j + 512), True, False)
-                    mm(v(SBANK[j]), v("IDM"), v("Q16", 1024 * hs + 512 * k, 1024 * hs + 512 * k + 512), False, True)
-                for j, (hs, k) in enumerate(SHARE):
-                    act(v("AB", 1024 * hs + 512 * k, 1024 * hs + 512 * k + 512), v(SBANK[j]), AF.Abs)
-        cp(v("VPU"), v("P7", 0, 16))
-        act(v("VF"), v("P7", 0, 16))
-        act(v("NV"), v("P7", 0, 16), scale=-1.0)
-        act(v("VG"), ind(v("TT", 0, 3072), v("VPU")))
-        for h in range(4):
-            sums("P0", "U16", "AB", h, h == 3)
-        mm(v("P6", 0, 256), v("RA"), v("VG"), True, True)
+            to_list("P2N", "P3")
+        test("X", "DF", 1, OP.subtract, Q4)
         if first:
-            lane_q(0)
-            table("S", 3)
-            table("S", 4)
-        for h in range(2):
-            test("X2", "L2", h, OP.is_lt)
-            sums("P2", "UC", "L2", h, False)
-        test("X2", "L2", 2, OP.is_lt)
+            ts(v("P2L"), v("P3", 0, 192), OFF, OP.add)
+            act(v("W1"), ind(v("PW"), v("P2L")))
+            dma(rows("PW", 2, 0, 3072), rows("W1", 4, 0, 3072))
+            dma(rows("PW", 1, 0, 3072), rows("W1", 3, 0, 3072))
+            dma(rows("NXR", 8, 0, 3072), v("BHB"))
+            dma(rows("NXR", 9, 0, 3072), v("BLB"))
+        for q in range(4):
+            test("X1", "L1", q, OP.is_lt, Q4)
+            sums("P1", "UC", "L1", q, q == 3)
+        act(v("AB", 0, 1024), v("DF", 0, 1024), AF.Abs)
+        act(v("AB", 1024, 2048), v("DF", 1024, 2048), AF.Abs)
+        sums("P0", "U16", "AB", 0, False)
+        sums("P0", "U16", "AB", 1, False)
+        sgather(0)
+        sgather(1)
+        test("X2", "L2", 0, OP.is_lt, Q4)
+        share(0)
+        sums("P2", "UC", "L2", 0, False)
+        share(1)
+        sabs(0)
+        sgather(2)
+        sabs(1)
+        share(2)
+        test("X2", "L2", 1, OP.is_lt, Q4)
+        sums("P2", "UC", "L2", 1, False)
+        sgather(3)
+        sums("P0", "U16", "AB", 2, False)
+        share(3)
+        sabs(2)
+        sabs(3)
+        test("X2", "L2", 2, OP.is_lt, Q4)
         sums("P2", "UC", "L2", 2, False)
-        for p in range(16):
-            act(v("EV", eo(p), eo(p + 1)), v("P6", 16 * p, 256), AF.Square, bias=v("NV", p, p + 1))
-        act(v("EW"), v("EV"), AF.Relu, scale=-1.0, bias=1.0)
-        test("X2", "L2", 3, OP.is_lt)
+        act(v("C1"), n("P1", H4), AF.Relu, scale=32.0)
+        sums("P0", "U16", "AB", 3, True)
+        mm(n("P2", H4), v("IDP"), v("C1"), False, False)
+        if not first:
+            act(n("VR"), n("P6", H4))
+            act(v("VF"), VL)
+        act(v("KB"), n("P0", H4), scale=-1.0, bias=BIG)
+        test("X2", "L2", 3, OP.is_lt, Q4)
         sums("P2", "UC", "L2", 3, True)
-        ts(v("DI"), ind(UT, v("VPU")), -1536.0, OP.add)
-        tt(v("KB"), v("KB2"), v("P0", 0, 256), OP.subtract)
-        tt(v("W1"), v("P1", 0, 256), v("KB"), OP.min)
-        tt(v("P4", 0, 256), v("W1"), v("P0", 0, 256), OP.max)
-        tt(v("W2"), v("P2", 0, 256), v("KB"), OP.min)
-        tt(v("KEY"), v("W2"), v("P4", 0, 256), OP.max)
+        if first: late_consts()
+        else:
+            act(v("NV"), VL, scale=-1.0)
+            act(v("VH"), VL)
+        squares(0)
+        equal(2)
+        tt(v("W2"), n("P2", H4), v("KB"), OP.min)
+        tt(v("KEY"), v("W2"), n("P0", H4), OP.max)
         scan(v("RI"), v("DB"), v("KEY"), 1000000.0, OP.add, OP.min)
+        count(2, True)
+        mm(n("P2", H4, A, slice(0, 6)), v("IDP"), v("WI"), True, False)
         ts(v("KI"), v("RI", 15, 256, 16), 15, OP.bitwise_and)
         cp(v("KU"), v("KI"))
         tt(v("OHD"), ind(v("E16"), v("KU")), v("DI"), OP.mult)
-        diag("P3", "UH", "OHD", 16)
-        ts(v("NFB"), v("RI", 15, 256, 16), 65536.0, OP.is_ge)
-        mm(v("P1", 0, 16), v("ONE"), v("NFB"), True, False)
-        mm(v("P1", 0, 16), v("CM4"), v("ON", 0, 16), False, True)
-        if first: cp(v("ULF", 0, 1536), v("ULI"))
-        ts(v("AU"), v("P3", 0, 16), 1536.0, OP.add)
-        cp(v("FB"), ind(v("ZZ"), v("AU")))
-        for ch in range(4):
-            for r4 in range(4):
-                b = 64 * ch + 16 * r4
-                mm(v("P4", ch, 64, 4), v("U3", 12 - 4 * r4, 140 - 4 * r4), v("FB", b, b + 16), r4 == 0, r4 == 3)
-        rsum(v("NRED"), v("P1", 0, 16))
-        ts(v("NI"), v("NRED"), 1.0 / 256, OP.mult, -127.0 / 256, OP.add)
-        ts(v("AM"), v("NI"), -256.0, OP.mult, v("NRED"), OP.add)
-        ts(v("A0F"), v("P3", 0, 16), 1536.0, OP.add)
-        ts(v("ZI"), v(Q), v("AM"), OP.add, 0.5, OP.mult)
-        cp(v("BLU"), v("P4", 0, 64))
-        for k in range(2):
-            tt(v("LW", 512 * k, 512 * k + 512), ind(v("X", 0, 3072), v("BLU", 32 * k, 32 * k + 32)), v("QW", 512 * k, 512 * k + 512), OP.is_lt)
-            for r in range(8 * k, 8 * k + 8):
-                mm(v("P5", 0, 64), usl("U", r), v("LW", 64 * r, 64 * r + 64), r == 0, r == 15)
-        cp(v("ZB%d" % t), v("ZI"))
-        for h in range(1, 4):
-            remote("z", t, h, v(Qn, 64 * h, 64 * h + 64), v("ZB%d" % t, 64 * h, 64 * h + 64))
+        diag(v("P3", 0, 16), "UH", "OHD", 16)
+        equal(3)
+        act(v("SG"), v("RI", 15, 256, 16), AF.Sign, bias=-65535.5)
+        mm(v("P4", 0, 16), v("ONE"), v("SG"), True, True)
+        act(v("JK"), v("P4", 0, 16), scale=0.25, bias=198655.75 / 16, acc=v("BC"))
+        act(v("NI", 0, 1), v("BC"), scale=1.0 / 128, bias=-12.49609375)
+        act(v("ZC"), v("NI", 0, 1), scale=-128.0, bias=v("BC"))
+        act(v("ZH"), v(Q), scale=0.5, bias=v("ZC"))
+        act(v("ZB%d" % t), v("ZH"), bias=-OFF)
+        remote("z", t, lambda h: v(Qn, 64 * h, 64 * h + 64), lambda h: v("ZB%d" % t, 64 * h, 64 * h + 64))
+        squares(1)
+        count(0)
+        ts(v("AU"), v("P3", 0, 16), OFF, OP.add)
+        ts(v("FB"), ind(v("PW"), v("AU")), -OFF, OP.add)
+        turn(n("TF"), v("FB"))
+        unturn("P5", "TF", slice(1, 5), H4)
+        unturn("P0", "TF", slice(0, 6), slice(0, 6), (slice(1, 6), slice(0, 5)))
+        count(3)
+        mm(v("P3", 0, 256), v("IDH"), v("DI"), True, False)
+        mm(v("P3", 0, 256), v("IDMH"), v("OHD"), False, True)
+        count(1, False, True)
+        act(v("DE"), n("P0", H4, A, slice(0, 6)))
+        if not first: act(v("RV"), n("P1", H4), AF.Relu, bias=-OFF)
+        ts(v("BLU"), n("P5", H4, A, H4), OFF, OP.add)
+        tt(v("LW"), ind(v("X", 0, 3072), v("BLU")), v(Q4), OP.is_lt)
+        for r in range(16):
+            mm(n("P2", H4, A, slice(1, 5)), usl("U", r), v("LW", r, 1024, 16), False, r == 15)
+        act(v("DM"), v("P3", 0, 256), bias=OFF)
         act(v(Qn, 0, 64), v("ZB%d" % t, 0, 64))
-        if not lastr: spread(t + 1, range(1))
-        ts(v("N5"), v("P5", 0, 64), 7.5, OP.is_lt, 3072.0, OP.mult)
-        scan(v("S1"), v("DW"), v("N5"), 0.0, OP.max, OP.min)
-        scan(v("S2"), v("DS"), v("S1"), 0.0, OP.mult, OP.add)
-        tt(v("O2"), v("S2", 3, 64, 4), v("A0F"), OP.add)
-        cp(v("GB"), ind(v("TT"), v("O2")))
-        for p in range(16):
-            mm(v("P6", 0, 16), usl("UW", p), v("GB", 16 * p, 16 * p + 16), p == 0, p == 15)
-        diag("P7", "UA", "GB", 16)
-        mm(v("P4", 0, 256), v("RA"), v("GB"), True, True)
-        for h in range(1, 4):
-            cp(v("MW%d" % t, 8 * h, 8 * h + 4), v("P6", h, 16, 4))
-            remote("w", t, h, v(Vn, 8 * h, 8 * h + 4), v("MW%d" % t, 8 * h, 8 * h + 4))
-        cp(v(Vn, 0, 4), v("P6", 0, 16, 4))
-        cp(v("AU2"), v("P7", 0, 16))
-        ts(v("AC"), v("P7", 0, 16), -1536.0, OP.add)
-        act(v("A2F"), v("P7", 0, 16))
-        ts(v("AR16"), v("P4", 0, 256), -1536.0, OP.add)
+        mm(v("P7", 0, 256), v("IDP"), v("PO"), True, False)
+        if not first:
+            diag(n("P1", 0, 0), "U", "RV", 16, False)
+            mm(n("P1", 0, 0), v("IDH"), v("VH"), False, True)
+        ts(v("G6"), n("P2", H4, A, slice(0, 6)), 7.5, OP.is_lt)
+        scan(v("SH"), v("DE"), v("G6"), 0.0, OP.add, OP.mult)
+        ts(v("AU2"), v("SH", 5, 96, 6), OFF, OP.add)
+        ts(v("GC", 0, 256), ind(v("PW"), v("AU2")), -OFF, OP.add)
+        if not lastr: act(v("GC", 256, 512), ind(v("NXR", 0, 3072), v("AU2")))
+        act(v("XA"), ind(v("X", 0, 3072), v("AU2")))
+        for h in range(4):
+            mm(n("P6", H4, h), v("RA"), v("GC", 64 * h, 64 * h + 64), True, True)
+        mm(n("P0", H4), v("RA"), v("GC", 0, 256), True, True)
+        m = 16 if lastr else 32
+        diag(v("P3", 0, m), "UW", "GC", m)
+        if not first: tt(v("OFV"), n("P1", 0, 0), v("DUV"), OP.min)
+        cp(v("AR"), n("P6", H4))
+        act(v("AR2"), n("P0", H4))
+        act(v("MW%d" % t), v("P3", 0, 16), bias=66 * OFF)
+        remote("w", t, lambda h: v(Vn, 4 + 4 * h, 8 + 4 * h), lambda h: v("MW%d" % t, 4 * h, 4 * h + 4))
         if not lastr:
-            act(v("N1B"), ind(v("NXR", 0, 3072), v("AU2")))
-            diag("P6", "UA", "N1B", 16)
-        for p in range(16):
-            ts(v("EA", eo(p), eo(p + 1)), v("AR16", 16 * p, 256), v("AC", p, p + 1), OP.is_equal)
-            dedupe_mm("P5", "EA", range(p, p + 1))
-            if p == 9 and not lastr:
-                cp(v("N1U"), v("P6", 0, 16))
-                act(v("NNB"), ind(v("NXR", 0, 3072), v("N1U")))
-                spread(t + 1, range(1, 4))
-        dedupe_mm("P0", "EW", range(16))
-        tt(v("XI"), ind(v("X", 0, 3072), v("AU2")), v("QI%d" % (1 + t % 2)), OP.add)
-        ts(v("XS"), v("XI"), 1, OP.arith_shift_right)
-        tt(v("OHA"), ind(v("E16"), v("KU")), v("AR16"), OP.mult)
-        mm(v("P7", 0, 256), v("IDH"), v("DI"), True, False)
-        mm(v("P7", 0, 256), v("IDMH"), v("OHD"), False, False)
-        mm(v("P7", 0, 256), v("IDH"), v("OHA"), False, True)
-        act(v("UV"), v("P7", 0, 256), bias=1536.0)
-        if not lastr: lane_q(t + 1)
-        dedupe_off("P5", "CM", "CS", "OM", "DUA", "A2F", "OFA")
+            for h in range(4):
+                act(v("N1U", h, 16, 4), v("P3", 16 + 4 * h, 20 + 4 * h))
+            act(v("NNB"), ind(v("NXR", 0, 3072), v("N1U")))
+        act(v(Vn, 4, 8), v("MW%d" % t, 0, 4))
+
+        def places():
+            tt(v("OHA"), ind(v("E16"), v("KU")), v("AR2"), OP.mult)
+            tt(ind(v("ULF"), VL if first else v("OFV")), v("DM"), v("OHA"), OP.add)
+        if lastr:
+            places()
+            dma(T.yu[:], v("ULF", 0, 1536))
+        mm(v("P7", 0, 256), v("IDH"), v("AR"), False, False)
+        e = 0
+        for h, c in HC:
+            p, o, w = 4 * h + c, 64 * c, 16 * h + 16
+            ts(v("EA", e, e + 256 - o), v("AR", o, 256), v("SH", 6 * p + 5, 6 * p + 6), OP.is_equal)
+            if c < 3: mm(v("P7", o + 64, 256), v("BB4"), v("EA", e + 64, e + 256 - o), False, False)
+            mm(v("P7", o, o + w), v("TR"), v("EA", e, e + w), False, p == 15)
+            if h < 3: mm(v("P7", o + w, o + 64), v("TRE"), v("EA", e + w, e + 64), False, False)
+            e += 256 - o
+            if p == 0:
+                for k in range(4):
+                    mm(n("P5", H4, k), v("IDP"), v("XA", 64 * k, 64 * k + 64), True, False)
+                    mm(n("P5", H4, k), v("IDP"), v(Q, 64 * k, 64 * k + 64), False, True)
+                act(v("XH"), n("P5", H4), scale=0.5, bias=1024.25)
+                act(v("XS"), v("XH"), bias=-1024.0)
+                if not lastr: act(v(Q4n), ind(v(Qn), v("Q4L")))
+        scan(v("CS"), v("D0"), v("P7", 0, 256), 0.0, OP.mult, OP.max)
+        tt(v("OFA"), v("CS", 15, 256, 16), v("DUA"), OP.min)
         if not lastr:
             cp(ind(v("NXR"), v("OFA")), v("NNB"))
-            diag("P3", "UA", "NXR", 192)
-        cp(ind(v("X"), v("OFA")), v("XS"))
-        if lastr: dma(T.yx[:], v("X", 0, 3072), "act")
-        dedupe_off("P0", "CMV", "CSV", "OMV", "DUV", "VF", "OFV")
-        cp(ind(v("ULF"), v("OFV")), v("UV"))
-        if not lastr: cp(v("NXL"), v("P3", 0, 192))
-        if lastr: dma(T.yu[:], v("ULF", 0, 1536))
+            for k in range(2):
+                for r in range(16):
+                    mm(v("P%d" % (3 + k), 0, 96), usl("UA", r), v("NXR", 1536 * k + r, 1536 * k + 1536, 16), r == 0, r == 15)
+                act(v("NXL", 96 * k, 96 * k + 96), v("P%d" % (3 + k), 0, 96))
+                if k == 0:
+                    cp(ind(v("X"), v("OFA")), v("XS"))
+                    act(v("X1", 0, 1536), ind(v("X", 0, 3072), v("NXL", 0, 96)))
+            act(v("X1", 1536, 3072), ind(v("X", 0, 3072), v("NXL", 96, 192)))
+            places()
+        else:
+            cp(ind(v("X"), v("OFA")), v("XS"))
+            dma(T.yx[:], v("X", 0, 3072))
     VE, QE = "VL%d" % NR, "QJ%d" % NR
-    act(v("QI1"), ind(v(QE), v("QIL")))
-    dma(T.yq[:], v("QI1"), "act")
     for h in range(4):
-        cp(v("YV", h, 16, 4), v(VE, 8 * h, 8 * h + 4))
-    dma(T.yv[:], v("YV"))
+        act(v("YQ", h, 256, 4), v(QE, 64 * h, 64 * h + 64))
+    dma(T.yq[:], v("YQ"), "act")
+    for h in range(4):
+        act(v("YV", h, 16, 4), v(VE, 4 + 4 * h, 8 + 4 * h))
+    for c in range(4):
+        dma(T.yv[:, 64 * c:64 * c + 64], v("YV", 4 * c, 4 * c + 4), "act")
     for q in ("V", "S", "P", "G"):
         g.wait_ge(T.sem["q" + q], cnt[q])
     for nm in sorted(total):

@@ -7,6 +7,17 @@ BIG = 131102.0
 OFF = 1536.0
 A = slice(None)
 H4 = slice(0, 4)
+X1V = 640
+
+TESTS = {"V": "d0 d1 r0 a0 a1 a2 a3 b0 b1 b2 b3",
+         "S": "g3 g4 x2 t1 g5 s3 s4 g6 s5 c1 v1 g7 s6 u1 s7 kb",
+         "P": "q3 q4 q5 q6 q7 m0 h3 Z0 h4 A0 A1 A2 A3 h5 Z1 B0 h6 B1 Z2 R1 h7 B2 C1 Z3 B3"}
+FIRST = {"V": "d0 a0 a1 a2 a3 b0 b1 b2 b3",
+         "S": "g1 g2 s1 t0 g3 g4 s2 s3 g5 g6 s4 g7 s5 s6 c1 s7 kb",
+         "P": "q1 q2 h1 q3 q4 q5 h2 q6 A0 Z0 A1 h3 q7 h4 A2 A3 h5 Z1 h6 B0 h7 B1 Z2 C1 B2 Z3 B3"}
+GS, X2V, W1V, X1F = (3, 5), 128, 1536, 1536
+XAT, NAT, UE, ES, DS, X1A, QL = (3, 1), (1, 0), True, 3, False, 0, 1
+XA = 768
 
 SCRATCH = {}
 
@@ -16,16 +27,15 @@ def _buf(dtype, **names):
         SCRATCH[k] = ("sbuf", [128] + (list(n) if isinstance(n, tuple) else [n]), dtype)
 
 
-_buf("bfloat16", X=3328, X1=3072, X2=3072, NXR=3328, BHB=192, BLB=192, QA=1024, QB=1024, DF=2048, AB=4096, L1=4096, L2=4096,
-     LW=1024, XG=2048, EA=2560, E16=16, SG=16, G6=96, WI=96)
+_buf("bfloat16", X=3328, X1=3072, X2=3072, NXR=3328, BHB=192, BLB=192, QA=1024, QB=1024, DF=4096, AB=4096, L1=4096, L2=4096,
+     LW=1024, XG=4096, EA=2560, E16=16, SG=16, G6=96, WI=96, EV0=(4, 4, 4, 16))
 for _c in range(4):
-    for _e in ("EV", "EW"):
-        _buf("bfloat16", **{"%s%d" % (_e, _c): (4, 4, 4 - _c, 16)})
-_buf("int32", ULI=1536, PW=3072, W1=3072, NXN=192, PVN=192, P2N=192, IDN=192, BHI=192, BLI=192, KI=16, RI=256)
-_buf("uint16", NXL=192, PVL=192, P2L=192, Q4L=64, DL=256, BLU=64)
-_buf("float16", DI=256, OHD=256, FB=256, GC=512, VG=256, AR=256, AR2=256, XH=256, ZH=256, NH=384, TN=384, VH=16, NI=8,
-     TD=(4, 2, 2, 16), TF=(4, 2, 2, 16), VR=(4, 4, 16))
-_buf("float32", ULF=1792, IN160=160, IG16=128, I64=64, I192=192, DE=96, SH=96)
+    _buf("bfloat16", **{"EW%d" % _c: (4, 4, 4 - _c, 16)})
+_buf("int32", ULI=1536, PW=3072, W1=3072, NXN=192, PVN=192, P2N=192, IDN=192, BHI=192, BLI=192, KI=16, RM=16)
+_buf("uint16", NXL=192, PVL=192, P2L=192, Q4L=64, Q4F=64, DL=256, BLU=64)
+_buf("float16", DI=256, OHD=256, FB=256, GC=512, VG=256, AR=256, XH=256, ZH=256, NH=384, TN=384, NI=8,
+     TD=(4, 2, 2, 16), TF=(4, 2, 2, 16), TG=(4, 2, 2, 16), VR=(4, 4, 16))
+_buf("float32", ULF=1792, IN160=160, IG16=128, I64=64, I64F=64, I192=192, DE=96, SH=96)
 for _t in range(NR + 1):
     SCRATCH["QJ%d" % _t] = ("sbuf", [128, 256], "bfloat16")
     SCRATCH["VL%d" % _t] = ("sbuf", [128, 32], "uint16")
@@ -36,16 +46,16 @@ for _k in range(8):
     SCRATCH["P%d" % _k] = ("psum", [128, 512] if _k in (3, 4, 7) else [128, 8, 4, 16], "float32")
 _PACK, _WIDTH = {}, {}
 for _w, _names, _dt, _n, _u in (
-        ("sm", "IP P16 G16 G15 IP16 M0 M1 C192 C24 WA WB W5 T1 T2 T3 NP BC ZC", "float32", 8, 1),
+        ("sm", "IP P16 G16 G15 IP16 M0 M1 C192 C24 C4 WA W5 T1 T2 BC ZC", "float32", 8, 1),
         ("ci", "IPI PI EI", "int32", 8, 1),
         ("lu", "KU AU AU2 OFA OFV N1U", "uint16", 16, 16),
-        ("lf", "DUA DUV I16 IV NV VF YV JK", "float32", 16, 16),
-        ("mat", "U U16 UC UA", "bfloat16", 144, 144),
-        ("mh", "UH UW B0 B1 B0N B1N", "float16", 160, 160),
-        ("sh", "IDH IDMH RA", "float16", 128, 128),
-        ("sq", "BB BB4 TR TRE ONE CB C15 IDP IDM", "bfloat16", 128, 128),
-        ("ff", "K16 DB D0 MK KB W2 KEY CS DM OHA", "float32", 256, 256),
-        ("bb", "QM NNB ON MON PO C1 XA XS RV YQ", "bfloat16", 256, 256)):
+        ("lf", "DUA DUV I16 IV VF RC JK", "float32", 16, 16),
+        ("mat", "U U16 U32 UM UC UA", "bfloat16", 144, 144),
+        ("mh", "UH B0 B1 B0N B1N B0S B1S", "float16", 160, 160),
+        ("sh", "IDH RA", "float16", 128, 128),
+        ("sq", "BB BB4 TR TRE ONE CB C15 IDP IDM ID4 IDM4", "bfloat16", 128, 128),
+        ("ff", "K16 DB D0 MK KB K0 W2 KEY RI CS CV DM OHA YG YR", "float32", 256, 256),
+        ("bb", "QM NNB ON MON PO C1 XA XS YQ OH EV N1B", "bfloat16", 256, 256)):
     for _j, _nm in enumerate(_names.split()):
         _PACK[_nm] = (_w, _j * _n)
         _WIDTH[_nm] = _u
@@ -59,6 +69,15 @@ for _t in range(NR):
 
 def shift(t, h):
     return 1 + (t + h - 1) % 7
+
+
+def weave(lists, needs, run):
+    todo = [x.split() for x in lists.values()]
+    done = set()
+    while any(todo):
+        nxt = next(q for q in todo if q and all(x in done for x in needs(q[0])))
+        run(nxt[0])
+        done.add(nxt.pop(0))
 
 
 def rank_program(g, core, T, topo):
@@ -198,6 +217,9 @@ def rank_program(g, core, T, topo):
     def usl(name, r): return v(name, 15 - r, 143 - r)
     def sel(f, e, neg=""): return v("B%d%s" % (f, neg), 16 + 16 * (f - e), 144 + 16 * (f - e))
 
+    def table(q, out, win, lst, lo, hi):
+        (cp if q == "V" else act)(v(out, lo, hi), ind(v(win, 0, 3072), v(lst, lo // 16, hi // 16)))
+
     def diag(out, mat, src, m, last=True):
         for r in range(16):
             mm(out, usl(mat, r), v(src, r, 16 * m, 16), r == 0, last and r == 15)
@@ -219,22 +241,35 @@ def rank_program(g, core, T, topo):
                 b = o + 32 * (m // 2) + 16 * e
                 mm(v(bank, m, 192, 12), sel(m % 2, e), v("TN", b, b + 16), e == 0, e == 1)
 
+    def turn_places(t):
+        if t == 0 or not DS: ts(v("DI"), ind(v("ULI") if t == 0 else v("ULF", 0, 1536), v("VL%d" % t, 4, 20)), -OFF, OP.add)
+        turn(n("TD"), v("DI"))
+        unturn("P5", "TD", A, A)
+
+    def list_places():
+        for q in range(4):
+            ts(v("DL", 64 * q, 64 * q + 64), n("P5", H4, A, slice(4 * q, 4 * q + 4)), OFF, OP.add)
+
     dma(v("NXN"), T.nx[:])
     dma(v("PVN"), T.pv[:], "act")
     dma(v("QM"), T.mv[:])
-    dma(v("X", 0, 3072), T.xd[:])
+    dma(v("X", 0, XA), T.xd[:, 0:XA])
 
-    fill(v("PW", 0, 1024), 0)
+    fill(v("PW", 0, 512), 0)
+    fill(v("PW", 512, 1536), 0)
     iota(v("IPI"), [[1, 1]], 0, 1, False)
     iota(v("IP"), [[1, 1]], 0, 1)
     iota(v("IN160"), [[1, 160]])
-    iota(v("I64"), [[16, 16], [0, 4]])
+    iota(v("PW", 2560, 3072), [[0, 512]], 0, 0, False)
+    iota(v("I64F"), [[1, 4], [64, 4], [0, 4]])
     iota(v("IV"), [[6, 4], [384, 4]])
     iota(v("IG16"), [[16, 8], [0, 16]])
     iota(v("I192"), [[1, 192]])
-    for k in range(1, 3):
-        act(v("PW", 1024 * k, 1024 * k + 1024), v("PW", 0, 1024))
+    iota(v("K16"), [[0, 16], [1, 16]])
+    for k in range(3, 5):
+        act(v("PW", 512 * k, 512 * k + 512), v("PW", 0, 512))
     dma(rows("PW", 4, 0, 3072), T.pv[:])
+    dma(v("X", XA, 3072), T.xd[:, XA:3072])
     dma(v("ULI"), T.ul[:])
     ts(v("EI"), v("IPI"), 4, OP.arith_shift_right, 1, OP.bitwise_and)
     ts(v("PI"), v("IPI"), 15, OP.bitwise_and)
@@ -244,82 +279,101 @@ def rank_program(g, core, T, topo):
     ts(v("M0"), v("M1"), -1.0, OP.mult, 1.0, OP.add)
     ts(v("B1"), v("IN160"), v("IP16"), OP.is_equal, v("M1"), OP.mult)
     ts(v("B0"), v("IN160"), v("IP16"), OP.is_equal, v("M0"), OP.mult)
+    ts(v("C4"), v("P16"), 4.0, OP.mult)
     fill(v("ON"), 1.0)
     tt(v("G16"), v("IP"), v("P16"), OP.subtract)
     to_list("PVN", "P4", 192)
     to_list("NXN", "P3")
-    act(v("Q4L"), v("I64"), bias=v("P16"))
-    for h in range(4):
-        act(v("QJ0", 64 * h, 64 * h + 64), v("QM", h, 256, 4))
-    ts(v("BHI"), v("NXN"), 6, OP.arith_shift_right)
-    ts(v("BLI"), v("NXN"), 63, OP.bitwise_and)
+    act(v("Q4F"), v("I64F"), bias=v("C4"))
+    act(v("QA", 0, 512), ind(v("QM"), v("Q4F", 0, 32)))
     ts(v("G15"), v("G16"), 15.0, OP.add)
-    cp(v("BHB"), v("BHI"))
-    cp(v("BLB"), v("BLI"))
-    ts(v("PVL"), v("P4", 0, 192), OFF, OP.add)
-    act(v("NXL"), v("P3", 0, 192), bias=OFF)
-    act(v("QA"), ind(v("QJ0"), v("Q4L")))
-    ts(v("U"), v("IN160", 0, 144), v("G15"), OP.is_equal)
     ts(v("C24"), v("P16"), 24.0, OP.mult)
     ts(v("C192"), v("P16"), 192.0, OP.mult)
+    ts(v("U"), v("IN160", 0, 144), v("G15"), OP.is_equal)
     ts(v("VL0", 4, 20), v("IV"), v("C24"), OP.add)
-    ts(v("IDN"), v("I192"), v("C192"), OP.add)
-    ts(v("BB"), v("IG16"), v("G16"), OP.is_equal)
-    ts(v("T1"), v("P16"), 8.0, OP.is_equal, 64.0, OP.mult)
-    ts(v("T2"), v("P16"), 9.0, OP.is_equal)
-    ts(v("T3"), v("P16"), 6.0, OP.is_equal)
-    ts(v("W5"), v("P16"), 5.0, OP.is_equal)
-    ts(v("NP"), v("P16"), -1.0, OP.mult)
-    ts(v("E16"), v("IN160", 0, 16), v("P16"), OP.is_equal)
-    ts(v("U16"), v("U"), 16.0, OP.mult)
-    ts(v("UC"), v("U"), 1048576.0, OP.mult)
-    ts(v("BB4"), v("BB"), 4096.0, OP.mult)
-    fill(v("CB"), -61440.0)
-    fill(v("C15"), 15.0 / 128)
-    fill(v("ONE"), 1.0)
     fill(v("MON"), -1.0)
-    keep(v("IDP"), v("ON", 0, 128), [[-1, 128]], OP.is_equal, 0, 1)
-    iota(v("K16"), [[0, 16], [1, 16]])
-    iota(v("I16"), [[16, 16]])
-    keep(v("IDM"), v("MON", 0, 128), [[-1, 128]], OP.is_equal, 0, 1)
-    keep(v("IDMH"), v("MON", 0, 128), [[-1, 128]], OP.is_equal, 0, 1)
-    keep(v("TR"), v("BB4"), [[1, 128]], OP.is_gt, 0, -1)
-    keep(v("TRE"), v("BB4"), [[1, 128]], OP.is_ge, 0, -1)
-    keep(v("D0"), v("ON"), [[0, 16], [1, 16]], OP.is_gt, 0, 0)
-    keep(v("DB"), v("MON"), [[0, 16], [1, 16]], OP.is_gt, 0, 0, 524288.0)
-    iota(v("WI"), [[0, 16], [-16, 6]], 16)
-    keep(v("WI"), v("WI"), [[0, 16], [-1, 6]], OP.is_ge, 0, 0)
-    gcp(v("UH", 0, 144), v("U"), 144)
-    gcp(v("IDH"), v("IDP"), 128)
-    gcp(v("ULF", 0, 1536), v("ULI"), 1536)
-    iota(v("NXR", 0, 3072), [[0, 3072]])
-    cp(v("W1"), ind(v("PW"), v("PVL")))
+    ts(v("PVL"), v("P4", 0, 192), OFF, OP.add)
+    ts(v("IDN"), v("I192"), v("C192"), OP.add)
+    for out, win, lst in (("W1", "PW", "PVL"), ("X1", "X", "NXL"), ("X2", "X1", "NXL")):
+        cut = {"W1": W1V, "X1": X1F, "X2": X2V}[out]
+        if cut: table("V", out, win, lst, 0, cut)
+        table("S", out, win, lst, cut, 3072)
+        if out == "W1":
+            ts(v("NXL"), v("P3", 0, 192), OFF, OP.add)
+            act(v("QA", 512, 1024), ind(v("QM"), v("Q4F", 32, 64)))
+            ts(v("BB"), v("IG16"), v("G16"), OP.is_equal)
+            fill(v("CB"), -61440.0)
+            fill(v("C15"), 15.0 / 128)
+            ts(v("U16"), v("U"), 16.0, OP.mult)
+            ts(v("U32"), v("U"), 32.0, OP.mult)
+            ts(v("UM"), v("U"), -16.0, OP.mult)
+            ts(v("UC"), v("U"), 1048576.0, OP.mult)
+            ts(v("BB4"), v("BB"), 4096.0, OP.mult)
     dma(v("P2N"), rows("W1", 4, 0, 3072))
     dma(rows("PW", 3, 0, 3072), rows("W1", 4, 0, 3072))
     dma(rows("PW", 5, 0, 3072), v("IDN"))
     dma(rows("PW", 6, 0, 3072), T.rc[:])
+    keep(v("IDP"), v("ON", 0, 128), [[-1, 128]], OP.is_equal, 0, 1)
+    iota(v("I16"), [[16, 16]])
+    keep(v("IDM"), v("MON", 0, 128), [[-1, 128]], OP.is_equal, 0, 1)
+    keep(v("TR"), v("BB4"), [[1, 128]], OP.is_gt, 0, -1)
+    keep(v("TRE"), v("BB4"), [[1, 128]], OP.is_ge, 0, -1)
+    keep(v("D0"), v("ON"), [[0, 16], [1, 16]], OP.is_gt, 0, 0)
+    keep(v("DB"), v("MON"), [[0, 16], [1, 16]], OP.is_gt, 0, 0, 524288.0)
+    keep(v("KB"), v("ON"), [[0, 16], [1, 16]], OP.is_gt, 0, 0, -524288.0)
+    iota(v("WI"), [[0, 16], [-16, 6]], 16)
+    keep(v("WI"), v("WI"), [[0, 16], [-1, 6]], OP.is_ge, 0, 0)
+    iota(v("I64"), [[16, 16], [0, 4]])
+    for h in range(4):
+        gcp(v("QJ0", 64 * h, 64 * h + 64), v("QM", h, 256, 4), 64)
+    gcp(v("UH", 0, 144), v("U"), 144)
+    gcp(v("IDH"), v("IDP"), 128)
+    gcp(v("ULF", 0, 1536), v("ULI"), 1536)
+    iota(v("NXR", 0, 3072), [[0, 3072]])
+    turn_places(0)
+    ts(v("BHI"), v("NXN"), 6, OP.arith_shift_right)
+    ts(v("BLI"), v("NXN"), 63, OP.bitwise_and)
+    gcp(v("BHB"), v("BHI"), 192)
+    gcp(v("BLB"), v("BLI"), 192)
+    dma(rows("NXR", 7, 0, 3072), v("BHB"))
+    dma(rows("NXR", 6, 0, 3072), v("BLB"))
+    list_places()
 
-    def late_consts():
-        act(v("B0N"), v("B0"), scale=-1.0)
-        act(v("B1N"), v("B1"), scale=-1.0)
-        act(v("MK"), v("K16"), AF.Square, bias=v("NP"))
-        act(v("WA"), v("T1"), bias=v("T2"))
-        act(v("MK"), v("MK"), AF.Sign)
-        act(v("WB"), v("WA"), bias=v("T3"))
-        act(v("PO"), v("MK"), scale=-4194304.0, bias=OFF)
-        act(v("RA"), v("BB"), scale=v("W5"))
-        act(v("UW", 0, 144), v("U"), scale=v("WB"))
-        act(v("UA"), v("U"), scale=v("WA"))
-        act(v("DUA"), v("I16"), bias=v("P16"))
-        act(v("DUV"), v("DUA"), bias=1536.0)
-        act(v("DUA"), v("DUA"), bias=3072.0)
+    def late_consts(part):
+        if part == 0:
+            ts(v("E16"), v("IN160", 0, 16), v("P16"), OP.is_equal)
+            fill(v("ONE"), 1.0)
+            ts(v("T1"), v("P16"), 7.0, OP.is_equal, 64.0, OP.mult)
+            ts(v("T2"), v("P16"), 6.0, OP.is_equal)
+            ts(v("W5"), v("P16"), 5.0, OP.is_equal)
+            act(v("B0N"), v("B0"), scale=-1.0)
+            act(v("B1N"), v("B1"), scale=-1.0)
+            act(v("P2L"), v("P7", 0, 192), bias=OFF)
+        if part == 1:
+            ts(v("MK"), v("K16"), v("P16"), OP.not_equal)
+            ts(v("PO"), v("MK"), -4194304.0, OP.mult, OFF, OP.add)
+        if part == 3:
+            ts(v("IDM4"), v("IDP"), -4096.0, OP.mult)
+            ts(v("ID4"), v("IDP"), 4096.0, OP.mult)
+            tt(v("WA"), v("T1"), v("T2"), OP.add)
+        if part == 4:
+            ts(v("RA"), v("BB"), v("W5"), OP.mult)
+            ts(v("UA"), v("U"), v("WA"), OP.mult)
+            ts(v("Q4L"), v("I64"), v("P16"), OP.add)
+            ts(v("DUV"), v("I16"), v("P16"), OP.add, 1536.0, OP.add)
+            ts(v("DUA"), v("I16"), v("P16"), OP.add, 3072.0, OP.add)
 
-    def test(x, out, q, op, Q4):
-        tt(v(out, 1024 * q, 1024 * q + 1024), ind(v(x, 0, 3072), v("DL", 64 * q, 64 * q + 64)), v(Q4), op)
+    def steps(lo, hi):
+        for k in range(lo, hi):
+            table("S", "W1", "PW", "P2L", 512 * k, 512 * k + 512)
+        if hi == 6:
+            dma(rows("PW", 2, 0, 3072), rows("W1", 4, 0, 3072))
+            dma(rows("PW", 1, 0, 3072), rows("W1", 3, 0, 3072))
 
-    def sums(bank, mat, src, q, last):
+    def sums(bank, mat, src, q, last, h0=0, h1=4):
         for r in range(16):
-            mm(n(bank, H4, A, slice(4 * q, 4 * q + 4)), usl(mat, r), v(src, 1024 * q + r, 1024 * q + 1024, 16), False, last and r == 15)
+            mm(n(bank, slice(h0, h1), A, slice(4 * q, 4 * q + 4)), usl(mat, r),
+               v(src, 1024 * q + 256 * h0 + r, 1024 * q + 256 * h1, 16), False, last and r == 15)
 
     HC = [(h, c) for c in range(4) for h in range(4)]
 
@@ -327,199 +381,219 @@ def rank_program(g, core, T, topo):
         Q, Qn, VL, Vn = "QJ%d" % t, "QJ%d" % (t + 1), v("VL%d" % t, 4, 20), "VL%d" % (t + 1)
         Q4, Q4n = ("QA", "QB") if t % 2 == 0 else ("QB", "QA")
         first, lastr = t == 0, t == NR - 1
-        UT = v("ULI") if first else v("ULF", 0, 1536)
+        lists = FIRST if first else TESTS
+        tens = lists["P"].split()
 
-        def share(j):
-            b = "P%d" % (3 + j % 2)
-            mm(v(b), v("IDP"), v("XG", 512 * j, 512 * j + 512), True, False)
-            mm(v(b), v("IDM"), v(Q4, 512 * (j % 2), 512 * (j % 2) + 512), False, True)
+        scal = lists["S"].split()
+        nv = min(int(y[1]) for y in scal if y[0] == "g")
 
-        def sgather(j): act(v("XG", 512 * j, 512 * j + 512), ind(v("X", 0, 3072), v("DL", 128 + 32 * j, 160 + 32 * j)))
-        def sabs(j): act(v("AB", 2048 + 512 * j, 2560 + 512 * j), v("P%d" % (3 + j % 2)), AF.Abs)
+        def test(x, out, q, op, m=1024):
+            tt(v(out, 1024 * q, 1024 * q + m), ind(v(x, 0, 3072), v("DL", 64 * q, 64 * q + m // 16)), v(Q4, 0, m), op)
 
-        def squares(c):
+        def needs(x):
+            k, j = x[0], x[1]
+            return {"t": ["d" + j], "s": ["h" + j], "A": ["a" + j], "B": ["b" + j], "R": ["v1"] + ["s3"] * (nv < 4), "u": ["R1"],
+                    "q": [y for y in scal if k == "q" and y == "s%d" % (int(j) - 5)],
+                    "h": ["g" + j, "q" + j], "b": [] if first else ["x2"],
+                    "r": ["d" + j], "m": ["d" + j],
+                    "Z": [y for y in scal + lists["V"].split() + tens if k == "Z" and y in ("t" + j, "r" + j, "m" + j, "s%d" % (2 * int(j)), "s%d" % (2 * int(j) + 1))],
+                    "c": ["A0", "A1", "A2", "A3"], "C": ["c1"], "k": ["Z0", "Z1", "Z2", "Z3"]}.get(k, [])
+
+        def run(x):
+            k, j = x[0], int(x[1]) if x[1].isdigit() else 0
+            last = lambda kinds: x == [y for y in tens if y[0] in kinds][-1]
+            bank = n(("P3", "P4", "P7", "P5", "P6")[(7 - j) % 5])
+            m = min(1024, 512 * nv - 1024 * j)
+            if k == "d": test("X", "DF", j, OP.subtract, m)
+            if k == "t": act(v("AB", 1024 * j, 1024 * j + m), v("DF", 1024 * j, 1024 * j + m), AF.Abs)
+            if k == "v":
+                act(v("VG"), ind(v("PW"), VL))
+                act(v("VF"), VL)
+            if k == "R": mm(n("P6", H4), v("RA"), v("VG"), True, True)
+            if k == "u": act(n("VR"), n("P6", H4))
+            if k == "a": test("X1", "L1", j, OP.is_lt)
+            if k == "b": test("X2", "L2", j, OP.is_lt)
+            if k == "g": act(v("XG", 512 * j, 512 * j + 512), ind(v("X", 0, 3072), v("DL", 32 * j, 32 * j + 32)))
+            if k == "s": act(v("AB", 512 * j, 512 * j + 512), bank, AF.Abs)
+            if k == "x": table("S", "X2", "X1", "NXL", 0, 3072)
+            if k == "c": act(v("C1"), n("P1", H4), AF.Relu, scale=32.0)
+            if k == "k": act(v("K0"), n("P0", H4))
+            if k == "q": mm(bank, v("IDM"), v(Q4, 512 * (j % 2), 512 * (j % 2) + 512), True, False)
+            if k == "h": mm(bank, v("IDP"), v("XG", 512 * j, 512 * j + 512), False, True)
+            if k == "r": ts(v("AB", 1024 * j, 1024 * j + 1024), v("DF", 1024 * j, 1024 * j + 1024), 0.0, OP.max)
+            if k == "m": sums("P0", "UM", "DF", j, False)
+            if k == "Z": sums("P0", "U32" if "m%d" % j in tens else "U16", "AB", j, last("Z"))
+            if k == "A": sums("P1", "UC", "L1", j, last("A"))
+            if k == "B": sums("P2", "UC", "L2", j, last("B"))
+            if k == "C": mm(n("P2", H4), v("IDP"), v("C1"), False, False)
+
+        def equal(c, hs=range(4)):
             if first: return
-            for h in range(4):
-                act(n("EV%d" % c, h), n("VR", A, slice(c, 4)), AF.Square, bias=v("NV", 4 * h + c, 4 * h + c + 1))
-            act(n("EW%d" % c), n("EV%d" % c), AF.Relu, scale=-1.0, bias=1.0)
-
-        def equal(c):
-            if first: return
-            for h in range(4):
+            for h in hs:
                 ts(n("EW%d" % c, h), n("VR", A, slice(c, 4)), v("VF", 4 * h + c, 4 * h + c + 1), OP.is_equal)
 
-        def count(c, start=False, stop=False):
+        def count(c, start=False, stop=False, hs=range(4)):
             if first: return
             if start: mm(n("P1", H4), v("IDP"), v("PO"), True, False)
             src = "EW%d" % c
-            for h in range(4):
+            for h in hs:
                 if c < 3: mm(n("P1", H4, slice(c + 1, 4)), v("BB4"), n(src, h, A, slice(1, 4 - c)), False, False)
                 mm(n("P1", slice(0, h + 1), c), v("TR"), n(src, h, slice(0, h + 1), 0), False, stop and h == 3)
                 if h < 3: mm(n("P1", slice(h + 1, 4), c), v("TRE"), n(src, h, slice(h + 1, 4), 0), False, False)
 
-        if first: act(v("X1"), ind(v("X", 0, 3072), v("NXL")))
-        ts(v("DI"), ind(UT, VL), -OFF, OP.add)
-        turn(n("TD"), v("DI"))
-        unturn("P5", "TD", A, A)
         mm(n("P0", H4), v("C15"), v("ON"), True, False)
         mm(n("P1", H4), v("CB"), v("ON"), True, False)
         mm(n("P2", H4), v("CB"), v("ON"), True, False)
-        for q in range(4):
-            ts(v("DL", 64 * q, 64 * q + 64), n("P5", H4, A, slice(4 * q, 4 * q + 4)), OFF, OP.add)
-        if not first:
-            act(v("VG"), ind(v("PW"), VL))
-            mm(n("P6", H4), v("RA"), v("VG"), True, True)
-        act(v("X2"), ind(v("X1"), v("NXL")))
-        test("X", "DF", 0, OP.subtract, Q4)
+        weave(lists, needs, run)
         if first:
-            to_list("P2N", "P3")
-        test("X", "DF", 1, OP.subtract, Q4)
-        if first:
-            ts(v("P2L"), v("P3", 0, 192), OFF, OP.add)
-            act(v("W1"), ind(v("PW"), v("P2L")))
-            dma(rows("PW", 2, 0, 3072), rows("W1", 4, 0, 3072))
-            dma(rows("PW", 1, 0, 3072), rows("W1", 3, 0, 3072))
-            dma(rows("NXR", 8, 0, 3072), v("BHB"))
-            dma(rows("NXR", 9, 0, 3072), v("BLB"))
-        for q in range(4):
-            test("X1", "L1", q, OP.is_lt, Q4)
-            sums("P1", "UC", "L1", q, q == 3)
-        act(v("AB", 0, 1024), v("DF", 0, 1024), AF.Abs)
-        act(v("AB", 1024, 2048), v("DF", 1024, 2048), AF.Abs)
-        sums("P0", "U16", "AB", 0, False)
-        sums("P0", "U16", "AB", 1, False)
-        sgather(0)
-        sgather(1)
-        test("X2", "L2", 0, OP.is_lt, Q4)
-        share(0)
-        sums("P2", "UC", "L2", 0, False)
-        share(1)
-        sabs(0)
-        sgather(2)
-        sabs(1)
-        share(2)
-        test("X2", "L2", 1, OP.is_lt, Q4)
-        sums("P2", "UC", "L2", 1, False)
-        sgather(3)
-        sums("P0", "U16", "AB", 2, False)
-        share(3)
-        sabs(2)
-        sabs(3)
-        test("X2", "L2", 2, OP.is_lt, Q4)
-        sums("P2", "UC", "L2", 2, False)
-        act(v("C1"), n("P1", H4), AF.Relu, scale=32.0)
-        sums("P0", "U16", "AB", 3, True)
-        mm(n("P2", H4), v("IDP"), v("C1"), False, False)
-        if not first:
-            act(n("VR"), n("P6", H4))
-            act(v("VF"), VL)
-        act(v("KB"), n("P0", H4), scale=-1.0, bias=BIG)
-        test("X2", "L2", 3, OP.is_lt, Q4)
-        sums("P2", "UC", "L2", 3, True)
-        if first: late_consts()
-        else:
-            act(v("NV"), VL, scale=-1.0)
-            act(v("VH"), VL)
-        squares(0)
-        equal(2)
-        tt(v("W2"), n("P2", H4), v("KB"), OP.min)
-        tt(v("KEY"), v("W2"), n("P0", H4), OP.max)
+            to_list("P2N", "P7")
+            late_consts(0)
+        else: equal(0, range(3))
+        scan(v("W2"), v("KB"), v("K0"), 0.0, OP.add, OP.max)
+        tt(v("KEY"), n("P2", H4), v("K0"), OP.max)
+        ts(v("RC"), v("W2", 15, 256, 16), -1.0, OP.mult, BIG, OP.add)
         scan(v("RI"), v("DB"), v("KEY"), 1000000.0, OP.add, OP.min)
-        count(2, True)
+        equal(3, (0,))
+        count(0, True, False, range(3))
         mm(n("P2", H4, A, slice(0, 6)), v("IDP"), v("WI"), True, False)
-        ts(v("KI"), v("RI", 15, 256, 16), 15, OP.bitwise_and)
+        tt(v("RM"), v("RI", 15, 256, 16), v("RC"), OP.min)
+        equal(3, (1,))
+        ts(v("KI"), v("RM"), 15, OP.bitwise_and)
+        equal(3, (2,))
+        act(v("SG"), v("RM"), AF.Sign, bias=-65535.5)
         cp(v("KU"), v("KI"))
+        equal(3, (3,))
+        mm(v("P4", 0, 16), v("ONE"), v("SG"), True, True)
+        count(3)
         tt(v("OHD"), ind(v("E16"), v("KU")), v("DI"), OP.mult)
         diag(v("P3", 0, 16), "UH", "OHD", 16)
-        equal(3)
-        act(v("SG"), v("RI", 15, 256, 16), AF.Sign, bias=-65535.5)
-        mm(v("P4", 0, 16), v("ONE"), v("SG"), True, True)
+        equal(0, (3,))
+        equal(1)
+        if first: late_consts(1)
         act(v("JK"), v("P4", 0, 16), scale=0.25, bias=198655.75 / 16, acc=v("BC"))
         act(v("NI", 0, 1), v("BC"), scale=1.0 / 128, bias=-12.49609375)
         act(v("ZC"), v("NI", 0, 1), scale=-128.0, bias=v("BC"))
         act(v("ZH"), v(Q), scale=0.5, bias=v("ZC"))
         act(v("ZB%d" % t), v("ZH"), bias=-OFF)
         remote("z", t, lambda h: v(Qn, 64 * h, 64 * h + 64), lambda h: v("ZB%d" % t, 64 * h, 64 * h + 64))
-        squares(1)
-        count(0)
+        act(v("OH"), ind(v("E16"), v("KU")))
+        if first: steps(0, GS[0])
+        count(0, False, False, (3,))
+        count(1)
         ts(v("AU"), v("P3", 0, 16), OFF, OP.add)
         ts(v("FB"), ind(v("PW"), v("AU")), -OFF, OP.add)
         turn(n("TF"), v("FB"))
-        unturn("P5", "TF", slice(1, 5), H4)
-        unturn("P0", "TF", slice(0, 6), slice(0, 6), (slice(1, 6), slice(0, 5)))
-        count(3)
-        mm(v("P3", 0, 256), v("IDH"), v("DI"), True, False)
-        mm(v("P3", 0, 256), v("IDMH"), v("OHD"), False, True)
-        count(1, False, True)
+        if first:
+            unturn("P5", "TF", 3, 0)
+            unturn("P6", "TF", slice(3, 5), slice(2, 4))
+            ts(v("AU"), n("P5", H4, A, 0), OFF, OP.add)
+            ts(v("FB"), ind(v("PW"), v("AU")), -OFF, OP.add)
+            turn(n("TG"), v("FB"))
+            unturn("P6", "TG", slice(3, 5), slice(0, 2))
+            terms = [("", "TF", 0, 0, 6), ("N", "TF", 1, 0, 5), ("", "TG", 3, 1, 2), ("N", "TG", 4, 1, 1), ("N", "TG", 2, 2, 1)]
+            for f in range(2):
+                for k, (neg, src, a, b, m) in enumerate(terms):
+                    for e in range(2):
+                        mm(n("P0", H4, slice(f, 4, 2), slice(b, b + m)), sel(f, e, neg), n(src, A, A, e, slice(a, a + m)), k + e == 0, k + e == 5)
+            late_consts(3)
+        else:
+            unturn("P5", "TF", slice(1, 5), H4)
+            unturn("P0", "TF", slice(0, 6), slice(0, 6), (slice(1, 6), slice(0, 5)))
+        equal(2)
         act(v("DE"), n("P0", H4, A, slice(0, 6)))
-        if not first: act(v("RV"), n("P1", H4), AF.Relu, bias=-OFF)
-        ts(v("BLU"), n("P5", H4, A, H4), OFF, OP.add)
+        if first: steps(GS[0], GS[1])
+        else:
+            count(2)
+            mm(n("P1", H4), v("IDH"), n("VR"), False, True)
+            act(v("CV"), n("P1", H4), bias=-OFF)
+        ts(v("BLU"), n("P6" if first else "P5", H4, A, H4), OFF, OP.add)
         tt(v("LW"), ind(v("X", 0, 3072), v("BLU")), v(Q4), OP.is_lt)
         for r in range(16):
             mm(n("P2", H4, A, slice(1, 5)), usl("U", r), v("LW", r, 1024, 16), False, r == 15)
+        mm(v("P3", 0, 256), v("IDH"), v("DI"), True, False)
+        mm(v("P3", 0, 256), v("IDM4"), v("OH"), False, True)
+        mm(v("P7", 0, 256), v("IDP"), v("PO"), True, False)
         act(v("DM"), v("P3", 0, 256), bias=OFF)
         act(v(Qn, 0, 64), v("ZB%d" % t, 0, 64))
-        mm(v("P7", 0, 256), v("IDP"), v("PO"), True, False)
-        if not first:
-            diag(n("P1", 0, 0), "U", "RV", 16, False)
-            mm(n("P1", 0, 0), v("IDH"), v("VH"), False, True)
+        mm(n("P0", H4), v("ID4"), v("OH"), True, False)
+        if first: late_consts(4)
+        else:
+            scan(v("CS"), v("D0"), v("CV"), 0.0, OP.mult, OP.max)
+            tt(v("OFV"), v("CS", 15, 256, 16), v("DUV"), OP.min)
         ts(v("G6"), n("P2", H4, A, slice(0, 6)), 7.5, OP.is_lt)
         scan(v("SH"), v("DE"), v("G6"), 0.0, OP.add, OP.mult)
         ts(v("AU2"), v("SH", 5, 96, 6), OFF, OP.add)
         ts(v("GC", 0, 256), ind(v("PW"), v("AU2")), -OFF, OP.add)
-        if not lastr: act(v("GC", 256, 512), ind(v("NXR", 0, 3072), v("AU2")))
+        if not lastr: act(v("N1B"), ind(v("NXR", 0, 3072), v("AU2")))
         act(v("XA"), ind(v("X", 0, 3072), v("AU2")))
         for h in range(4):
             mm(n("P6", H4, h), v("RA"), v("GC", 64 * h, 64 * h + 64), True, True)
-        mm(n("P0", H4), v("RA"), v("GC", 0, 256), True, True)
-        m = 16 if lastr else 32
-        diag(v("P3", 0, m), "UW", "GC", m)
-        if not first: tt(v("OFV"), n("P1", 0, 0), v("DUV"), OP.min)
+        turn(n("TF"), v("GC", 0, 256))
+        unturn("P5", "TF", 6, 0)
+        mm(n("P0", H4), v("RA"), v("GC", 0, 256), False, True)
         cp(v("AR"), n("P6", H4))
-        act(v("AR2"), n("P0", H4))
-        act(v("MW%d" % t), v("P3", 0, 16), bias=66 * OFF)
+        act(v("MW%d" % t), n("P5", H4, A, 0), bias=OFF)
         remote("w", t, lambda h: v(Vn, 4 + 4 * h, 8 + 4 * h), lambda h: v("MW%d" % t, 4 * h, 4 * h + 4))
-        if not lastr:
+        if lastr: act(v("OHA"), n("P0", H4), bias=OFF - 4096.0)
+        if t >= ES:
             for h in range(4):
-                act(v("N1U", h, 16, 4), v("P3", 16 + 4 * h, 20 + 4 * h))
-            act(v("NNB"), ind(v("NXR", 0, 3072), v("N1U")))
+                act(v("EV", 64 * h, 64 * h + 64), v("AR", 192, 256), AF.Square, scale=-1.0, bias=v("SH", 24 * h + 23, 24 * h + 24))
+            act(v("EA", 2304, 2560), v("EV"), AF.Relu, scale=-1.0, bias=1.0)
+        if not lastr: act(v("OHA"), n("P0", H4), bias=OFF - 4096.0)
         act(v(Vn, 4, 8), v("MW%d" % t, 0, 4))
 
+        def followers():
+            diag(n("P1", 0, 0), "UA", "N1B", 16)
+            for h in range(4):
+                act(v("N1U", h, 16, 4), n("P1", 0, 0, slice(4 * h, 4 * h + 4)))
+            act(v("NNB"), ind(v("NXR", 0, 3072), v("N1U")))
+            if t >= QL: act(v(Q4n), ind(v(Qn), v("Q4L")))
+
         def places():
-            tt(v("OHA"), ind(v("E16"), v("KU")), v("AR2"), OP.mult)
-            tt(ind(v("ULF"), VL if first else v("OFV")), v("DM"), v("OHA"), OP.add)
-        if lastr:
-            places()
-            dma(T.yu[:], v("ULF", 0, 1536))
+            tt(ind(v("ULF"), VL if first else v("OFV")), v("DM"), v("OHA"), OP.max)
+            if lastr: dma(T.yu[:], v("ULF", 0, 1536))
+        for k in range(4):
+            mm(n("P2", H4, k), v("IDP"), v("XA", 64 * k, 64 * k + 64), True, False)
+            mm(n("P2", H4, k), v("IDP"), v(Q, 64 * k, 64 * k + 64), False, True)
+        act(v("XH"), n("P2", H4), scale=0.5, bias=1024.25)
+        act(v("XS"), v("XH"), bias=-1024.0)
         mm(v("P7", 0, 256), v("IDH"), v("AR"), False, False)
         e = 0
         for h, c in HC:
             p, o, w = 4 * h + c, 64 * c, 16 * h + 16
-            ts(v("EA", e, e + 256 - o), v("AR", o, 256), v("SH", 6 * p + 5, 6 * p + 6), OP.is_equal)
+            if c < 3 or t < ES: ts(v("EA", e, e + 256 - o), v("AR", o, 256), v("SH", 6 * p + 5, 6 * p + 6), OP.is_equal)
             if c < 3: mm(v("P7", o + 64, 256), v("BB4"), v("EA", e + 64, e + 256 - o), False, False)
             mm(v("P7", o, o + w), v("TR"), v("EA", e, e + w), False, p == 15)
             if h < 3: mm(v("P7", o + w, o + 64), v("TRE"), v("EA", e + w, e + 64), False, False)
             e += 256 - o
-            if p == 0:
-                for k in range(4):
-                    mm(n("P5", H4, k), v("IDP"), v("XA", 64 * k, 64 * k + 64), True, False)
-                    mm(n("P5", H4, k), v("IDP"), v(Q, 64 * k, 64 * k + 64), False, True)
-                act(v("XH"), n("P5", H4), scale=0.5, bias=1024.25)
-                act(v("XS"), v("XH"), bias=-1024.0)
-                if not lastr: act(v(Q4n), ind(v(Qn), v("Q4L")))
+            if lastr and (h, c) == (2, 0): places()
+            if not lastr and (h, c) == NAT: followers()
+            if first and (h, c) == NAT:
+                steps(GS[1], 6)
+                act(v(Q4n), ind(v(Qn), v("Q4L")))
+        if not lastr and UE: places()
         scan(v("CS"), v("D0"), v("P7", 0, 256), 0.0, OP.mult, OP.max)
         tt(v("OFA"), v("CS", 15, 256, 16), v("DUA"), OP.min)
         if not lastr:
             cp(ind(v("NXR"), v("OFA")), v("NNB"))
-            for k in range(2):
+            def third(k):
                 for r in range(16):
-                    mm(v("P%d" % (3 + k), 0, 96), usl("UA", r), v("NXR", 1536 * k + r, 1536 * k + 1536, 16), r == 0, r == 15)
-                act(v("NXL", 96 * k, 96 * k + 96), v("P%d" % (3 + k), 0, 96))
-                if k == 0:
-                    cp(ind(v("X"), v("OFA")), v("XS"))
-                    act(v("X1", 0, 1536), ind(v("X", 0, 3072), v("NXL", 0, 96)))
-            act(v("X1", 1536, 3072), ind(v("X", 0, 3072), v("NXL", 96, 192)))
-            places()
+                    mm(v(("P3", "P4", "P7" if X1V else "P4")[k], 64 * k, 64 * k + 64), usl("UA", r), v("NXR", 1024 * k + r, 1024 * k + 1024, 16), r == 0, r == 15)
+            third(0)
+            third(1)
+            if DS: act(v("DI"), ind(v("ULF", 0, 1536), v(Vn, 4, 20)), bias=-OFF)
+            act(v("NXL", 0, 64), v("P3", 0, 64))
+            cp(ind(v("X"), v("OFA")), v("XS"))
+            table("S", "X1", "X", "NXL", 0, 1024)
+            turn_places(t + 1)
+            third(2)
+            if X1V:
+                cp(v("NXL", 64, 128), v("P4", 64, 128))
+                table("V", "X1", "X", "NXL", 1024, 1024 + X1V)
+                act(v("NXL", 128, 192), v("P7", 128, 192))
+            else: act(v("NXL", 64, 192), v("P4", 64, 192))
+            table("S", "X1", "X", "NXL", 1024 + X1V, 3072)
+            list_places()
         else:
             cp(ind(v("X"), v("OFA")), v("XS"))
             dma(T.yx[:], v("X", 0, 3072))
@@ -527,10 +601,11 @@ def rank_program(g, core, T, topo):
     for h in range(4):
         act(v("YQ", h, 256, 4), v(QE, 64 * h, 64 * h + 64))
     dma(T.yq[:], v("YQ"), "act")
+    act(v("YG"), ind(v("PW"), v(VE, 4, 20)))
     for h in range(4):
-        act(v("YV", h, 16, 4), v(VE, 4 + 4 * h, 8 + 4 * h))
-    for c in range(4):
-        dma(T.yv[:, 64 * c:64 * c + 64], v("YV", 4 * c, 4 * c + 4), "act")
+        act(v("YR", h, 256, 4), v("YG", 64 * h, 64 * h + 64))
+    b = _PACK["YR"][1]
+    dma(T.yv[:], (T.ff[5:128:16, b:b + 256], v("YR")[1], []), "act")
     for q in ("V", "S", "P", "G"):
         g.wait_ge(T.sem["q" + q], cnt[q])
     for nm in sorted(total):

@@ -7,17 +7,19 @@ BIG = 131102.0
 OFF = 1536.0
 A = slice(None)
 H4 = slice(0, 4)
-X1V = 640
 
-TESTS = {"V": "d0 d1 r0 a0 a1 a2 a3 b0 b1 b2 b3",
-         "S": "g3 g4 x2 t1 g5 s3 s4 g6 s5 c1 v1 g7 s6 u1 s7 kb",
-         "P": "q3 q4 q5 q6 q7 m0 h3 Z0 h4 A0 A1 A2 A3 h5 Z1 B0 h6 B1 Z2 R1 h7 B2 C1 Z3 B3"}
-FIRST = {"V": "d0 a0 a1 a2 a3 b0 b1 b2 b3",
-         "S": "g1 g2 s1 t0 g3 g4 s2 s3 g5 g6 s4 g7 s5 s6 c1 s7 kb",
-         "P": "q1 q2 h1 q3 q4 q5 h2 q6 A0 Z0 A1 h3 q7 h4 A2 A3 h5 Z1 h6 B0 h7 B1 Z2 C1 B2 Z3 B3"}
-GS, X2V, W1V, X1F = (3, 5), 128, 1536, 1536
-XAT, NAT, UE, ES, DS, X1A, QL = (3, 1), (1, 0), True, 3, False, 0, 1
-XA = 768
+TESTS = {"V": "N X n1 y8-16 y16-17 j l0 l1 l2 l3 d0 r0 a0 a1 a2 a3 b0 b1 b2 b3 w8",
+         "S": "W i n0 y0-8 n2 y17-24 v g23 x0-24 s2 s3 g45 s4 s5 g67 s6 s7 c k",
+         "P": "T0 T1 T2 J q2 q3 o D q4 q5 q6 m0 h2 Z0 h3 A0 p q7 A1 A2 h4 Z1 A3 h5 B0 h6 B1 Z2 h7 B2 Z3 C B3",
+         "Y": "Q"}
+FIRST = {"V": "l0 l1 l2 l3 d0 a0 L a1 a2 a3 b0 b1 b2 b3",
+         "S": "g1 g2 s1 t0 g3 M g5 g4 s2 g7 s3 g6 s4 s5 s6 s7 c k",
+         "P": "o D q1 q4 q2 h1 q3 h2 K q6 A0 Z0 A1 p h3 A2 q5 q7 h4 A3 h5 Z1 h6 B0 h7 B1 Z2 Z3 B2 C B3"}
+SHARE = {"W1": 1536, "X1": 1536, "X2": 256}
+STEPS = (416, 416, 416, 416, 416, 480)
+COST = dict(cycle=0.95, pe=0.48, gather=1.55, scatter=3.5, act=65, hop=120, dma=700, row=45, rate=18.0, issue=300, first=1500,
+            remote=600, far=55)
+PASSES = 2
 
 SCRATCH = {}
 
@@ -27,15 +29,13 @@ def _buf(dtype, **names):
         SCRATCH[k] = ("sbuf", [128] + (list(n) if isinstance(n, tuple) else [n]), dtype)
 
 
-_buf("bfloat16", X=3328, X1=3072, X2=3072, NXR=3328, BHB=192, BLB=192, QA=1024, QB=1024, DF=4096, AB=4096, L1=4096, L2=4096,
-     LW=1024, XG=4096, EA=2560, E16=16, SG=16, G6=96, WI=96, EV0=(4, 4, 4, 16))
-for _c in range(4):
-    _buf("bfloat16", **{"EW%d" % _c: (4, 4, 4 - _c, 16)})
-_buf("int32", ULI=1536, PW=3072, W1=3072, NXN=192, PVN=192, P2N=192, IDN=192, BHI=192, BLI=192, KI=16, RM=16)
-_buf("uint16", NXL=192, PVL=192, P2L=192, Q4L=64, Q4F=64, DL=256, BLU=64)
-_buf("float16", DI=256, OHD=256, FB=256, GC=512, VG=256, AR=256, XH=256, ZH=256, NH=384, TN=384, NI=8,
-     TD=(4, 2, 2, 16), TF=(4, 2, 2, 16), TG=(4, 2, 2, 16), VR=(4, 4, 16))
-_buf("float32", ULF=1792, IN160=160, IG16=128, I64=64, I64F=64, I192=192, DE=96, SH=96)
+_buf("bfloat16", X=3328, X1=3072, X2=3072, NXR=3328, BHB=192, BLB=192, QA=1024, QB=1024, QC=(4, 4, 16), QD=(16, 4, 16), DF=1024,
+     AB=4096, L1=4096, L2=4096, LW=1024, XG=4096, EA=2560, E16=16, SG=16, G6=96, WI=96, EW=(4, 4, 4, 4, 16))
+_buf("int32", ULI=1536, PW=3072, W1=3072, NXN=192, PVN=192, P2N=192, IDW=3072, BHI=192, BLI=192, KI=16, RM=16)
+_buf("uint16", NXL=192, PVL=192, P2L=192, DL=256, BLU=64, VC=48)
+_buf("float16", DI=256, FB=256, R4=256, XH=256, ZH=256, NH=384, TN=384, NI=8, VR=256, AR=256, IDH=128,
+     TD=(4, 2, 2, 16), TF=(4, 2, 2, 16), TG=(4, 2, 2, 16))
+_buf("float32", ULF=1792, IN160=160, SHF=160, IG16=128, DE=96, DR=96, SH=96, SR=96)
 for _t in range(NR + 1):
     SCRATCH["QJ%d" % _t] = ("sbuf", [128, 256], "bfloat16")
     SCRATCH["VL%d" % _t] = ("sbuf", [128, 32], "uint16")
@@ -46,16 +46,15 @@ for _k in range(8):
     SCRATCH["P%d" % _k] = ("psum", [128, 512] if _k in (3, 4, 7) else [128, 8, 4, 16], "float32")
 _PACK, _WIDTH = {}, {}
 for _w, _names, _dt, _n, _u in (
-        ("sm", "IP P16 G16 G15 IP16 M0 M1 C192 C24 C4 WA W5 T1 T2 BC ZC", "float32", 8, 1),
-        ("ci", "IPI PI EI", "int32", 8, 1),
-        ("lu", "KU AU AU2 OFA OFV N1U", "uint16", 16, 16),
-        ("lf", "DUA DUV I16 IV VF RC JK", "float32", 16, 16),
-        ("mat", "U U16 U32 UM UC UA", "bfloat16", 144, 144),
-        ("mh", "UH B0 B1 B0N B1N B0S B1S", "float16", 160, 160),
-        ("sh", "IDH RA", "float16", 128, 128),
-        ("sq", "BB BB4 TR TRE ONE CB C15 IDP IDM ID4 IDM4", "bfloat16", 128, 128),
-        ("ff", "K16 DB D0 MK KB K0 W2 KEY RI CS CV DM OHA YG YR", "float32", 256, 256),
-        ("bb", "QM NNB ON MON PO C1 XA XS YQ OH EV N1B", "bfloat16", 256, 256)):
+        ("sm", "IP P16 G16 G15 C24 WA W11 T1 T2 BC ZC", "float32", 8, 1),
+        ("ci", "IPI PI", "int32", 8, 1),
+        ("lu", "KU AU AU2 AU4 OFA OFV N1U", "uint16", 16, 16),
+        ("lf", "DUA DUV I16 IV VF D15 JK", "float32", 16, 16),
+        ("mat", "U UM UC UA", "bfloat16", 144, 144),
+        ("mh", "UR B0 B1 B0N B1N", "float16", 160, 160),
+        ("sq", "BB4 TR TRE ONE CB C15 IDP IDM ID4 IDM4", "bfloat16", 128, 128),
+        ("ff", "DB D0 K1 K0 DD SL RI CS CV CW DM OHA YG YR", "float32", 256, 256),
+        ("bb", "K16 MK QM NNB ON MON PO C1 XA XS YQ OH N1B NF", "bfloat16", 256, 256)):
     for _j, _nm in enumerate(_names.split()):
         _PACK[_nm] = (_w, _j * _n)
         _WIDTH[_nm] = _u
@@ -65,6 +64,7 @@ NDMA = 30
 SEMAPHORES = ["qV", "qS", "qP", "qG", "sent"] + ["d%d" % _k for _k in range(NDMA)]
 for _t in range(NR):
     SEMAPHORES += ["z%d" % _t, "w%d" % _t]
+PLAN = []
 
 
 def shift(t, h):
@@ -72,12 +72,88 @@ def shift(t, h):
 
 
 def weave(lists, needs, run):
-    todo = [x.split() for x in lists.values()]
+    todo = {q: x.split() for q, x in lists.items()}
+    every = [x for q in todo for x in todo[q]]
     done = set()
-    while any(todo):
-        nxt = next(q for q in todo if q and all(x in done for x in needs(q[0])))
-        run(nxt[0])
-        done.add(nxt.pop(0))
+    while any(todo.values()):
+        q = next(q for q in todo if todo[q] and all(y in done for y in every if needs(todo[q][0], y)))
+        run(todo[q][0], q)
+        done.add(todo[q].pop(0))
+
+
+def is_bank(nm):
+    return nm[0] == "P" and nm[1:].isdigit()
+
+
+def apart(x, y):
+    return (x[2] <= y[1] or y[2] <= x[1] or x[4] is not None and y[4] is not None and x[4] != y[4]
+            or x[3] == y[3] > 1 and (x[1] - y[1]) % x[3] != 0)
+
+
+def before(calls):
+    log, bank, pred = {}, {}, []
+    for k, (q, _t, lead, w, r, flags, _g) in enumerate(calls):
+        need = {}
+        for keys, wr in ((w, True), (r, False)):
+            for x in keys:
+                nm = x[0]
+                if is_bank(nm):
+                    B = bank.setdefault(nm, {"start": None, "mid": [], "other": None, "wrote": None})
+                    if q == "P":
+                        ps = [B["start"], B["other"]] + (B["mid"] if flags[0] or flags[1] else [])
+                        if flags[0]: B["start"], B["mid"] = k, []
+                        else: B["mid"].append(k)
+                    else:
+                        ps = [B["start"], B["other"], B["wrote"]] + B["mid"]
+                    for j in ps:
+                        if j is not None and j != k:
+                            free = calls[j][0] == q and (q == "P" or wr or j != B["wrote"])
+                            need[j] = max(need.get(j, 0), 0 if free else COST["hop"])
+                    if q != "P":
+                        B["other"] = k
+                        if any(y[0] == nm for y in w) and (not wr or all(y[0] != nm for y in r)): B["wrote"] = k
+                    continue
+                L = log.setdefault(nm, [])
+                for y, wrote, j in L:
+                    if j != k and (wrote or wr) and not apart(x, y): need[j] = 0 if calls[j][0] == q == "P" else COST["hop"]
+                if wr and x[3] == 1 and x[4] is None: L[:] = [e for e in L if not (x[1] <= e[0][1] and e[0][2] <= x[2])]
+                L.append((x, wr, k))
+        pred.append([(j, d + lead) for j, d in need.items()])
+    return pred
+
+
+def place(calls, pred, seq, gaps=True):
+    start, end, busy = {}, {}, {}
+    for k in seq:
+        q, d = calls[k][0], calls[k][1]
+        t = max([end[j] + x for j, x in pred[k]], default=calls[k][2])
+        B = busy.setdefault(q, [])
+        i = len(B)
+        if gaps:
+            while i and B[i - 1][1] > t: i -= 1
+            while i < len(B) and B[i][0] < t + d:
+                t = max(t, B[i][1]); i += 1
+        elif B: t = max(t, B[-1][1])
+        B.insert(i, (t, t + d))
+        start[k], end[k] = t, t + d
+    return start, end
+
+
+def arrange(calls):
+    pred = before(calls)
+    succ = [[] for _ in calls]
+    for k, ps in enumerate(pred):
+        for j, x in ps: succ[j].append((k, x))
+    back = [c[:2] + (0,) for c in calls]
+    start, end = place(calls, pred, range(len(calls)), False)
+    tried = []
+    for _ in range(PASSES):
+        late = place(back, succ, sorted(start, key=lambda k: (-end[k], -k)))[1]
+        start, end = place(calls, pred, sorted(start, key=lambda k: (-late[k], k)))
+        tried.append((max(end.values()), len(tried), start, end))
+    start, end = min(tried)[2:]
+    ready = lambda k: max([end[j] + x for j, x in pred[k]], default=0) if calls[k][5] == "act" else start[k]
+    return sorted(start, key=lambda k: (ready(k) - calls[k][2], k))
 
 
 def rank_program(g, core, T, topo):
@@ -100,18 +176,27 @@ def rank_program(g, core, T, topo):
         if hi is None: hi = _WIDTH[name] if name in _PACK else T[w].shape[1]
         lo, hi = lo + b, hi + b
         ap = T[w][:, lo:hi:step] if step != 1 else T[w][:, lo:hi]
-        return (ap, [(w, lo, hi, step, None)], [])
+        return (ap, [(w, lo, hi, step, None)], [], len(range(lo, hi, step)))
 
-    def n(name, *ix):
+    def n(name, *ix, key=None):
         f = ix[0] if ix else A
         lo, hi = (f, f + 1) if isinstance(f, int) else (f.start or 0, f.stop or 64)
-        return (T[name][(A,) + ix], [(name, lo, hi, 1, None)], [])
+        m = 1
+        for k, d in enumerate(SCRATCH[name][1][1:]):
+            if k >= len(ix) or isinstance(ix[k], slice): m *= len(range(d)[ix[k] if k < len(ix) else A])
+        return (T[name][(A,) + ix], [(name,) + (key or (lo, hi, 1)) + (None,)], [], m)
 
-    def rows(name, f, lo, hi):
-        return (T[name][f:128:16, lo:hi], [(name, lo, hi, 1, f)], [])
+    def ew(h, c, d, hs=A):
+        return n("EW", h, c, d, hs, key=(4 * h, 4 * h + 4, 1) if c == A else (4 * h + c, 4 * h + c + 1, 1))
+
+    def rows(name, f, lo=0, hi=3072):
+        w, b = _PACK.get(name, (name, 0))
+        return (T[w][f:128:16, lo + b:hi + b], [(w, lo + b, hi + b, 1, f)], [], hi - lo)
 
     def ind(win, off):
-        return (win[0].indirect(off[0]), win[1], off[1])
+        return (win[0].indirect(off[0]), win[1], off[1], 16 * off[3])
+
+    def width(x): return 4 if SCRATCH[x[1][0][0]][2] in ("float32", "int32") else 2
 
     def order(q, w, r):
         need = {}
@@ -119,15 +204,11 @@ def rank_program(g, core, T, topo):
             if tok[0] == q == "P": return
             if know[q].get(tok[0], 0) < tok[1]: need[tok[0]] = max(need.get(tok[0], 0), tok[1])
         for keys, wr in ((w, True), (r, False)):
-            for (nm, lo, hi, stp, prt) in keys:
-                ps = nm[0] == "P" and nm[1:].isdigit()
-                for (l2, h2, kind, tok, s2, p2) in log.get(nm, []):
-                    if ps:
+            for x in keys:
+                for y, kind, tok in log.get(x[0], []):
+                    if is_bank(x[0]):
                         if tok[0] != q or (kind == "w" and not wr): dep(tok)
-                    elif l2 < hi and lo < h2 and (kind == "w" or wr):
-                        if prt is not None and p2 is not None and prt != p2: continue
-                        if stp == s2 and stp > 1 and (lo - l2) % stp: continue
-                        dep(tok)
+                    elif (kind == "w" or wr) and not apart(x, y): dep(tok)
         for a in sorted(need):
             if any(b != a and snap.get((b, need[b]), {}).get(a, 0) >= need[a] for b in need): continue
             ENG[q].wait_ge(T.sem["q" + a if a in cnt else a], need[a] * unit[a])
@@ -137,62 +218,90 @@ def rank_program(g, core, T, topo):
 
     def note(tok, w, r):
         for keys, kind in ((w, "w"), (r, "r")):
-            for (nm, lo, hi, stp, prt) in keys:
-                ps = nm[0] == "P" and nm[1:].isdigit()
-                if ps: lo, hi = 0, 512
-                L = log.setdefault(nm, [])
-                if ps and kind == "r":
-                    L[:] = [e for e in L if e[2] == "w" and e[3][0] == "P"][-1:] + [(lo, hi, "r", tok, 1, None)]
+            for x in keys:
+                L = log.setdefault(x[0], [])
+                if is_bank(x[0]):
+                    L[:] = ([e for e in L if e[1] == "w"][-1:] if kind == "r" else []) + [(x, kind, tok)]
                 else:
-                    if kind == "w" and stp == 1 and prt is None: L[:] = [e for e in L if not (lo <= e[0] and e[1] <= hi)]
-                    L.append((lo, hi, kind, tok, stp, prt))
+                    if kind == "w" and x[3] == 1 and x[4] is None: L[:] = [e for e in L if not (x[1] <= e[0][1] and e[0][2] <= x[2])]
+                    L.append((x, kind, tok))
 
-    def emit(q, fn, outs, ins):
+    calls = []
+
+    def emit(q, fn, outs, ins, twice=False, flags=None, gp=None):
         w, r = [], []
         for o in outs: w += o[1]; r += o[2]
         for i in ins: r += i[1] + i[2]
-        order(q, w, r)
-        cnt[q] += 1
-        fn().then_inc(T.sem["q" + q], 1)
-        now = dict(know[q]); now[q] = cnt[q]
-        snap[(q, cnt[q])] = now
-        note((q, cnt[q]), w, r)
+        m, C = outs[0][3], COST
+        if q == "P": time = C["pe"] * max(64, m)
+        elif q == "G": time = gp + 2 * C["cycle"] * m
+        elif outs[0][2]: time = 50 + C["scatter"] * C["cycle"] * m
+        elif ins and ins[0][2]: time = {"V": 50, "S": 65}[q] + C["gather"] * C["cycle"] * m
+        elif q == "S": time = C["act"] + C["cycle"] * m
+        else:
+            half = all(width(x) == 2 for x in outs + ins if x[3] == m)
+            both = twice and not any(is_bank(x[1][0][0]) for x in ins)
+            time = C["cycle"] * max(64, m * (0.5 if half else 1) * (2 if both else 1))
+
+        def go():
+            order(q, w, r)
+            cnt[q] += 1
+            fn().then_inc(T.sem["q" + q], 1)
+            now = dict(know[q]); now[q] = cnt[q]
+            snap[(q, cnt[q])] = now
+            note((q, cnt[q]), w, r)
+        calls.append((q, time, 0, w, r, flags, go))
 
     def dma(out, in_, q="sync"):
         qk = {"sync": "sync", "act": "S"}[q]
         w = out[1] if isinstance(out, tuple) else []
         r = in_[1] if isinstance(in_, tuple) else []
-        order(qk, w, r)
-        nm = "d%d" % nd[0]; nd[0] += 1
-        o = out[0] if isinstance(out, tuple) else out
-        i = in_[0] if isinstance(in_, tuple) else in_
-        ENG[q].dma_start(o, i).then_inc(T.sem[nm], 16)
-        unit[nm] = 16; total[nm] = 1
-        snap[(nm, 1)] = dict(know[qk])
-        note((nm, 1), w, r)
+        sides = [x for x in (out, in_) if isinstance(x, tuple)]
+        full = [x for x in sides if x[1][0][4] is None]
+        x = (full or sides)[0]
+        time = 8 * (COST["row"] + x[3] * width(x) / COST["rate"]) if full else COST["row"] + x[3] * width(x) / 2 / COST["rate"]
+
+        def go():
+            order(qk, w, r)
+            nm = "d%d" % nd[0]; nd[0] += 1
+            o = out[0] if isinstance(out, tuple) else out
+            i = in_[0] if isinstance(in_, tuple) else in_
+            ENG[q].dma_start(o, i).then_inc(T.sem[nm], 16)
+            unit[nm] = 16; total[nm] = 1
+            snap[(nm, 1)] = dict(know[qk])
+            note((nm, 1), w, r)
+        calls.append(("D", time, COST["dma"], w, r, q, go))
 
     def engines(src, dst, h):
-        return topo.engines(src, dst)[2 * h - 2:2 * h]
+        return topo.engines(src, dst)[{1: slice(0, 4), 2: slice(4, 8), 3: slice(0, 8)}[h]]
 
     def remote(kind, t, dst, src):
         nm = "%s%d" % (kind, t)
-        order("G", [], [k for h in range(1, 4) for k in src(h)[1]])
-        trs = []
-        for h in range(1, 4):
-            d = T.cores[(me + shift(t, h)) % N]
-            rid, pid, _s = topo.addr(d)
-            es = engines(core, d, h)
-            trs.append(RemoteDMATransfer(dst_ids=[DstId(rid=rid, pnc=pid)], dma_engine_mask=sum(1 << e for e in es),
-                                         remote_sem=T.sem[nm], src=src(h)[0], dst=dst(h)[0]))
-            sent[0] += len(es)
-        g.remote_dma_fused(trs, local_sem=T.sem.sent)
-        unit[nm] = sum(len(engines(T.cores[(me - shift(t, h)) % N], core, h)) for h in range(1, 4))
-        total[nm] = 1
-        snap[(nm, 1)] = {}
-        note((nm, 1), [k for h in range(1, 4) for k in dst(h)[1]], [])
+        src, dst = [None] + [src(h) for h in range(1, 4)], [None] + [dst(h) for h in range(1, 4)]
+        w, r = [k for x in dst[1:] for k in x[1]], [k for x in src[1:] for k in x[1]]
+
+        def go():
+            order("G", [], r)
+            for hs in ((1, 2), (3,)):
+                trs = []
+                for h in hs:
+                    d = T.cores[(me + shift(t, h)) % N]
+                    rid, pid, _s = topo.addr(d)
+                    es = engines(core, d, h)
+                    trs.append(RemoteDMATransfer(dst_ids=[DstId(rid=rid, pnc=pid)], dma_engine_mask=sum(1 << e for e in es),
+                                                 remote_sem=T.sem[nm], src=src[h][0], dst=dst[h][0]))
+                    sent[0] += len(es)
+                g.remote_dma_fused(trs, local_sem=T.sem.sent)
+            unit[nm] = sum(len(engines(T.cores[(me - shift(t, h)) % N], core, h)) for h in range(1, 4))
+            total[nm] = 1
+            snap[(nm, 1)] = {}
+            note((nm, 1), w, [])
+        tok = [(nm, 0, 1, 1, None)]
+        calls.append(("G", 2 * COST["issue"] + COST["first"] * (nm == "z0"), 0, tok, r, None, go))
+        calls.append(("R", 48 * (COST["far"] + src[1][3] * 2 / COST["rate"]), COST["remote"], w, tok, None, None))
 
     def cp(o, i): emit("V", lambda: g.vector.tensor_copy(o[0], i[0]), [o], [i])
-    def tt(o, a, b, op): emit("V", lambda: g.vector.tensor_tensor(o[0], a[0], b[0], op), [o], [a, b])
+    def tt(o, a, b, op): emit("V", lambda: g.vector.tensor_tensor(o[0], a[0], b[0], op), [o], [a, b], True)
     def ts(o, a, s1, op0, s2=None, op1=None):
         ex = [s for s in (s1, s2) if isinstance(s, tuple)]
         x1 = s1[0] if isinstance(s1, tuple) else s1
@@ -208,136 +317,117 @@ def rank_program(g, core, T, topo):
         s = scale[0] if isinstance(scale, tuple) else scale
         if acc is None: emit("S", lambda: g.scalar.activation(o[0], i[0], f, bias=b, scale=s), [o], [i] + ex)
         else: emit("S", lambda: g.scalar.activation(o[0], i[0], f, bias=b, scale=s, accum_out=acc[0]), [o, acc], [i] + ex)
-    def mm(o, l, r, start, stop): emit("P", lambda: g.tensor.matmul(o[0], l[0], r[0], start, stop), [o], [l, r])
+    def mm(o, l, r, start, stop): emit("P", lambda: g.tensor.matmul(o[0], l[0], r[0], start, stop), [o], [l, r], flags=(start, stop))
     def iota(o, pat, base=0, cm=0, small=True):
-        if small: emit("G", lambda: g.iota(o[0], pat, base, cm, allow_small_or_imprecise_dtypes=True), [o], [])
-        else: emit("G", lambda: g.iota(o[0], pat, base, cm), [o], [])
-    def keep(o, i, pat, op, base, cm, other=0.0): emit("G", lambda: g.affine_select(o[0], i[0], pat, op, other, base, cm), [o], [i])
-    def gcp(o, i, m): keep(o, i, [[0, m]], OP.is_ge, 0, 0)
+        if small: emit("G", lambda: g.iota(o[0], pat, base, cm, allow_small_or_imprecise_dtypes=True), [o], [], gp=130)
+        else: emit("G", lambda: g.iota(o[0], pat, base, cm), [o], [], gp=130)
+    def keep(o, i, pat, op, base, cm, other=0.0): emit("G", lambda: g.affine_select(o[0], i[0], pat, op, other, base, cm), [o], [i], gp=170)
+    def gcp(o, i): keep(o, i, [[0, o[3]]], OP.is_ge, 0, 0)
     def usl(name, r): return v(name, 15 - r, 143 - r)
     def sel(f, e, neg=""): return v("B%d%s" % (f, neg), 16 + 16 * (f - e), 144 + 16 * (f - e))
+
+    def add(q, o, i, c):
+        if q == "V": ts(o, i, c, OP.add)
+        else: act(o, i, bias=c)
 
     def table(q, out, win, lst, lo, hi):
         (cp if q == "V" else act)(v(out, lo, hi), ind(v(win, 0, 3072), v(lst, lo // 16, hi // 16)))
 
-    def diag(out, mat, src, m, last=True):
+    def diag(out, mat, src, start=True):
         for r in range(16):
-            mm(out, usl(mat, r), v(src, r, 16 * m, 16), r == 0, last and r == 15)
+            mm(out, usl(mat, r), v(src, r, 256, 16), start and r == 0, r == 15)
 
-    def unturn(bank, src, ks, ko, neg=None):
-        for f in range(2):
-            o = slice(f, 4, 2)
-            for e in range(2):
-                mm(n(bank, H4, o, ko), sel(f, e), n(src, A, A, e, ks), e == 0, e == 1 and neg is None)
-            if neg is not None:
-                for e in range(2):
-                    mm(n(bank, H4, o, neg[1]), sel(f, e, "N"), n(src, A, A, e, neg[0]), False, e == 1)
+    def unturn(bank, part, terms, stop=True):
+        each = [(f, e, x) for x in terms for f in range(2) for e in range(2)]
+        for k, (f, e, (neg, src, a, b, m)) in enumerate(each):
+            mm(n(bank, part, slice(f, 4, 2), slice(b, b + m)), sel(f, e, neg), n(src, A, A, e, slice(a, a + m)),
+               k == 0, stop and k == len(each) - 1)
 
     def to_list(nat, bank, o=0):
-        ts(v("NH", o, o + 192), v(nat), -OFF, OP.add)
-        turn(v("TN", o, o + 192), v("NH", o, o + 192))
-        for m in range(12):
+        if nat:
+            ts(v("NH", o, o + 192), v(nat), -OFF, OP.add)
+            turn(v("TN", o, o + 192), v("NH", o, o + 192))
+        for m in range(12 if bank else 0):
             for e in range(2):
                 b = o + 32 * (m // 2) + 16 * e
                 mm(v(bank, m, 192, 12), sel(m % 2, e), v("TN", b, b + 16), e == 0, e == 1)
 
-    def turn_places(t):
-        if t == 0 or not DS: ts(v("DI"), ind(v("ULI") if t == 0 else v("ULF", 0, 1536), v("VL%d" % t, 4, 20)), -OFF, OP.add)
-        turn(n("TD"), v("DI"))
-        unturn("P5", "TD", A, A)
-
-    def list_places():
-        for q in range(4):
-            ts(v("DL", 64 * q, 64 * q + 64), n("P5", H4, A, slice(4 * q, 4 * q + 4)), OFF, OP.add)
+    def repeat(classes, qs):
+        for h in range(4):
+            (gcp if qs[h] == "G" else act)(n("QC", A, h, key=(h, 64, 4)), classes[h])
+        for k in range(4):
+            gcp(n("QD", A, k, key=(k, 64, 4)), n("QC"))
 
     dma(v("NXN"), T.nx[:])
     dma(v("PVN"), T.pv[:], "act")
     dma(v("QM"), T.mv[:])
-    dma(v("X", 0, XA), T.xd[:, 0:XA])
-
-    fill(v("PW", 0, 512), 0)
-    fill(v("PW", 512, 1536), 0)
+    fill(v("PW", 0, 512), 1536)
+    iota(v("SHF"), [[32, 5], [1016, 2], [1, 16]], -16, -1)
+    ts(v("B1"), v("SHF"), 0.0, OP.is_equal)
+    ts(v("B0"), v("SHF"), 1000.0, OP.is_equal)
+    for k in (1, 2): fill(v("PW", 512 * k, 512 * k + 512), 1536)
+    iota(v("PW", 2560, 3072), [[0, 512]], 1536, 0, False)
     iota(v("IPI"), [[1, 1]], 0, 1, False)
     iota(v("IP"), [[1, 1]], 0, 1)
     iota(v("IN160"), [[1, 160]])
-    iota(v("PW", 2560, 3072), [[0, 512]], 0, 0, False)
-    iota(v("I64F"), [[1, 4], [64, 4], [0, 4]])
-    iota(v("IV"), [[6, 4], [384, 4]])
+    iota(v("IV"), [[384, 4], [6, 4]])
     iota(v("IG16"), [[16, 8], [0, 16]])
-    iota(v("I192"), [[1, 192]])
-    iota(v("K16"), [[0, 16], [1, 16]])
-    for k in range(3, 5):
-        act(v("PW", 512 * k, 512 * k + 512), v("PW", 0, 512))
-    dma(rows("PW", 4, 0, 3072), T.pv[:])
-    dma(v("X", XA, 3072), T.xd[:, XA:3072])
+    for k in (3, 4): act(v("PW", 512 * k, 512 * k + 512), v("PW", 0, 512))
+    dma(rows("PW", 4), T.pv[:])
+    dma(rows("PW", 11), T.rc[:], "act")
+    dma(v("X", 0, 3072), T.xd[:])
     dma(v("ULI"), T.ul[:])
-    ts(v("EI"), v("IPI"), 4, OP.arith_shift_right, 1, OP.bitwise_and)
-    ts(v("PI"), v("IPI"), 15, OP.bitwise_and)
-    ts(v("IP16"), v("IP"), 16.0, OP.add)
-    cp(v("M1"), v("EI"))
-    cp(v("P16"), v("PI"))
-    ts(v("M0"), v("M1"), -1.0, OP.mult, 1.0, OP.add)
-    ts(v("B1"), v("IN160"), v("IP16"), OP.is_equal, v("M1"), OP.mult)
-    ts(v("B0"), v("IN160"), v("IP16"), OP.is_equal, v("M0"), OP.mult)
-    ts(v("C4"), v("P16"), 4.0, OP.mult)
-    fill(v("ON"), 1.0)
-    tt(v("G16"), v("IP"), v("P16"), OP.subtract)
+
     to_list("PVN", "P4", 192)
     to_list("NXN", "P3")
-    act(v("Q4F"), v("I64F"), bias=v("C4"))
-    act(v("QA", 0, 512), ind(v("QM"), v("Q4F", 0, 32)))
+    ts(v("PI"), v("IPI"), 15, OP.bitwise_and)
+    cp(v("P16"), v("PI"))
+    fill(v("ON"), 1.0)
+    tt(v("G16"), v("IP"), v("P16"), OP.subtract)
+    repeat([v("QM", h, 256, 4) for h in range(4)], "GGGG")
     ts(v("G15"), v("G16"), 15.0, OP.add)
     ts(v("C24"), v("P16"), 24.0, OP.mult)
-    ts(v("C192"), v("P16"), 192.0, OP.mult)
     ts(v("U"), v("IN160", 0, 144), v("G15"), OP.is_equal)
-    ts(v("VL0", 4, 20), v("IV"), v("C24"), OP.add)
+    ts(v("VC", 0, 16), v("IV"), v("C24"), OP.add)
     fill(v("MON"), -1.0)
     ts(v("PVL"), v("P4", 0, 192), OFF, OP.add)
-    ts(v("IDN"), v("I192"), v("C192"), OP.add)
     for out, win, lst in (("W1", "PW", "PVL"), ("X1", "X", "NXL"), ("X2", "X1", "NXL")):
-        cut = {"W1": W1V, "X1": X1F, "X2": X2V}[out]
-        if cut: table("V", out, win, lst, 0, cut)
-        table("S", out, win, lst, cut, 3072)
+        table("V", out, win, lst, 0, SHARE[out])
+        table("S", out, win, lst, SHARE[out], 3072)
         if out == "W1":
             ts(v("NXL"), v("P3", 0, 192), OFF, OP.add)
-            act(v("QA", 512, 1024), ind(v("QM"), v("Q4F", 32, 64)))
-            ts(v("BB"), v("IG16"), v("G16"), OP.is_equal)
+            ts(v("BB4"), v("IG16"), v("G16"), OP.is_equal, 4096.0, OP.mult)
             fill(v("CB"), -61440.0)
-            fill(v("C15"), 15.0 / 128)
-            ts(v("U16"), v("U"), 16.0, OP.mult)
-            ts(v("U32"), v("U"), 32.0, OP.mult)
-            ts(v("UM"), v("U"), -16.0, OP.mult)
             ts(v("UC"), v("U"), 1048576.0, OP.mult)
-            ts(v("BB4"), v("BB"), 4096.0, OP.mult)
-    dma(v("P2N"), rows("W1", 4, 0, 3072))
-    dma(rows("PW", 3, 0, 3072), rows("W1", 4, 0, 3072))
-    dma(rows("PW", 5, 0, 3072), v("IDN"))
-    dma(rows("PW", 6, 0, 3072), T.rc[:])
+            fill(v("C15"), 15.0 / 16 / 128)
+            ts(v("UM"), v("U"), -1.0, OP.mult)
+            ts(v("B0N"), v("B0"), -1.0, OP.mult)
+            ts(v("B1N"), v("B1"), -1.0, OP.mult)
+    dma(v("P2N"), rows("W1", 4))
+    dma(rows("PW", 3), rows("W1", 4))
+    dma(rows("PW", 10), rows("W1", 11))
+    keep(v("IDM"), v("MON", 0, 128), [[-1, 128]], OP.is_equal, 0, 1)
     keep(v("IDP"), v("ON", 0, 128), [[-1, 128]], OP.is_equal, 0, 1)
     iota(v("I16"), [[16, 16]])
-    keep(v("IDM"), v("MON", 0, 128), [[-1, 128]], OP.is_equal, 0, 1)
+    iota(v("K16"), [[0, 16], [1, 16]])
     keep(v("TR"), v("BB4"), [[1, 128]], OP.is_gt, 0, -1)
     keep(v("TRE"), v("BB4"), [[1, 128]], OP.is_ge, 0, -1)
     keep(v("D0"), v("ON"), [[0, 16], [1, 16]], OP.is_gt, 0, 0)
     keep(v("DB"), v("MON"), [[0, 16], [1, 16]], OP.is_gt, 0, 0, 524288.0)
-    keep(v("KB"), v("ON"), [[0, 16], [1, 16]], OP.is_gt, 0, 0, -524288.0)
     iota(v("WI"), [[0, 16], [-16, 6]], 16)
     keep(v("WI"), v("WI"), [[0, 16], [-1, 6]], OP.is_ge, 0, 0)
-    iota(v("I64"), [[16, 16], [0, 4]])
+    gcp(v("IDH"), v("IDP"))
     for h in range(4):
-        gcp(v("QJ0", 64 * h, 64 * h + 64), v("QM", h, 256, 4), 64)
-    gcp(v("UH", 0, 144), v("U"), 144)
-    gcp(v("IDH"), v("IDP"), 128)
-    gcp(v("ULF", 0, 1536), v("ULI"), 1536)
-    iota(v("NXR", 0, 3072), [[0, 3072]])
-    turn_places(0)
-    ts(v("BHI"), v("NXN"), 6, OP.arith_shift_right)
-    ts(v("BLI"), v("NXN"), 63, OP.bitwise_and)
-    gcp(v("BHB"), v("BHI"), 192)
-    gcp(v("BLB"), v("BLI"), 192)
-    dma(rows("NXR", 7, 0, 3072), v("BHB"))
-    dma(rows("NXR", 6, 0, 3072), v("BLB"))
-    list_places()
+        gcp(v("QJ0", 64 * h, 64 * h + 64), v("QM", h, 256, 4))
+    ts(v("DI"), ind(v("ULI"), v("VC", 0, 16)), -OFF, OP.add)
+    cp(v("QA"), n("QD"))
+    turn(n("TD"), v("DI"))
+    unturn("P5", H4, [("", "TD", 0, 0, 16)])
+    for k in range(3):
+        iota(v("IDW", 1024 * k, 1024 * k + 1024), [[1, 1024]], 1024 * k, 0, False)
+    dma(rows("PW", 5), rows("IDW", 5))
+    dma(v("NXR", 0, 3072), v("X", 0, 3072))
+    gcp(v("ULF", 0, 1536), v("ULI"))
 
     def late_consts(part):
         if part == 0:
@@ -345,267 +435,258 @@ def rank_program(g, core, T, topo):
             fill(v("ONE"), 1.0)
             ts(v("T1"), v("P16"), 7.0, OP.is_equal, 64.0, OP.mult)
             ts(v("T2"), v("P16"), 6.0, OP.is_equal)
-            ts(v("W5"), v("P16"), 5.0, OP.is_equal)
-            act(v("B0N"), v("B0"), scale=-1.0)
-            act(v("B1N"), v("B1"), scale=-1.0)
-            act(v("P2L"), v("P7", 0, 192), bias=OFF)
-        if part == 1:
+            ts(v("W11"), v("P16"), 11.0, OP.is_equal)
             ts(v("MK"), v("K16"), v("P16"), OP.not_equal)
             ts(v("PO"), v("MK"), -4194304.0, OP.mult, OFF, OP.add)
-        if part == 3:
+        if part == 1:
+            ts(v("BHI"), v("NXN"), 6, OP.arith_shift_right)
+            ts(v("BLI"), v("NXN"), 63, OP.bitwise_and)
+            gcp(v("BHB"), v("BHI"))
+            gcp(v("BLB"), v("BLI"))
+            dma(rows("NXR", 7), v("BHB"))
+            dma(rows("NXR", 6), v("BLB"))
+        if part == 2:
             ts(v("IDM4"), v("IDP"), -4096.0, OP.mult)
             ts(v("ID4"), v("IDP"), 4096.0, OP.mult)
             tt(v("WA"), v("T1"), v("T2"), OP.add)
-        if part == 4:
-            ts(v("RA"), v("BB"), v("W5"), OP.mult)
+            ts(v("UR", 0, 144), v("U"), v("W11"), OP.mult)
+        if part == 3:
             ts(v("UA"), v("U"), v("WA"), OP.mult)
-            ts(v("Q4L"), v("I64"), v("P16"), OP.add)
             ts(v("DUV"), v("I16"), v("P16"), OP.add, 1536.0, OP.add)
             ts(v("DUA"), v("I16"), v("P16"), OP.add, 3072.0, OP.add)
 
-    def steps(lo, hi):
-        for k in range(lo, hi):
-            table("S", "W1", "PW", "P2L", 512 * k, 512 * k + 512)
-        if hi == 6:
-            dma(rows("PW", 2, 0, 3072), rows("W1", 4, 0, 3072))
-            dma(rows("PW", 1, 0, 3072), rows("W1", 3, 0, 3072))
+    def steps(*ks):
+        for k in ks:
+            table("S", "W1", "PW", "P2L", sum(STEPS[:k]), sum(STEPS[:k + 1]))
 
-    def sums(bank, mat, src, q, last, h0=0, h1=4):
+    def sums(bank, mat, src, q, last):
         for r in range(16):
-            mm(n(bank, slice(h0, h1), A, slice(4 * q, 4 * q + 4)), usl(mat, r),
-               v(src, 1024 * q + 256 * h0 + r, 1024 * q + 256 * h1, 16), False, last and r == 15)
+            mm(n(bank, H4, A, slice(4 * q, 4 * q + 4)), usl(mat, r), v(src, 1024 * q + r, 1024 * q + 1024, 16), False, last and r == 15)
 
-    HC = [(h, c) for c in range(4) for h in range(4)]
+    EIGHTH = ("P3", "P4", "P7", "P5", "P6")
+    HALVES = ((0, 128, "P3"), (128, 256, "P4"))
 
     for t in range(NR):
-        Q, Qn, VL, Vn = "QJ%d" % t, "QJ%d" % (t + 1), v("VL%d" % t, 4, 20), "VL%d" % (t + 1)
-        Q4, Q4n = ("QA", "QB") if t % 2 == 0 else ("QB", "QA")
+        Q, Qn, VL, Vn = "QJ%d" % t, "QJ%d" % (t + 1), v("VC", 16 * t, 16 * t + 16), "VL%d" % (t + 1)
+        Q4, ZB, MW = ("QA", "QB")[t % 2], "ZB%d" % t, "MW%d" % t
         first, lastr = t == 0, t == NR - 1
         lists = FIRST if first else TESTS
         tens = lists["P"].split()
-
-        scal = lists["S"].split()
-        nv = min(int(y[1]) for y in scal if y[0] == "g")
+        m0 = 512 * min(int(y[1]) for y in lists["S"].split() if y[0] == "g")
 
         def test(x, out, q, op, m=1024):
             tt(v(out, 1024 * q, 1024 * q + m), ind(v(x, 0, 3072), v("DL", 64 * q, 64 * q + m // 16)), v(Q4, 0, m), op)
 
-        def needs(x):
-            k, j = x[0], x[1]
-            return {"t": ["d" + j], "s": ["h" + j], "A": ["a" + j], "B": ["b" + j], "R": ["v1"] + ["s3"] * (nv < 4), "u": ["R1"],
-                    "q": [y for y in scal if k == "q" and y == "s%d" % (int(j) - 5)],
-                    "h": ["g" + j, "q" + j], "b": [] if first else ["x2"],
-                    "r": ["d" + j], "m": ["d" + j],
-                    "Z": [y for y in scal + lists["V"].split() + tens if k == "Z" and y in ("t" + j, "r" + j, "m" + j, "s%d" % (2 * int(j)), "s%d" % (2 * int(j) + 1))],
-                    "c": ["A0", "A1", "A2", "A3"], "C": ["c1"], "k": ["Z0", "Z1", "Z2", "Z3"]}.get(k, [])
+        def needs(x, y):
+            k, j = x[0], int(x[1]) if x[1:2].isdigit() else 0
+            if k in "xy":
+                lo, hi = [int(u) for u in x[1:].split("-")]
+                return y[0] == "y" if k == "x" else y == "X" or y in ["n%d" % u for u in range(lo // 8, (hi + 7) // 8)]
+            if y[0] in {"a": "yQ", "b": "xQ", "d": "XQ", "g": "X", "q": "Q", "c": "A", "k": "Z", "m": "o", "Z": "o", "A": "o", "B": "p",
+                        "C": "pc", "i": "W", "v": "W", "j": "i", "J": "j", "l": "J", "T": "N", "w": "v", "D": "j", "p": "D", "K": "L",
+                        "M": "K"}.get(k, ""): return True
+            if k == "h" and y[0] == "g": return x[1] in y
+            return y in {"n": ["T%d" % j], "d": ["l0"], "g": ["l%d" % (j // 2)], "a": ["l%d" % j], "b": ["l%d" % j],
+                         "t": ["d0"], "r": ["d0"], "m": ["d0"], "s": ["h%d" % j], "A": ["a%d" % j], "B": ["b%d" % j],
+                         "q": ["s%d" % (j - 5)] + (["l0", "l1", "l2", "l3"] if j == 4 else ["n%d" % (7 - j)] + ["M"] * (j == 5)),
+                         "h": ["q%d" % j], "Z": ["t%d" % j, "r%d" % j, "m%d" % j, "s%d" % (2 * j), "s%d" % (2 * j + 1)]}.get(k, [])
 
-        def run(x):
-            k, j = x[0], int(x[1]) if x[1].isdigit() else 0
+        def run(x, q):
+            k, j = x[0], int(x[1]) if x[1:2].isdigit() else 0
             last = lambda kinds: x == [y for y in tens if y[0] in kinds][-1]
-            bank = n(("P3", "P4", "P7", "P5", "P6")[(7 - j) % 5])
-            m = min(1024, 512 * nv - 1024 * j)
-            if k == "d": test("X", "DF", j, OP.subtract, m)
-            if k == "t": act(v("AB", 1024 * j, 1024 * j + m), v("DF", 1024 * j, 1024 * j + m), AF.Abs)
+            bank = EIGHTH[(7 - j) % 5]
+            if k == "X": cp(ind(v("X"), v("OFA")), v("XS"))
+            if k == "N": cp(ind(v("NXR"), v("OFA")), v("NNB"))
+            if k == "W":
+                for h in range(1, 4): add(q, v("VC", 16 * t + h, 16 * t + 16, 4), v("VL%d" % t, 4 + 4 * h, 8 + 4 * h), 0.0)
+            if k == "Q": dma(v(Q4), n("QD"))
+            if k == "i": add(q, v("DI"), ind(v("ULF", 0, 1536), VL), -OFF)
+            if k == "L": to_list("P2N", None)
+            if k == "K": to_list(None, "P7")
+            if k == "M": add(q, v("P2L"), v("P7", 0, 192), OFF)
+            if k == "j": turn(n("TD"), v("DI"))
+            if k == "J": unturn("P5", H4, [("", "TD", 0, 0, 16)])
+            if k == "l": add(q, v("DL", 64 * j, 64 * j + 64), n("P5", H4, A, slice(4 * j, 4 * j + 4)), OFF)
+            if k == "T":
+                for r in range(16):
+                    mm(v(EIGHTH[j], 0, 64), usl("UA", r), v("NXR", 1024 * j + r, 1024 * j + 1024, 16), r == 0, r == 15)
+            if k == "n": add(q, v("NXL", 64 * j, 64 * j + 64), v(EIGHTH[j], 0, 64), 0.0)
+            if k in "xy":
+                lo, hi = [128 * int(u) for u in x[1:].split("-")]
+                table(q, *(("X2", "X1") if k == "x" else ("X1", "X")), "NXL", lo, hi)
             if k == "v":
-                act(v("VG"), ind(v("PW"), VL))
+                act(v("VR"), ind(v("IDW"), VL))
                 act(v("VF"), VL)
-            if k == "R": mm(n("P6", H4), v("RA"), v("VG"), True, True)
-            if k == "u": act(n("VR"), n("P6", H4))
+            if k == "d": test("X", "DF", 0, OP.subtract, m0)
+            if k == "t": act(v("AB", 0, m0), v("DF", 0, m0), AF.Abs)
+            if k == "r": ts(v("AB", 0, m0), v("DF", 0, m0), 0.0, OP.max, 2.0, OP.mult)
             if k == "a": test("X1", "L1", j, OP.is_lt)
             if k == "b": test("X2", "L2", j, OP.is_lt)
-            if k == "g": act(v("XG", 512 * j, 512 * j + 512), ind(v("X", 0, 3072), v("DL", 32 * j, 32 * j + 32)))
-            if k == "s": act(v("AB", 512 * j, 512 * j + 512), bank, AF.Abs)
-            if k == "x": table("S", "X2", "X1", "NXL", 0, 3072)
+            if k == "g":
+                u = j + len(x) - 1
+                act(v("XG", 512 * j, 512 * u), ind(v("X", 0, 3072), v("DL", 32 * j, 32 * u)))
+            if k == "s": act(v("AB", 512 * j, 512 * j + 512), n(bank), AF.Abs)
             if k == "c": act(v("C1"), n("P1", H4), AF.Relu, scale=32.0)
-            if k == "k": act(v("K0"), n("P0", H4))
-            if k == "q": mm(bank, v("IDM"), v(Q4, 512 * (j % 2), 512 * (j % 2) + 512), True, False)
-            if k == "h": mm(bank, v("IDP"), v("XG", 512 * j, 512 * j + 512), False, True)
-            if k == "r": ts(v("AB", 1024 * j, 1024 * j + 1024), v("DF", 1024 * j, 1024 * j + 1024), 0.0, OP.max)
-            if k == "m": sums("P0", "UM", "DF", j, False)
-            if k == "Z": sums("P0", "U32" if "m%d" % j in tens else "U16", "AB", j, last("Z"))
+            if k == "k":
+                act(v("K0"), n("P0", H4), scale=16.0)
+                act(v("K1"), n("P0", H4), scale=-16.0, bias=BIG)
+            if k == "o": mm(n("P0", H4), v("C15"), v("ON"), True, False)
+            if k in "op": mm(n("P1" if k == "o" else "P2", H4), v("CB"), v("ON"), True, False)
+            if k == "D": unturn("P2", slice(4, 8), [("N", "TD", 0, 0, 16), ("", "TD", 0, 1, 15)])
+            if k == "w": equal(j)
+            if k == "q": mm(n(bank), v("IDM"), v(Q4, 512 * (j % 2), 512 * (j % 2) + 512), True, False)
+            if k == "h": mm(n(bank), v("IDP"), v("XG", 512 * j, 512 * j + 512), False, True)
+            if k == "m": sums("P0", "UM", "DF", 0, False)
+            if k == "Z": sums("P0", "U", "AB", j, last("Z"))
             if k == "A": sums("P1", "UC", "L1", j, last("A"))
-            if k == "B": sums("P2", "UC", "L2", j, last("B"))
-            if k == "C": mm(n("P2", H4), v("IDP"), v("C1"), False, False)
+            if k == "B": sums("P2", "UC", "L2", j, last("BC"))
+            if k == "C": mm(n("P2", H4), v("IDP"), v("C1"), False, last("BC"))
 
-        def equal(c, hs=range(4)):
-            if first: return
+        pairs = [] if first else [(h, c) for h in range(4) for c in range(4)]
+
+        def equal(m):
+            for h, c in pairs[:m]:
+                ts(ew(h, c, slice(0, 4 - c)), v("VR", 64 * c, 256), v("VF", 4 * c + h, 4 * c + h + 1), OP.is_equal)
+            del pairs[:m]
+
+        def count(*hs):
             for h in hs:
-                ts(n("EW%d" % c, h), n("VR", A, slice(c, 4)), v("VF", 4 * h + c, 4 * h + c + 1), OP.is_equal)
+                if h == 0: mm(n("P1", H4), v("IDP"), v("PO"), True, False)
+                for c in range(3):
+                    mm(n("P1", slice(c + 1, 4)), v("BB4"), ew(h, c, slice(1, 4 - c)), False, False)
+                mm(n("P1", H4, slice(0, h + 1)), v("TR"), ew(h, A, 0, slice(0, h + 1)), False, False)
+                if h < 3: mm(n("P1", H4, slice(h + 1, 4)), v("TRE"), ew(h, A, 0, slice(h + 1, 4)), False, False)
 
-        def count(c, start=False, stop=False, hs=range(4)):
-            if first: return
-            if start: mm(n("P1", H4), v("IDP"), v("PO"), True, False)
-            src = "EW%d" % c
-            for h in hs:
-                if c < 3: mm(n("P1", H4, slice(c + 1, 4)), v("BB4"), n(src, h, A, slice(1, 4 - c)), False, False)
-                mm(n("P1", slice(0, h + 1), c), v("TR"), n(src, h, slice(0, h + 1), 0), False, stop and h == 3)
-                if h < 3: mm(n("P1", slice(h + 1, 4), c), v("TRE"), n(src, h, slice(h + 1, 4), 0), False, False)
-
-        mm(n("P0", H4), v("C15"), v("ON"), True, False)
-        mm(n("P1", H4), v("CB"), v("ON"), True, False)
-        mm(n("P2", H4), v("CB"), v("ON"), True, False)
         weave(lists, needs, run)
         if first:
-            to_list("P2N", "P7")
             late_consts(0)
-        else: equal(0, range(3))
-        scan(v("W2"), v("KB"), v("K0"), 0.0, OP.add, OP.max)
-        tt(v("KEY"), n("P2", H4), v("K0"), OP.max)
-        ts(v("RC"), v("W2", 15, 256, 16), -1.0, OP.mult, BIG, OP.add)
-        scan(v("RI"), v("DB"), v("KEY"), 1000000.0, OP.add, OP.min)
-        equal(3, (0,))
-        count(0, True, False, range(3))
-        mm(n("P2", H4, A, slice(0, 6)), v("IDP"), v("WI"), True, False)
-        tt(v("RM"), v("RI", 15, 256, 16), v("RC"), OP.min)
-        equal(3, (1,))
-        ts(v("KI"), v("RM"), 15, OP.bitwise_and)
-        equal(3, (2,))
-        act(v("SG"), v("RM"), AF.Sign, bias=-65535.5)
-        cp(v("KU"), v("KI"))
-        equal(3, (3,))
-        mm(v("P4", 0, 16), v("ONE"), v("SG"), True, True)
-        count(3)
-        tt(v("OHD"), ind(v("E16"), v("KU")), v("DI"), OP.mult)
-        diag(v("P3", 0, 16), "UH", "OHD", 16)
-        equal(0, (3,))
-        equal(1)
+            steps(0)
+        cp(v("D15"), v("DL", 195, 256, 4))
+        for a, b, key in HALVES: tt(v(key, 0, 128), n("P2", slice(a // 64, b // 64)), v("K0", a, b), OP.max)
+        act(v("DD"), n("P2", slice(4, 8)))
+        for a, b, key in HALVES: tt(v(key, 0, 128), v(key, 0, 128), v("K1", a, b), OP.min)
+        for a, b, key in HALVES: scan(v("RI", a, b), v("DB", a, b), v(key, 0, 128), 1000000.0, OP.add, OP.min)
+        if not first:
+            count(0, 1)
+            mm(v("P7", 0, 256), v("IDP"), v("PO"), True, False)
+        for a, b, key in HALVES: tt(v("NF", a, b), v(key, 0, 128), v("RI", a, b), OP.not_equal)
+        for a, b, key in HALVES: scan(v("SL", a, b), v("DD", a, b), v("NF", a, b), 0.0, OP.add, OP.mult)
+        for a, b, key in HALVES: tt(v("AU", a // 16, b // 16), v("SL", a + 15, b, 16), v("D15", a // 16, b // 16), OP.add)
+        equal(2)
         if first: late_consts(1)
+        cp(v("RM"), v("RI", 15, 256, 16))
+        ts(v("KI"), v("RM"), 15, OP.bitwise_and)
+        cp(v("KU"), v("KI"))
+        act(v("SG"), v("RI", 15, 256, 16), AF.Sign, bias=-65535.5)
+        mm(v("P4", 0, 16), v("ONE"), v("SG"), True, True)
+        mm(n("P2", H4, A, slice(0, 6)), v("IDP"), v("WI"), True, False)
+        mm(v("P3", 0, 256), v("IDH"), v("DI"), True, False)
         act(v("JK"), v("P4", 0, 16), scale=0.25, bias=198655.75 / 16, acc=v("BC"))
         act(v("NI", 0, 1), v("BC"), scale=1.0 / 128, bias=-12.49609375)
         act(v("ZC"), v("NI", 0, 1), scale=-128.0, bias=v("BC"))
+        for q, (a, b, key) in zip("SV", HALVES): add(q, v("FB", a, b), ind(v("PW"), v("AU", a // 16, b // 16)), -OFF)
         act(v("ZH"), v(Q), scale=0.5, bias=v("ZC"))
-        act(v("ZB%d" % t), v("ZH"), bias=-OFF)
-        remote("z", t, lambda h: v(Qn, 64 * h, 64 * h + 64), lambda h: v("ZB%d" % t, 64 * h, 64 * h + 64))
-        act(v("OH"), ind(v("E16"), v("KU")))
-        if first: steps(0, GS[0])
-        count(0, False, False, (3,))
-        count(1)
-        ts(v("AU"), v("P3", 0, 16), OFF, OP.add)
-        ts(v("FB"), ind(v("PW"), v("AU")), -OFF, OP.add)
+        act(v(ZB), v("ZH"), bias=-OFF)
+        remote("z", t, lambda h: v(Qn, 64 * h, 64 * h + 64), lambda h: v(ZB, 64 * h, 64 * h + 64))
+        if first: steps(1, 2)
+        equal(2)
         turn(n("TF"), v("FB"))
+        dons, recs = [("", "TF", 0, 0, 6), ("N", "TF", 1, 0, 5)], [("", "TF", 6, 0, 6), ("N", "TF", 7, 0, 5)]
         if first:
-            unturn("P5", "TF", 3, 0)
-            unturn("P6", "TF", slice(3, 5), slice(2, 4))
+            unturn("P5", H4, [("", "TF", 3, 0, 1)])
+            late_consts(2)
             ts(v("AU"), n("P5", H4, A, 0), OFF, OP.add)
             ts(v("FB"), ind(v("PW"), v("AU")), -OFF, OP.add)
             turn(n("TG"), v("FB"))
-            unturn("P6", "TG", slice(3, 5), slice(0, 2))
-            terms = [("", "TF", 0, 0, 6), ("N", "TF", 1, 0, 5), ("", "TG", 3, 1, 2), ("N", "TG", 4, 1, 1), ("N", "TG", 2, 2, 1)]
-            for f in range(2):
-                for k, (neg, src, a, b, m) in enumerate(terms):
-                    for e in range(2):
-                        mm(n("P0", H4, slice(f, 4, 2), slice(b, b + m)), sel(f, e, neg), n(src, A, A, e, slice(a, a + m)), k + e == 0, k + e == 5)
+            unturn("P6", H4, [("", "TF", 3, 2, 2), ("", "TG", 3, 0, 2)])
+            dons += [("", "TG", 3, 1, 2), ("N", "TG", 4, 1, 1)]
+            recs += [("", "TG", 10, 2, 2), ("N", "TG", 10, 1, 2)]
             late_consts(3)
-        else:
-            unturn("P5", "TF", slice(1, 5), H4)
-            unturn("P0", "TF", slice(0, 6), slice(0, 6), (slice(1, 6), slice(0, 5)))
-        equal(2)
-        act(v("DE"), n("P0", H4, A, slice(0, 6)))
-        if first: steps(GS[0], GS[1])
-        else:
-            count(2)
-            mm(n("P1", H4), v("IDH"), n("VR"), False, True)
-            act(v("CV"), n("P1", H4), bias=-OFF)
-        ts(v("BLU"), n("P6" if first else "P5", H4, A, H4), OFF, OP.add)
+        else: unturn("P6", H4, [("", "TF", 1, 0, 4)])
+        unturn("P0", H4, dons)
+        unturn("P5", H4, recs, False)
+        equal(3)
+        ts(v("BLU"), n("P6", H4, A, H4), OFF, OP.add)
+        equal(16)
+        act(v("AU4"), n("P6", H4, A, 0), bias=OFF)
+        act(v("R4"), ind(v("PW"), v("AU4")), bias=-OFF)
         tt(v("LW"), ind(v("X", 0, 3072), v("BLU")), v(Q4), OP.is_lt)
+        if first:
+            for k in (2816, 2560): table("V", "W1", "PW", "P2L", k, k + 256)
+        else:
+            count(2, 3)
+            mm(n("P1", H4), v("IDH"), v("VR"), False, True)
+            act(v("CV"), n("P1", H4), bias=-OFF)
+        diag(n("P5", H4, A, 1), "UR", "R4", False)
+        act(v("DE"), n("P0", H4, A, slice(0, 6)))
+        act(v("DR"), n("P5", H4, A, slice(0, 6)))
+        act(v("OH"), ind(v("E16"), v("KU")))
+        if first: steps(3)
         for r in range(16):
             mm(n("P2", H4, A, slice(1, 5)), usl("U", r), v("LW", r, 1024, 16), False, r == 15)
-        mm(v("P3", 0, 256), v("IDH"), v("DI"), True, False)
+        act(v(Qn, 0, 64), v(ZB, 0, 64))
         mm(v("P3", 0, 256), v("IDM4"), v("OH"), False, True)
-        mm(v("P7", 0, 256), v("IDP"), v("PO"), True, False)
+        if first: mm(v("P7", 0, 256), v("IDP"), v("PO"), True, False)
         act(v("DM"), v("P3", 0, 256), bias=OFF)
-        act(v(Qn, 0, 64), v("ZB%d" % t, 0, 64))
-        mm(n("P0", H4), v("ID4"), v("OH"), True, False)
-        if first: late_consts(4)
+        if first: steps(4)
         else:
-            scan(v("CS"), v("D0"), v("CV"), 0.0, OP.mult, OP.max)
-            tt(v("OFV"), v("CS", 15, 256, 16), v("DUV"), OP.min)
+            scan(v("CW"), v("D0"), v("CV"), 0.0, OP.mult, OP.max)
+            tt(v("OFV"), v("CW", 15, 256, 16), v("DUV"), OP.min)
         ts(v("G6"), n("P2", H4, A, slice(0, 6)), 7.5, OP.is_lt)
-        scan(v("SH"), v("DE"), v("G6"), 0.0, OP.add, OP.mult)
-        ts(v("AU2"), v("SH", 5, 96, 6), OFF, OP.add)
-        ts(v("GC", 0, 256), ind(v("PW"), v("AU2")), -OFF, OP.add)
-        if not lastr: act(v("N1B"), ind(v("NXR", 0, 3072), v("AU2")))
-        act(v("XA"), ind(v("X", 0, 3072), v("AU2")))
+        mm(n("P0", H4), v("ID4"), v("OH"), True, False)
         for h in range(4):
-            mm(n("P6", H4, h), v("RA"), v("GC", 64 * h, 64 * h + 64), True, True)
-        turn(n("TF"), v("GC", 0, 256))
-        unturn("P5", "TF", 6, 0)
-        mm(n("P0", H4), v("RA"), v("GC", 0, 256), False, True)
-        cp(v("AR"), n("P6", H4))
-        act(v("MW%d" % t), n("P5", H4, A, 0), bias=OFF)
-        remote("w", t, lambda h: v(Vn, 4 + 4 * h, 8 + 4 * h), lambda h: v("MW%d" % t, 4 * h, 4 * h + 4))
-        if lastr: act(v("OHA"), n("P0", H4), bias=OFF - 4096.0)
-        if t >= ES:
-            for h in range(4):
-                act(v("EV", 64 * h, 64 * h + 64), v("AR", 192, 256), AF.Square, scale=-1.0, bias=v("SH", 24 * h + 23, 24 * h + 24))
-            act(v("EA", 2304, 2560), v("EV"), AF.Relu, scale=-1.0, bias=1.0)
-        if not lastr: act(v("OHA"), n("P0", H4), bias=OFF - 4096.0)
-        act(v(Vn, 4, 8), v("MW%d" % t, 0, 4))
-
-        def followers():
-            diag(n("P1", 0, 0), "UA", "N1B", 16)
-            for h in range(4):
-                act(v("N1U", h, 16, 4), n("P1", 0, 0, slice(4 * h, 4 * h + 4)))
-            act(v("NNB"), ind(v("NXR", 0, 3072), v("N1U")))
-            if t >= QL: act(v(Q4n), ind(v(Qn), v("Q4L")))
-
-        def places():
-            tt(ind(v("ULF"), VL if first else v("OFV")), v("DM"), v("OHA"), OP.max)
-            if lastr: dma(T.yu[:], v("ULF", 0, 1536))
-        for k in range(4):
-            mm(n("P2", H4, k), v("IDP"), v("XA", 64 * k, 64 * k + 64), True, False)
-            mm(n("P2", H4, k), v("IDP"), v(Q, 64 * k, 64 * k + 64), False, True)
-        act(v("XH"), n("P2", H4), scale=0.5, bias=1024.25)
-        act(v("XS"), v("XH"), bias=-1024.0)
+            mm(n("P2", H4, h), v("IDP"), v(Q, 64 * h, 64 * h + 64), h == 0, False)
+        scan(v("SH"), v("DE"), v("G6"), 0.0, OP.add, OP.mult)
+        scan(v("SR"), v("DR"), v("G6"), 0.0, OP.add, OP.mult)
+        ts(v("AU2"), v("SH", 5, 96, 6), OFF, OP.add)
+        for q, h in (("V", 2), ("S", 1), ("S", 3)): add(q, v(MW, 4 * h, 4 * h + 4), v("SR", 6 * h + 5, 96, 24), OFF)
+        ts(v("AR"), ind(v("IDW"), v("AU2")), -OFF, OP.add)
+        remote("w", t, lambda h: v(Vn, 4 + 4 * h, 8 + 4 * h), lambda h: v(MW, 4 * h, 4 * h + 4))
+        if not lastr: repeat([v(ZB, 0, 64)] + [v(Qn, 64 * h, 64 * h + 64) for h in range(1, 4)], "GGSS")
+        act(v("XA"), ind(v("X", 0, 3072), v("AU2")))
+        if not lastr: act(v("N1B"), ind(v("NXR", 0, 3072), v("AU2")))
+        ts(v(Vn, 4, 8) if lastr else v("VC", 16 * t + 16, 16 * t + 32, 4), v("SR", 5, 96, 24), OFF, OP.add)
         mm(v("P7", 0, 256), v("IDH"), v("AR"), False, False)
+        mm(n("P0", H4), v("IDH"), v("AR"), False, True)
+        act(v("OHA"), n("P0", H4), bias=OFF - 4096.0)
+        if lastr:
+            for h in range(4):
+                act(v("YQ", h, 256, 4), v(Qn, 64 * h, 64 * h + 64))
+            dma(T.yq[:], v("YQ"), "act")
         e = 0
-        for h, c in HC:
-            p, o, w = 4 * h + c, 64 * c, 16 * h + 16
-            if c < 3 or t < ES: ts(v("EA", e, e + 256 - o), v("AR", o, 256), v("SH", 6 * p + 5, 6 * p + 6), OP.is_equal)
+        for p in range(16):
+            c, h = p // 4, p % 4
+            o, w = 64 * c, 16 * h + 16
+            ts(v("EA", e, e + 256 - o), v("AR", o, 256), v("SH", 6 * p + 5, 6 * p + 6), OP.is_equal)
             if c < 3: mm(v("P7", o + 64, 256), v("BB4"), v("EA", e + 64, e + 256 - o), False, False)
             mm(v("P7", o, o + w), v("TR"), v("EA", e, e + w), False, p == 15)
             if h < 3: mm(v("P7", o + w, o + 64), v("TRE"), v("EA", e + w, e + 64), False, False)
             e += 256 - o
-            if lastr and (h, c) == (2, 0): places()
-            if not lastr and (h, c) == NAT: followers()
-            if first and (h, c) == NAT:
-                steps(GS[1], 6)
-                act(v(Q4n), ind(v(Qn), v("Q4L")))
-        if not lastr and UE: places()
+            if p == 1:
+                mm(n("P2", H4), v("IDP"), v("XA"), False, True)
+                act(v("XH"), n("P2", H4), scale=0.5, bias=1024.25)
+                act(v("XS"), v("XH"), bias=-1024.0)
+                if first:
+                    steps(5)
+                    for a in (3, 4, 10, 11): dma(rows("PW", a - 2), rows("W1", a))
+                if not lastr:
+                    diag(n("P1", 0, 0), "UA", "N1B")
+                    act(v("N1U"), n("P1", 0, 0))
+                    act(v("NNB"), ind(v("NXR", 0, 3072), v("N1U")))
+            if p == (4 if lastr else 15):
+                tt(ind(v("ULF"), VL if first else v("OFV")), v("DM"), v("OHA"), OP.max)
+                if lastr: dma(T.yu[:], v("ULF", 0, 1536))
         scan(v("CS"), v("D0"), v("P7", 0, 256), 0.0, OP.mult, OP.max)
         tt(v("OFA"), v("CS", 15, 256, 16), v("DUA"), OP.min)
-        if not lastr:
-            cp(ind(v("NXR"), v("OFA")), v("NNB"))
-            def third(k):
-                for r in range(16):
-                    mm(v(("P3", "P4", "P7" if X1V else "P4")[k], 64 * k, 64 * k + 64), usl("UA", r), v("NXR", 1024 * k + r, 1024 * k + 1024, 16), r == 0, r == 15)
-            third(0)
-            third(1)
-            if DS: act(v("DI"), ind(v("ULF", 0, 1536), v(Vn, 4, 20)), bias=-OFF)
-            act(v("NXL", 0, 64), v("P3", 0, 64))
-            cp(ind(v("X"), v("OFA")), v("XS"))
-            table("S", "X1", "X", "NXL", 0, 1024)
-            turn_places(t + 1)
-            third(2)
-            if X1V:
-                cp(v("NXL", 64, 128), v("P4", 64, 128))
-                table("V", "X1", "X", "NXL", 1024, 1024 + X1V)
-                act(v("NXL", 128, 192), v("P7", 128, 192))
-            else: act(v("NXL", 64, 192), v("P4", 64, 192))
-            table("S", "X1", "X", "NXL", 1024 + X1V, 3072)
-            list_places()
-        else:
-            cp(ind(v("X"), v("OFA")), v("XS"))
-            dma(T.yx[:], v("X", 0, 3072))
-    VE, QE = "VL%d" % NR, "QJ%d" % NR
-    for h in range(4):
-        act(v("YQ", h, 256, 4), v(QE, 64 * h, 64 * h + 64))
-    dma(T.yq[:], v("YQ"), "act")
-    act(v("YG"), ind(v("PW"), v(VE, 4, 20)))
+    run("X", "V")
+    dma(T.yx[:], v("X", 0, 3072))
+    act(v("YG"), ind(v("IDW"), v("VL%d" % NR, 4, 20)))
     for h in range(4):
         act(v("YR", h, 256, 4), v("YG", 64 * h, 64 * h + 64))
-    b = _PACK["YR"][1]
-    dma(T.yv[:], (T.ff[5:128:16, b:b + 256], v("YR")[1], []), "act")
+    dma(T.yv[:], rows("YR", 5, 0, 256), "act")
+    if not PLAN: PLAN.extend(arrange(calls))
+    for k in PLAN:
+        if calls[k][6]: calls[k][6]()
     for q in ("V", "S", "P", "G"):
         g.wait_ge(T.sem["q" + q], cnt[q])
     for nm in sorted(total):

@@ -8,18 +8,34 @@ OFF = 1536.0
 A = slice(None)
 H4 = slice(0, 4)
 
-TESTS = {"V": "N X n1 y8-16 y16-17 j l0 l1 l2 l3 d0 r0 a0 a1 a2 a3 b0 b1 b2 b3 w8",
-         "S": "W i n0 y0-8 n2 y17-24 v g23 x0-24 s2 s3 g45 s4 s5 g67 s6 s7 c k",
-         "P": "T0 T1 T2 J q2 q3 o D q4 q5 q6 m0 h2 Z0 h3 A0 p q7 A1 A2 h4 Z1 A3 h5 B0 h6 B1 Z2 h7 B2 Z3 C B3",
-         "Y": "Q"}
+START = {"V": "PW B1 B0 PI PW P16 G16 G15 U E16 NH TN NH TN PVL W1 NXL X1 DI TD X2",
+         "S": "PW*3 B0N B1N C24 VC UC UM WA PO W1 X1 X2", "P": "P4<TN P3<TN",
+         "G": "SHF IPI IP IN160 PW IV QD*6 IDM IDP PO*4 DB BB4*3 IDH WI*2 QJ*4 IDW*3 BHB BLB TR TRE D0 IDM4 ID4 I16 J16"}
+QUICK = ()
+DEEP = True
+_V = "%sP3 P4 RI RI NF NF SL SL AU AU FB TF %sBLU LW LW G6 TH SH AU2 AR G6 EA SH EA AU2 SR EA*2 MW EA*4 CS %s"
+_S = "C1 C1 DD SG JK NI FB ZC ZH ZB %sAU4 R4 DE OH DM %s"
+_P = "%sP1<LW P3<OH P0<OH P2<LW P5<TH P4<AR P4<EA*8 P7<AR %sP7<EA*8"
+_2 = ("AU FB TG ", "FB CV ") if not DEEP else ("", "CV ")
+_W = ("TE EA*4 OFA EA*4 X CS NXR OFA", "N1B XA DR AR N1B XA XS N1U NNB XS OHA*2", "P6<TE*2 ")
+CHAIN = [{"V": _V % ("W1 ", "AU FB TG ", _W[0]), "S": _S % ("FB ", _W[1]), "P": _P % ("", _W[2])},
+         {"V": _V % ("EW*16 ", _2[0], _W[0]), "S": _S % (_2[1], _W[1]), "P": _P % ("P6<CV ", _W[2])},
+         {"V": _V % ("EW*16 ", _2[0], "ULF EA ULF OFA EA*7 X CS OFA X"), "S": _S % (_2[1], "XA DR OHA AR OHA XA XS XS"),
+          "P": _P % ("P6<CV ", "")}]
+TESTS = {"V": "N0 X0 U1 U0 n1 y8-11 W i j y11-13 l0 l1 l2 l3 d0 r0 a0 a1 a2 a3 b0 b1 b2 b3",
+         "S": "n0 y0-8 n2 y13-24 v g23 x0-24 g45 s2 s3 g67 s4 s5 s6 s7 c k",
+         "P": "T0 T1 T2 J q2 q3 o D q4 q5 q6 m0 h2 Z0 h3 A0 p q7 A1 A2 h4 Z1 A3 h5 B0 h6 B1 Z2 h7 B2 Z3 C B3"}
 FIRST = {"V": "l0 l1 l2 l3 d0 a0 L a1 a2 a3 b0 b1 b2 b3",
          "S": "g1 g2 s1 t0 g3 M g5 g4 s2 g7 s3 g6 s4 s5 s6 s7 c k",
          "P": "o D q1 q4 q2 h1 q3 h2 K q6 A0 Z0 A1 p h3 A2 q5 q7 h4 A3 h5 Z1 h6 B0 h7 B1 Z2 Z3 B2 C B3"}
 SHARE = {"W1": 1536, "X1": 1536, "X2": 256}
-STEPS = (416, 416, 416, 416, 416, 480)
+WALK = 320
+STEPS = (512,) + (128,) * 20
 COST = dict(cycle=0.95, pe=0.48, gather=1.55, scatter=3.5, act=65, hop=120, dma=700, row=45, rate=18.0, issue=300, first=1500,
-            remote=600, far=55)
-PASSES = 2
+            remote=600, far=55, scale=100)
+COSTS = [COST, dict(COST, cycle=0.9, gather=1.15, scatter=2.2, pe=0.55, hop=150, dma=1200, remote=900, scale=90),
+         dict(COST, cycle=1.1, gather=1.95, scatter=5.0, hop=90, row=25, rate=30.0, far=30, first=800, scale=130)]
+PASSES, TRIES, REACH, DEPTH, LEAN = 2, 4000, 40, 3, 0.2
 
 SCRATCH = {}
 
@@ -29,16 +45,16 @@ def _buf(dtype, **names):
         SCRATCH[k] = ("sbuf", [128] + (list(n) if isinstance(n, tuple) else [n]), dtype)
 
 
-_buf("bfloat16", X=3328, X1=3072, X2=3072, NXR=3328, BHB=192, BLB=192, QA=1024, QB=1024, QC=(4, 4, 16), QD=(16, 4, 16), DF=1024,
-     AB=4096, L1=4096, L2=4096, LW=1024, XG=4096, EA=2560, E16=16, SG=16, G6=96, WI=96, EW=(4, 4, 4, 4, 16))
-_buf("int32", ULI=1536, PW=3072, W1=3072, NXN=192, PVN=192, P2N=192, IDW=3072, BHI=192, BLI=192, KI=16, RM=16)
-_buf("uint16", NXL=192, PVL=192, P2L=192, DL=256, BLU=64, VC=48)
-_buf("float16", DI=256, FB=256, R4=256, XH=256, ZH=256, NH=384, TN=384, NI=8, VR=256, AR=256, IDH=128,
-     TD=(4, 2, 2, 16), TF=(4, 2, 2, 16), TG=(4, 2, 2, 16))
+_buf("bfloat16", X=3328, X1=3072, X2=3072, NXR=3328, BHB=192, BLB=192, QA=1024, QB=1024, QD=(16, 4, 16), DF=1024,
+     AB=4096, L1=4096, L2=4096, LW=1024, XG=4096, EA=1536, E16=16, SG=16, G6=96, WI=(16, 6), EW=(4, 4, 2, 4, 16))
+_buf("int32", ULI=1536, PW=3072, W1=3072, NXN=192, PVN=192, P2N=192, IDW=3072, BHI=192, BLI=192, KI=16, RM=16, XS=256)
+_buf("uint16", NXL=192, PVL=192, P2L=192, DL=256, BLU=64, VC=64)
+_buf("float16", N1B=256, DI=256, FB=256, R4=256, XH=256, ZH=256, NH=384, TN=384, NI=8, VH=16, VR=256, AR=256, IDH=128,
+     TD=(4, 2, 2, 16), TE=(4, 2, 2, 16), TH=(4, 2, 2, 16), TF=(4, 2, 2, 16), TG=(4, 2, 2, 16))
 _buf("float32", ULF=1792, IN160=160, SHF=160, IG16=128, DE=96, DR=96, SH=96, SR=96)
 for _t in range(NR + 1):
     SCRATCH["QJ%d" % _t] = ("sbuf", [128, 256], "bfloat16")
-    SCRATCH["VL%d" % _t] = ("sbuf", [128, 32], "uint16")
+    SCRATCH["VL%d" % _t] = ("sbuf", [128, 48], "uint16")
     if _t < NR:
         SCRATCH["ZB%d" % _t] = ("sbuf", [128, 256], "bfloat16")
         SCRATCH["MW%d" % _t] = ("sbuf", [128, 16], "uint16")
@@ -49,12 +65,12 @@ for _w, _names, _dt, _n, _u in (
         ("sm", "IP P16 G16 G15 C24 WA W11 T1 T2 BC ZC", "float32", 8, 1),
         ("ci", "IPI PI", "int32", 8, 1),
         ("lu", "KU AU AU2 AU4 OFA OFV N1U", "uint16", 16, 16),
-        ("lf", "DUA DUV I16 IV VF D15 JK", "float32", 16, 16),
+        ("lf", "DUA DUV I16 J16 IV VF D15 JK", "float32", 16, 16),
         ("mat", "U UM UC UA", "bfloat16", 144, 144),
         ("mh", "UR B0 B1 B0N B1N", "float16", 160, 160),
         ("sq", "BB4 TR TRE ONE CB C15 IDP IDM ID4 IDM4", "bfloat16", 128, 128),
-        ("ff", "DB D0 K1 K0 DD SL RI CS CV CW DM OHA YG YR", "float32", 256, 256),
-        ("bb", "K16 MK QM NNB ON MON PO C1 XA XS YQ OH N1B NF", "bfloat16", 256, 256)):
+        ("ff", "DB D0 K1 K0 DD SL RI CS DM OHA YG YR", "float32", 256, 256),
+        ("bb", "K16 MK QM NNB ON MON PO C1 XA YQ OH NF CV", "bfloat16", 256, 256)):
     for _j, _nm in enumerate(_names.split()):
         _PACK[_nm] = (_w, _j * _n)
         _WIDTH[_nm] = _u
@@ -92,7 +108,7 @@ def apart(x, y):
 
 def before(calls):
     log, bank, pred = {}, {}, []
-    for k, (q, _t, lead, w, r, flags, _g) in enumerate(calls):
+    for k, (q, _t, lead, w, r, flags, _g, _n) in enumerate(calls):
         need = {}
         for keys, wr in ((w, True), (r, False)):
             for x in keys:
@@ -108,18 +124,34 @@ def before(calls):
                     for j in ps:
                         if j is not None and j != k:
                             free = calls[j][0] == q and (q == "P" or wr or j != B["wrote"])
-                            need[j] = max(need.get(j, 0), 0 if free else COST["hop"])
+                            need[j] = max(need.get(j, 0), 0 if free else 1)
                     if q != "P":
                         B["other"] = k
                         if any(y[0] == nm for y in w) and (not wr or all(y[0] != nm for y in r)): B["wrote"] = k
                     continue
                 L = log.setdefault(nm, [])
                 for y, wrote, j in L:
-                    if j != k and (wrote or wr) and not apart(x, y): need[j] = 0 if calls[j][0] == q == "P" else COST["hop"]
+                    if j != k and (wrote or wr) and not apart(x, y): need[j] = 0 if calls[j][0] == q == "P" or x[0][0] == "_" else 1
                 if wr and x[3] == 1 and x[4] is None: L[:] = [e for e in L if not (x[1] <= e[0][1] and e[0][2] <= x[2])]
                 L.append((x, wr, k))
-        pred.append([(j, d + lead) for j, d in need.items()])
+        pred.append(need)
     return pred
+
+
+def named(calls):
+    pairs = []
+    for q in "VSPG":
+        was = None
+        for t in range(-1, NR * (q != "G")):
+            left = [k for k, c in enumerate(calls) if c[0] == q and c[7][0] == t]
+            for x in START[q].split() if t < 0 else (
+                    [y + "*9" for y in (TESTS if t else FIRST)[q].split()[:5 * (t > 0) if q == "P" else None]] + CHAIN[t][q].split()):
+                x, _s, m = x.partition("*")
+                for k in [k for k in left if calls[k][7][1] == x][:int(m or 1)]:
+                    if was is not None: pairs.append((was, k))
+                    left.remove(k)
+                    was = k
+    return pairs
 
 
 def place(calls, pred, seq, gaps=True):
@@ -139,21 +171,80 @@ def place(calls, pred, seq, gaps=True):
     return start, end
 
 
+def replay(each, pred, seq):
+    end, cause, last = [0.0] * len(each), [None] * len(each), {}
+    for k in seq:
+        q, d, t = each[k]
+        why = last.get(q)
+        if why is not None and end[why] > t: t = end[why]
+        for j, x in pred[k]:
+            if end[j] + x > t: t, why = end[j] + x, j
+        end[k], cause[k], last[q] = t + d, why, k
+    return end, cause
+
+
 def arrange(calls):
-    pred = before(calls)
-    succ = [[] for _ in calls]
-    for k, ps in enumerate(pred):
-        for j, x in ps: succ[j].append((k, x))
-    back = [c[:2] + (0,) for c in calls]
-    start, end = place(calls, pred, range(len(calls)), False)
-    tried = []
+    needs = before(calls)
+    preds = [[[(j, d * C["hop"] + calls[k][2][m]) for j, d in need.items()] for k, need in enumerate(needs)] for m, C in enumerate(COSTS)]
+    each = [[(c[0], c[1][m], c[2][m]) for c in calls] for m in range(len(COSTS))]
+
+    def after(pred):
+        succ = [[] for _ in calls]
+        for k, ps in enumerate(pred):
+            for j, x in ps: succ[j].append((k, x))
+        return succ
+
+    pred = [list(x) for x in preds[0]]
+    for j, k in named(calls): pred[k].append((j, 0))
+    succ, seq, done = after(pred), [], set()
+    while len(seq) < len(calls):
+        seq.append(next(k for k in range(len(calls)) if k not in done and all(j in done for j, _x in pred[k])))
+        done.add(seq[-1])
+    back = [c[:2] + (0,) for c in each[0]]
+    start, end = place(each[0], pred, seq, False)
     for _ in range(PASSES):
-        late = place(back, succ, sorted(start, key=lambda k: (-end[k], -k)))[1]
-        start, end = place(calls, pred, sorted(start, key=lambda k: (-late[k], k)))
-        tried.append((max(end.values()), len(tried), start, end))
-    start, end = min(tried)[2:]
-    ready = lambda k: max([end[j] + x for j, x in pred[k]], default=0) if calls[k][5] == "act" else start[k]
-    return sorted(start, key=lambda k: (ready(k) - calls[k][2], k))
+        late = place(back, succ, sorted(start, key=lambda k: (-end[k], -start[k])))[1]
+        start, end = place(each[0], pred, sorted(start, key=lambda k: (-late[k], start[k])))
+    seq = sorted(start, key=lambda k: (start[k] - each[0][k][2], k))
+    pred = preds[0]
+    succ = after(pred)
+
+    def worth(s):
+        runs = [replay(e, p, s) for e, p in zip(each, preds)]
+        return sum((max(x[0]) + LEAN * sum(x[0]) / len(s)) / C["scale"] for x, C in zip(runs, COSTS)), runs
+
+    def moved(s, a, b, links):
+        along, want = [], {s[b]}
+        for i in range(b, a - 1, -1):
+            if s[i] in want:
+                along.append(s[i])
+                want.update(j for j, _x in links[s[i]])
+        return None if along[-1] == s[a] else s[:a] + along[::-1] + [k for k in s[a:b + 1] if k not in want] + s[b + 1:]
+
+    best, runs = worth(seq)
+    tries, better = 0, True
+    while better and tries < TRIES:
+        better = False
+        for m in range(len(COSTS)):
+            end, cause = runs[m]
+            k, links = max(seq, key=lambda j: end[j]), []
+            while cause[k] is not None:
+                if calls[cause[k]][0] == calls[k][0] and all(j != cause[k] for j, _x in pred[k]): links.append((cause[k], k))
+                k = cause[k]
+            for j, k in links:
+                a, b = seq.index(j), seq.index(k)
+                if a > b: continue
+                same = [i for i in range(max(0, a - REACH), min(len(seq), b + REACH)) if calls[seq[i]][0] == calls[k][0]]
+                rev, z = seq[::-1], len(seq) - 1
+                for s in ([moved(seq, i, b, pred) for i in same[::-1] if i <= a][:DEPTH]
+                          + [(moved(rev, z - i, z - a, succ) or [])[::-1] for i in same if i >= b][:DEPTH]):
+                    if not s: continue
+                    tries += 1
+                    w, r = worth(s)
+                    if w < best - 1e-9:
+                        best, runs, seq, better = w, r, s, True
+                        break
+    return seq
 
 
 def rank_program(g, core, T, topo):
@@ -176,7 +267,7 @@ def rank_program(g, core, T, topo):
         if hi is None: hi = _WIDTH[name] if name in _PACK else T[w].shape[1]
         lo, hi = lo + b, hi + b
         ap = T[w][:, lo:hi:step] if step != 1 else T[w][:, lo:hi]
-        return (ap, [(w, lo, hi, step, None)], [], len(range(lo, hi, step)))
+        return (ap, [(w, lo, hi, step, None)], [], len(range(lo, hi, step)), name.rstrip("012") if name[:2] in ("QJ", "ZB", "MW") else name)
 
     def n(name, *ix, key=None):
         f = ix[0] if ix else A
@@ -184,17 +275,17 @@ def rank_program(g, core, T, topo):
         m = 1
         for k, d in enumerate(SCRATCH[name][1][1:]):
             if k >= len(ix) or isinstance(ix[k], slice): m *= len(range(d)[ix[k] if k < len(ix) else A])
-        return (T[name][(A,) + ix], [(name,) + (key or (lo, hi, 1)) + (None,)], [], m)
+        return (T[name][(A,) + ix], [(name,) + (key or (lo, hi, 1)) + (None,)], [], m, name)
 
     def ew(h, c, d, hs=A):
-        return n("EW", h, c, d, hs, key=(4 * h, 4 * h + 4, 1) if c == A else (4 * h + c, 4 * h + c + 1, 1))
+        return n("EW", h, c, d, hs, key=(4 * h + c, 4 * h + c + 1, 1) if isinstance(c, int) else (4 * h, 4 * h + 4, 1))
 
     def rows(name, f, lo=0, hi=3072):
         w, b = _PACK.get(name, (name, 0))
-        return (T[w][f:128:16, lo + b:hi + b], [(w, lo + b, hi + b, 1, f)], [], hi - lo)
+        return (T[w][f:128:16, lo + b:hi + b], [(w, lo + b, hi + b, 1, f)], [], hi - lo, name)
 
     def ind(win, off):
-        return (win[0].indirect(off[0]), win[1], off[1], 16 * off[3])
+        return (win[0].indirect(off[0]), win[1], off[1], 16 * off[3], win[4])
 
     def width(x): return 4 if SCRATCH[x[1][0][0]][2] in ("float32", "int32") else 2
 
@@ -226,22 +317,24 @@ def rank_program(g, core, T, topo):
                     if kind == "w" and x[3] == 1 and x[4] is None: L[:] = [e for e in L if not (x[1] <= e[0][1] and e[0][2] <= x[2])]
                     L.append((x, kind, tok))
 
+    none, at = [0] * len(COSTS), [0, None]
     calls = []
 
     def emit(q, fn, outs, ins, twice=False, flags=None, gp=None):
         w, r = [], []
         for o in outs: w += o[1]; r += o[2]
         for i in ins: r += i[1] + i[2]
-        m, C = outs[0][3], COST
-        if q == "P": time = C["pe"] * max(64, m)
-        elif q == "G": time = gp + 2 * C["cycle"] * m
-        elif outs[0][2]: time = 50 + C["scatter"] * C["cycle"] * m
-        elif ins and ins[0][2]: time = {"V": 50, "S": 65}[q] + C["gather"] * C["cycle"] * m
-        elif q == "S": time = C["act"] + C["cycle"] * m
-        else:
+        m = outs[0][3]
+
+        def time(C):
+            if q == "P": return C["pe"] * max(64, m)
+            if q == "G": return gp + 2 * C["cycle"] * m
+            if outs[0][2]: return 50 + C["scatter"] * C["cycle"] * m
+            if ins and ins[0][2]: return {"V": 50, "S": 65}[q] + C["gather"] * C["cycle"] * m
+            if q == "S": return C["act"] + C["cycle"] * m
             half = all(width(x) == 2 for x in outs + ins if x[3] == m)
             both = twice and not any(is_bank(x[1][0][0]) for x in ins)
-            time = C["cycle"] * max(64, m * (0.5 if half else 1) * (2 if both else 1))
+            return C["cycle"] * max(64, m * (0.5 if half else 1) * (2 if both else 1))
 
         def go():
             order(q, w, r)
@@ -250,7 +343,13 @@ def rank_program(g, core, T, topo):
             now = dict(know[q]); now[q] = cnt[q]
             snap[(q, cnt[q])] = now
             note((q, cnt[q]), w, r)
-        calls.append((q, time, 0, w, r, flags, go))
+        name = at[1] or (outs[0][4] + "<" + ins[1][4] if q == "P" else outs[0][4])
+        calls.append((q, [time(C) for C in COSTS], none, w, r, flags, go, (at[0], name)))
+
+    def join(k):
+        part = calls[k:]
+        calls[k:] = [("P", [sum(x) for x in zip(*[c[1] for c in part])], none, [x for c in part for x in c[3]],
+                      [x for c in part for x in c[4]], (part[0][5][0], part[-1][5][1]), lambda: [c[6]() for c in part], part[0][7])]
 
     def dma(out, in_, q="sync"):
         qk = {"sync": "sync", "act": "S"}[q]
@@ -259,7 +358,7 @@ def rank_program(g, core, T, topo):
         sides = [x for x in (out, in_) if isinstance(x, tuple)]
         full = [x for x in sides if x[1][0][4] is None]
         x = (full or sides)[0]
-        time = 8 * (COST["row"] + x[3] * width(x) / COST["rate"]) if full else COST["row"] + x[3] * width(x) / 2 / COST["rate"]
+        time = [8 * (C["row"] + x[3] * width(x) / C["rate"]) if full else C["row"] + x[3] * width(x) / 2 / C["rate"] for C in COSTS]
 
         def go():
             order(qk, w, r)
@@ -270,7 +369,9 @@ def rank_program(g, core, T, topo):
             unit[nm] = 16; total[nm] = 1
             snap[(nm, 1)] = dict(know[qk])
             note((nm, 1), w, r)
-        calls.append(("D", time, COST["dma"], w, r, q, go))
+        tok = [("_%d" % len(calls), 0, 1, 1, None)] if q == "act" else []
+        if tok: calls.append(("S", [C["act"] for C in COSTS], none, tok + w, r, None, go, (at[0], "dma")))
+        calls.append(("D", time, [C["dma"] for C in COSTS], w, r + tok, None, None if tok else go, (at[0], "dma")))
 
     def engines(src, dst, h):
         return topo.engines(src, dst)[{1: slice(0, 4), 2: slice(4, 8), 3: slice(0, 8)}[h]]
@@ -296,9 +397,10 @@ def rank_program(g, core, T, topo):
             total[nm] = 1
             snap[(nm, 1)] = {}
             note((nm, 1), w, [])
-        tok = [(nm, 0, 1, 1, None)]
-        calls.append(("G", 2 * COST["issue"] + COST["first"] * (nm == "z0"), 0, tok, r, None, go))
-        calls.append(("R", 48 * (COST["far"] + src[1][3] * 2 / COST["rate"]), COST["remote"], w, tok, None, None))
+        tok = [("_" + nm, 0, 1, 1, None)]
+        calls.append(("G", [2 * C["issue"] + C["first"] * (nm == "z0") for C in COSTS], none, tok + w, r, None, go, (t, nm)))
+        calls.append(("R", [48 * (C["far"] + src[1][3] * 2 / C["rate"]) for C in COSTS], [C["remote"] for C in COSTS], w, tok, None,
+                      None, (t, nm)))
 
     def cp(o, i): emit("V", lambda: g.vector.tensor_copy(o[0], i[0]), [o], [i])
     def tt(o, a, b, op): emit("V", lambda: g.vector.tensor_tensor(o[0], a[0], b[0], op), [o], [a, b], True)
@@ -336,12 +438,14 @@ def rank_program(g, core, T, topo):
     def diag(out, mat, src, start=True):
         for r in range(16):
             mm(out, usl(mat, r), v(src, r, 256, 16), start and r == 0, r == 15)
+        join(-16)
 
-    def unturn(bank, part, terms, stop=True):
+    def unturn(bank, part, terms, stop=True, start=True):
         each = [(f, e, x) for x in terms for f in range(2) for e in range(2)]
         for k, (f, e, (neg, src, a, b, m)) in enumerate(each):
             mm(n(bank, part, slice(f, 4, 2), slice(b, b + m)), sel(f, e, neg), n(src, A, A, e, slice(a, a + m)),
-               k == 0, stop and k == len(each) - 1)
+               start and k == 0, stop and k == len(each) - 1)
+            if k % 4 == 3: join(-4)
 
     def to_list(nat, bank, o=0):
         if nat:
@@ -351,120 +455,118 @@ def rank_program(g, core, T, topo):
             for e in range(2):
                 b = o + 32 * (m // 2) + 16 * e
                 mm(v(bank, m, 192, 12), sel(m % 2, e), v("TN", b, b + 16), e == 0, e == 1)
+        if bank: join(-24)
 
-    def repeat(classes, qs):
-        for h in range(4):
-            (gcp if qs[h] == "G" else act)(n("QC", A, h, key=(h, 64, 4)), classes[h])
-        for k in range(4):
-            gcp(n("QD", A, k, key=(k, 64, 4)), n("QC"))
+    def repeat(classes, out):
+        for h in range(4): gcp(n("QD", slice(h, 16, 4), 0, key=(h, 16, 4)), classes[h])
+        for k in (1, 2): gcp(n("QD", A, slice(k, 2 * k), key=(16 * k, 32 * k, 1)), n("QD", A, slice(0, k), key=(0, 16 * k, 1)))
+        (cp if at[0] in QUICK else dma)(v(out), n("QD"))
 
-    dma(v("NXN"), T.nx[:])
-    dma(v("PVN"), T.pv[:], "act")
+    at[0] = -1
+    dma(v("PVN"), T.pv[:])
+    dma(v("NXN"), T.nx[:], "act")
     dma(v("QM"), T.mv[:])
     fill(v("PW", 0, 512), 1536)
     iota(v("SHF"), [[32, 5], [1016, 2], [1, 16]], -16, -1)
     ts(v("B1"), v("SHF"), 0.0, OP.is_equal)
     ts(v("B0"), v("SHF"), 1000.0, OP.is_equal)
-    for k in (1, 2): fill(v("PW", 512 * k, 512 * k + 512), 1536)
-    iota(v("PW", 2560, 3072), [[0, 512]], 1536, 0, False)
+    fill(v("PW", 512, 1024), 1536)
+    iota(v("PW", 2688, 3072), [[0, 384]], 1536, 0, False)
     iota(v("IPI"), [[1, 1]], 0, 1, False)
     iota(v("IP"), [[1, 1]], 0, 1)
     iota(v("IN160"), [[1, 160]])
     iota(v("IV"), [[384, 4], [6, 4]])
-    iota(v("IG16"), [[16, 8], [0, 16]])
-    for k in (3, 4): act(v("PW", 512 * k, 512 * k + 512), v("PW", 0, 512))
+    for a, b in ((1024, 1536), (1536, 2048), (2048, 2688)): act(v("PW", a, b), v("PW", 0, b - a))
     dma(rows("PW", 4), T.pv[:])
     dma(rows("PW", 11), T.rc[:], "act")
     dma(v("X", 0, 3072), T.xd[:])
     dma(v("ULI"), T.ul[:])
 
+    def eye(name, c): keep(v(name), v("C15"), [[-1, 128]], OP.not_equal, 0, 1, c)
     to_list("PVN", "P4", 192)
     to_list("NXN", "P3")
+    fill(v("C15"), 0.0)
+    fill(v("ON"), 1.0)
+    fill(v("MON"), -1.0)
+    fill(v("CB"), -61440.0)
     ts(v("PI"), v("IPI"), 15, OP.bitwise_and)
     cp(v("P16"), v("PI"))
-    fill(v("ON"), 1.0)
     tt(v("G16"), v("IP"), v("P16"), OP.subtract)
-    repeat([v("QM", h, 256, 4) for h in range(4)], "GGGG")
     ts(v("G15"), v("G16"), 15.0, OP.add)
-    ts(v("C24"), v("P16"), 24.0, OP.mult)
     ts(v("U"), v("IN160", 0, 144), v("G15"), OP.is_equal)
-    ts(v("VC", 0, 16), v("IV"), v("C24"), OP.add)
-    fill(v("MON"), -1.0)
+    ts(v("E16"), v("IN160", 0, 16), v("P16"), OP.is_equal)
+    act(v("C24"), v("P16"), scale=24.0)
+    act(v("VC", 0, 16), v("IV"), bias=v("C24"))
+    act(v("B0N"), v("B0"), scale=-1.0)
+    act(v("B1N"), v("B1"), scale=-1.0)
+    act(v("UC"), v("U"), scale=1048576.0)
+    act(v("UM"), v("U"), scale=-1.0)
+    act(v("WA"), v("E16", 7, 8), scale=64.0, bias=v("E16", 6, 7))
+    act(v("UA"), v("U"), scale=v("WA"))
+    act(v("PO", 0, 16), v("E16"), scale=4195840.0, bias=-4194304.0)
+    iota(v("I16"), [[16, 16]], 1536)
+    iota(v("J16"), [[16, 16]], 3072)
+    act(v("DUV"), v("I16"), bias=v("P16"))
+    act(v("DUA"), v("J16"), bias=v("P16"))
     ts(v("PVL"), v("P4", 0, 192), OFF, OP.add)
+    repeat([v("QM", h, 256, 4) for h in range(4)], "QA")
     for out, win, lst in (("W1", "PW", "PVL"), ("X1", "X", "NXL"), ("X2", "X1", "NXL")):
         table("V", out, win, lst, 0, SHARE[out])
         table("S", out, win, lst, SHARE[out], 3072)
-        if out == "W1":
-            ts(v("NXL"), v("P3", 0, 192), OFF, OP.add)
-            ts(v("BB4"), v("IG16"), v("G16"), OP.is_equal, 4096.0, OP.mult)
-            fill(v("CB"), -61440.0)
-            ts(v("UC"), v("U"), 1048576.0, OP.mult)
-            fill(v("C15"), 15.0 / 16 / 128)
-            ts(v("UM"), v("U"), -1.0, OP.mult)
-            ts(v("B0N"), v("B0"), -1.0, OP.mult)
-            ts(v("B1N"), v("B1"), -1.0, OP.mult)
-    dma(v("P2N"), rows("W1", 4))
+        if out == "W1": ts(v("NXL"), v("P3", 0, 192), OFF, OP.add)
+    if DEEP: dma(v("P2N"), rows("W1", 4))
     dma(rows("PW", 3), rows("W1", 4))
     dma(rows("PW", 10), rows("W1", 11))
-    keep(v("IDM"), v("MON", 0, 128), [[-1, 128]], OP.is_equal, 0, 1)
-    keep(v("IDP"), v("ON", 0, 128), [[-1, 128]], OP.is_equal, 0, 1)
-    iota(v("I16"), [[16, 16]])
-    iota(v("K16"), [[0, 16], [1, 16]])
+    for name, c in (("IDM", -1.0), ("IDP", 1.0), ("IDH", 1.0), ("IDM4", -4096.0), ("ID4", 4096.0)): eye(name, c)
+    iota(v("BB4"), [[0, 128]], 4096)
+    keep(v("BB4"), v("BB4"), [[-16, 8], [0, 16]], OP.is_ge, 0, 1)
+    keep(v("BB4"), v("BB4"), [[16, 8], [0, 16]], OP.is_ge, 15, -1)
     keep(v("TR"), v("BB4"), [[1, 128]], OP.is_gt, 0, -1)
     keep(v("TRE"), v("BB4"), [[1, 128]], OP.is_ge, 0, -1)
     keep(v("D0"), v("ON"), [[0, 16], [1, 16]], OP.is_gt, 0, 0)
     keep(v("DB"), v("MON"), [[0, 16], [1, 16]], OP.is_gt, 0, 0, 524288.0)
-    iota(v("WI"), [[0, 16], [-16, 6]], 16)
-    keep(v("WI"), v("WI"), [[0, 16], [-1, 6]], OP.is_ge, 0, 0)
-    gcp(v("IDH"), v("IDP"))
+    iota(n("WI"), [[0, 16], [-16, 6]], 16)
+    keep(n("WI"), n("WI"), [[0, 16], [-1, 6]], OP.is_ge, 0, 0)
+    for k in (16, 32, 64, 128): gcp(v("PO", k, 2 * k), v("PO", 0, k))
     for h in range(4):
         gcp(v("QJ0", 64 * h, 64 * h + 64), v("QM", h, 256, 4))
     ts(v("DI"), ind(v("ULI"), v("VC", 0, 16)), -OFF, OP.add)
-    cp(v("QA"), n("QD"))
     turn(n("TD"), v("DI"))
     unturn("P5", H4, [("", "TD", 0, 0, 16)])
     for k in range(3):
         iota(v("IDW", 1024 * k, 1024 * k + 1024), [[1, 1024]], 1024 * k, 0, False)
     dma(rows("PW", 5), rows("IDW", 5))
     dma(v("NXR", 0, 3072), v("X", 0, 3072))
-    gcp(v("ULF", 0, 1536), v("ULI"))
-
-    def late_consts(part):
-        if part == 0:
-            ts(v("E16"), v("IN160", 0, 16), v("P16"), OP.is_equal)
-            fill(v("ONE"), 1.0)
-            ts(v("T1"), v("P16"), 7.0, OP.is_equal, 64.0, OP.mult)
-            ts(v("T2"), v("P16"), 6.0, OP.is_equal)
-            ts(v("W11"), v("P16"), 11.0, OP.is_equal)
-            ts(v("MK"), v("K16"), v("P16"), OP.not_equal)
-            ts(v("PO"), v("MK"), -4194304.0, OP.mult, OFF, OP.add)
-        if part == 1:
-            ts(v("BHI"), v("NXN"), 6, OP.arith_shift_right)
-            ts(v("BLI"), v("NXN"), 63, OP.bitwise_and)
-            gcp(v("BHB"), v("BHI"))
-            gcp(v("BLB"), v("BLI"))
-            dma(rows("NXR", 7), v("BHB"))
-            dma(rows("NXR", 6), v("BLB"))
-        if part == 2:
-            ts(v("IDM4"), v("IDP"), -4096.0, OP.mult)
-            ts(v("ID4"), v("IDP"), 4096.0, OP.mult)
-            tt(v("WA"), v("T1"), v("T2"), OP.add)
-            ts(v("UR", 0, 144), v("U"), v("W11"), OP.mult)
-        if part == 3:
-            ts(v("UA"), v("U"), v("WA"), OP.mult)
-            ts(v("DUV"), v("I16"), v("P16"), OP.add, 1536.0, OP.add)
-            ts(v("DUA"), v("I16"), v("P16"), OP.add, 3072.0, OP.add)
+    for k in range(3): gcp(v("ULF", 512 * k, 512 * k + 512), v("ULI", 512 * k, 512 * k + 512))
+    ts(v("BHI"), v("NXN"), 6, OP.arith_shift_right)
+    ts(v("BLI"), v("NXN"), 63, OP.bitwise_and)
+    gcp(v("BHB"), v("BHI"))
+    gcp(v("BLB"), v("BLI"))
+    dma(rows("NXR", 7), v("BHB"))
+    dma(rows("NXR", 6), v("BLB"))
 
     def steps(*ks):
         for k in ks:
-            table("S", "W1", "PW", "P2L", sum(STEPS[:k]), sum(STEPS[:k + 1]))
+            table("SV"[k < 5], "W1", "PW", "P2L", sum(STEPS[:k]), sum(STEPS[:k + 1]))
 
     def sums(bank, mat, src, q, last):
         for r in range(16):
             mm(n(bank, H4, A, slice(4 * q, 4 * q + 4)), usl(mat, r), v(src, 1024 * q + r, 1024 * q + 1024, 16), False, last and r == 15)
+            if r % 8 == 7: join(-8)
 
     EIGHTH = ("P3", "P4", "P7", "P5", "P6")
     HALVES = ((0, 128, "P3"), (128, 256, "P4"))
+
+    def places(t, j):
+        a, b = HALVES[j][:2]
+        if t: tt(ind(v("ULF"), v("OFV", a // 16, b // 16)), v("DM", a, b), v("OHA", a, b), OP.max)
+        elif j == 0: tt(ind(v("ULF"), v("VC", 0, 16)), v("DM"), v("OHA"), OP.max)
+
+    def lay(t, q):
+        for h in range(4):
+            at[1] = "W" if h and t < NR else None
+            add(q if h else "S", v("VC", 16 * t + h, 16 * t + 16, 4) if t < NR else v("VC", 16 * t + 4 * h, 16 * t + 4 * h + 4),
+                v("VL%d" % t, 17 * h - 16, 16 * h, 4) if h else v("MW%d" % (t - 1), 0, 16, 4), 0.0)
 
     for t in range(NR):
         Q, Qn, VL, Vn = "QJ%d" % t, "QJ%d" % (t + 1), v("VC", 16 * t, 16 * t + 16), "VL%d" % (t + 1)
@@ -481,9 +583,9 @@ def rank_program(g, core, T, topo):
             k, j = x[0], int(x[1]) if x[1:2].isdigit() else 0
             if k in "xy":
                 lo, hi = [int(u) for u in x[1:].split("-")]
-                return y[0] == "y" if k == "x" else y == "X" or y in ["n%d" % u for u in range(lo // 8, (hi + 7) // 8)]
+                return y[0] == "y" if k == "x" else y[0] == "X" or y in ["n%d" % u for u in range(lo // 8, (hi + 7) // 8)]
             if y[0] in {"a": "yQ", "b": "xQ", "d": "XQ", "g": "X", "q": "Q", "c": "A", "k": "Z", "m": "o", "Z": "o", "A": "o", "B": "p",
-                        "C": "pc", "i": "W", "v": "W", "j": "i", "J": "j", "l": "J", "T": "N", "w": "v", "D": "j", "p": "D", "K": "L",
+                        "C": "pc", "i": "WU", "v": "W", "j": "i", "J": "j", "l": "J", "T": "N", "w": "v", "D": "j", "p": "D", "K": "L",
                         "M": "K"}.get(k, ""): return True
             if k == "h" and y[0] == "g": return x[1] in y
             return y in {"n": ["T%d" % j], "d": ["l0"], "g": ["l%d" % (j // 2)], "a": ["l%d" % j], "b": ["l%d" % j],
@@ -492,24 +594,26 @@ def rank_program(g, core, T, topo):
                          "h": ["q%d" % j], "Z": ["t%d" % j, "r%d" % j, "m%d" % j, "s%d" % (2 * j), "s%d" % (2 * j + 1)]}.get(k, [])
 
         def run(x, q):
+            at[1] = x
             k, j = x[0], int(x[1]) if x[1:2].isdigit() else 0
             last = lambda kinds: x == [y for y in tens if y[0] in kinds][-1]
             bank = EIGHTH[(7 - j) % 5]
-            if k == "X": cp(ind(v("X"), v("OFA")), v("XS"))
-            if k == "N": cp(ind(v("NXR"), v("OFA")), v("NNB"))
-            if k == "W":
-                for h in range(1, 4): add(q, v("VC", 16 * t + h, 16 * t + 16, 4), v("VL%d" % t, 4 + 4 * h, 8 + 4 * h), 0.0)
-            if k == "Q": dma(v(Q4), n("QD"))
+            if k in "XN":
+                a, b = HALVES[j][:2]
+                cp(ind(v({"X": "X", "N": "NXR"}[k]), v("OFA", a // 16, b // 16)), v({"X": "XS", "N": "NNB"}[k], a, b))
+            if k == "U": places(t - 1, j)
+            if k == "W": lay(t, q)
             if k == "i": add(q, v("DI"), ind(v("ULF", 0, 1536), VL), -OFF)
-            if k == "L": to_list("P2N", None)
-            if k == "K": to_list(None, "P7")
-            if k == "M": add(q, v("P2L"), v("P7", 0, 192), OFF)
+            if k == "L" and DEEP: to_list("P2N", None)
+            if k == "K" and DEEP: to_list(None, "P7")
+            if k == "M" and DEEP: add(q, v("P2L"), v("P7", 0, 192), OFF)
             if k == "j": turn(n("TD"), v("DI"))
             if k == "J": unturn("P5", H4, [("", "TD", 0, 0, 16)])
             if k == "l": add(q, v("DL", 64 * j, 64 * j + 64), n("P5", H4, A, slice(4 * j, 4 * j + 4)), OFF)
             if k == "T":
                 for r in range(16):
                     mm(v(EIGHTH[j], 0, 64), usl("UA", r), v("NXR", 1024 * j + r, 1024 * j + 1024, 16), r == 0, r == 15)
+                join(-16)
             if k == "n": add(q, v("NXL", 64 * j, 64 * j + 64), v(EIGHTH[j], 0, 64), 0.0)
             if k in "xy":
                 lo, hi = [128 * int(u) for u in x[1:].split("-")]
@@ -517,6 +621,7 @@ def rank_program(g, core, T, topo):
             if k == "v":
                 act(v("VR"), ind(v("IDW"), VL))
                 act(v("VF"), VL)
+                gcp(v("VH", 0, 16), v("VF"))
             if k == "d": test("X", "DF", 0, OP.subtract, m0)
             if k == "t": act(v("AB", 0, m0), v("DF", 0, m0), AF.Abs)
             if k == "r": ts(v("AB", 0, m0), v("DF", 0, m0), 0.0, OP.max, 2.0, OP.mult)
@@ -528,8 +633,7 @@ def rank_program(g, core, T, topo):
             if k == "s": act(v("AB", 512 * j, 512 * j + 512), n(bank), AF.Abs)
             if k == "c": act(v("C1"), n("P1", H4), AF.Relu, scale=32.0)
             if k == "k":
-                act(v("K0"), n("P0", H4), scale=16.0)
-                act(v("K1"), n("P0", H4), scale=-16.0, bias=BIG)
+                for a, b, key in HALVES: act(v(key, 0, 128), n("P0", slice(a // 64, b // 64)), scale=-16.0, bias=65536.0)
             if k == "o": mm(n("P0", H4), v("C15"), v("ON"), True, False)
             if k in "op": mm(n("P1" if k == "o" else "P2", H4), v("CB"), v("ON"), True, False)
             if k == "D": unturn("P2", slice(4, 8), [("N", "TD", 0, 0, 16), ("", "TD", 0, 1, 15)])
@@ -541,146 +645,138 @@ def rank_program(g, core, T, topo):
             if k == "A": sums("P1", "UC", "L1", j, last("A"))
             if k == "B": sums("P2", "UC", "L2", j, last("BC"))
             if k == "C": mm(n("P2", H4), v("IDP"), v("C1"), False, last("BC"))
+            at[1] = None
 
         pairs = [] if first else [(h, c) for h in range(4) for c in range(4)]
 
         def equal(m):
             for h, c in pairs[:m]:
-                ts(ew(h, c, slice(0, 4 - c)), v("VR", 64 * c, 256), v("VF", 4 * c + h, 4 * c + h + 1), OP.is_equal)
+                ts(ew(h, c, slice(0, 2 - c % 2)), v("VR", 64 * c, 128 * (c // 2 + 1)), v("VF", 4 * c + h, 4 * c + h + 1), OP.is_equal)
             del pairs[:m]
 
         def count(*hs):
             for h in hs:
                 if h == 0: mm(n("P1", H4), v("IDP"), v("PO"), True, False)
-                for c in range(3):
-                    mm(n("P1", slice(c + 1, 4)), v("BB4"), ew(h, c, slice(1, 4 - c)), False, False)
                 mm(n("P1", H4, slice(0, h + 1)), v("TR"), ew(h, A, 0, slice(0, h + 1)), False, False)
                 if h < 3: mm(n("P1", H4, slice(h + 1, 4)), v("TRE"), ew(h, A, 0, slice(h + 1, 4)), False, False)
+                mm(n("P1", slice(1, 4, 2)), v("BB4"), ew(h, slice(0, 4, 2), 1), False, h == 3)
 
+        def aside():
+            act(v("RM"), v("RI", 15, 256, 16), bias=131087.0)
+            ts(v("KI"), v("RM"), 15, OP.bitwise_and)
+            act(v("KU"), v("KI"))
+            act(v("OH"), ind(v("E16"), v("KU")))
+            mm(v("P3", 0, 256), v("IDM4"), v("OH"), False, True)
+            act(v("DM"), v("P3", 0, 256), bias=OFF)
+            gcp(v(Qn, 0, 64), v(ZB, 0, 64))
+            if not first:
+                act(v("CV"), n("P1", H4), AF.Relu, bias=-OFF)
+                mm(n("P6", 0, 0), v("IDH"), v("VH", 0, 16), True, False)
+                diag(n("P6", 0, 0), "U", "CV", False)
+                tt(v("OFV"), n("P6", 0, 0), v("DUV"), OP.min)
+
+        at[0] = t
         weave(lists, needs, run)
-        if first:
-            late_consts(0)
-            steps(0)
         cp(v("D15"), v("DL", 195, 256, 4))
-        for a, b, key in HALVES: tt(v(key, 0, 128), n("P2", slice(a // 64, b // 64)), v("K0", a, b), OP.max)
+        equal(16)
+        for a, b, key in HALVES: act(v("C1", a, b), n("P2", slice(a // 64, b // 64)), AF.Sign)
         act(v("DD"), n("P2", slice(4, 8)))
-        for a, b, key in HALVES: tt(v(key, 0, 128), v(key, 0, 128), v("K1", a, b), OP.min)
+        for a, b, key in HALVES: tt(v(key, 0, 128), v(key, 0, 128), v("C1", a, b), OP.mult)
         for a, b, key in HALVES: scan(v("RI", a, b), v("DB", a, b), v(key, 0, 128), 1000000.0, OP.add, OP.min)
-        if not first:
-            count(0, 1)
-            mm(v("P7", 0, 256), v("IDP"), v("PO"), True, False)
+        if not first: count(0, 1, 2, 3)
+        act(v("SG"), v("RI", 15, 256, 16), AF.Sign)
         for a, b, key in HALVES: tt(v("NF", a, b), v(key, 0, 128), v("RI", a, b), OP.not_equal)
+        mm(v("P4", 0, 16), v("ON", 0, 128), v("SG"), True, True)
         for a, b, key in HALVES: scan(v("SL", a, b), v("DD", a, b), v("NF", a, b), 0.0, OP.add, OP.mult)
-        for a, b, key in HALVES: tt(v("AU", a // 16, b // 16), v("SL", a + 15, b, 16), v("D15", a // 16, b // 16), OP.add)
-        equal(2)
-        if first: late_consts(1)
-        cp(v("RM"), v("RI", 15, 256, 16))
-        ts(v("KI"), v("RM"), 15, OP.bitwise_and)
-        cp(v("KU"), v("KI"))
-        act(v("SG"), v("RI", 15, 256, 16), AF.Sign, bias=-65535.5)
-        mm(v("P4", 0, 16), v("ONE"), v("SG"), True, True)
-        mm(n("P2", H4, A, slice(0, 6)), v("IDP"), v("WI"), True, False)
-        mm(v("P3", 0, 256), v("IDH"), v("DI"), True, False)
         act(v("JK"), v("P4", 0, 16), scale=0.25, bias=198655.75 / 16, acc=v("BC"))
+        for a, b, key in HALVES: tt(v("AU", a // 16, b // 16), v("SL", a + 15, b, 16), v("D15", a // 16, b // 16), OP.add)
+        mm(v("P3", 0, 256), v("IDH"), v("DI"), True, False)
         act(v("NI", 0, 1), v("BC"), scale=1.0 / 128, bias=-12.49609375)
-        act(v("ZC"), v("NI", 0, 1), scale=-128.0, bias=v("BC"))
         for q, (a, b, key) in zip("SV", HALVES): add(q, v("FB", a, b), ind(v("PW"), v("AU", a // 16, b // 16)), -OFF)
+        act(v("ZC"), v("NI", 0, 1), scale=-128.0, bias=v("BC"))
         act(v("ZH"), v(Q), scale=0.5, bias=v("ZC"))
         act(v(ZB), v("ZH"), bias=-OFF)
         remote("z", t, lambda h: v(Qn, 64 * h, 64 * h + 64), lambda h: v(ZB, 64 * h, 64 * h + 64))
-        if first: steps(1, 2)
-        equal(2)
         turn(n("TF"), v("FB"))
         dons, recs = [("", "TF", 0, 0, 6), ("N", "TF", 1, 0, 5)], [("", "TF", 6, 0, 6), ("N", "TF", 7, 0, 5)]
-        if first:
+        if first or not DEEP:
             unturn("P5", H4, [("", "TF", 3, 0, 1)])
-            late_consts(2)
             ts(v("AU"), n("P5", H4, A, 0), OFF, OP.add)
-            ts(v("FB"), ind(v("PW"), v("AU")), -OFF, OP.add)
+            for q, (a, b, key) in zip("SV", HALVES): add(q, v("FB", a, b), ind(v("PW"), v("AU", a // 16, b // 16)), -OFF)
             turn(n("TG"), v("FB"))
             unturn("P6", H4, [("", "TF", 3, 2, 2), ("", "TG", 3, 0, 2)])
             dons += [("", "TG", 3, 1, 2), ("N", "TG", 4, 1, 1)]
             recs += [("", "TG", 10, 2, 2), ("N", "TG", 10, 1, 2)]
-            late_consts(3)
         else: unturn("P6", H4, [("", "TF", 1, 0, 4)])
         unturn("P0", H4, dons)
         unturn("P5", H4, recs, False)
-        equal(3)
         ts(v("BLU"), n("P6", H4, A, H4), OFF, OP.add)
-        equal(16)
-        act(v("AU4"), n("P6", H4, A, 0), bias=OFF)
+        for a, b in ((512, 1024), (0, 512)):
+            tt(v("LW", a, b), ind(v("X", 0, 3072), v("BLU", a // 16, b // 16)), v(Q4, a, b), OP.is_lt)
+        act(v("AU4"), v("BLU", 0, 64, 4))
         act(v("R4"), ind(v("PW"), v("AU4")), bias=-OFF)
-        tt(v("LW"), ind(v("X", 0, 3072), v("BLU")), v(Q4), OP.is_lt)
-        if first:
-            for k in (2816, 2560): table("V", "W1", "PW", "P2L", k, k + 256)
-        else:
-            count(2, 3)
-            mm(n("P1", H4), v("IDH"), v("VR"), False, True)
-            act(v("CV"), n("P1", H4), bias=-OFF)
-        diag(n("P5", H4, A, 1), "UR", "R4", False)
         act(v("DE"), n("P0", H4, A, slice(0, 6)))
+        turn(n("TH"), v("R4"))
+        unturn("P5", H4, [("", "TH", 11, 1, 1)], True, False)
         act(v("DR"), n("P5", H4, A, slice(0, 6)))
-        act(v("OH"), ind(v("E16"), v("KU")))
-        if first: steps(3)
-        for r in range(16):
-            mm(n("P2", H4, A, slice(1, 5)), usl("U", r), v("LW", r, 1024, 16), False, r == 15)
-        act(v(Qn, 0, 64), v(ZB, 0, 64))
-        mm(v("P3", 0, 256), v("IDM4"), v("OH"), False, True)
-        if first: mm(v("P7", 0, 256), v("IDP"), v("PO"), True, False)
-        act(v("DM"), v("P3", 0, 256), bias=OFF)
-        if first: steps(4)
-        else:
-            scan(v("CW"), v("D0"), v("CV"), 0.0, OP.mult, OP.max)
-            tt(v("OFV"), v("CW", 15, 256, 16), v("DUV"), OP.min)
-        ts(v("G6"), n("P2", H4, A, slice(0, 6)), 7.5, OP.is_lt)
-        mm(n("P0", H4), v("ID4"), v("OH"), True, False)
-        for h in range(4):
-            mm(n("P2", H4, h), v("IDP"), v(Q, 64 * h, 64 * h + 64), h == 0, False)
-        scan(v("SH"), v("DE"), v("G6"), 0.0, OP.add, OP.mult)
-        scan(v("SR"), v("DR"), v("G6"), 0.0, OP.add, OP.mult)
-        ts(v("AU2"), v("SH", 5, 96, 6), OFF, OP.add)
-        for q, h in (("V", 2), ("S", 1), ("S", 3)): add(q, v(MW, 4 * h, 4 * h + 4), v("SR", 6 * h + 5, 96, 24), OFF)
-        ts(v("AR"), ind(v("IDW"), v("AU2")), -OFF, OP.add)
-        remote("w", t, lambda h: v(Vn, 4 + 4 * h, 8 + 4 * h), lambda h: v(MW, 4 * h, 4 * h + 4))
-        if not lastr: repeat([v(ZB, 0, 64)] + [v(Qn, 64 * h, 64 * h + 64) for h in range(1, 4)], "GGSS")
-        act(v("XA"), ind(v("X", 0, 3072), v("AU2")))
-        if not lastr: act(v("N1B"), ind(v("NXR", 0, 3072), v("AU2")))
-        ts(v(Vn, 4, 8) if lastr else v("VC", 16 * t + 16, 16 * t + 32, 4), v("SR", 5, 96, 24), OFF, OP.add)
-        mm(v("P7", 0, 256), v("IDH"), v("AR"), False, False)
-        mm(n("P0", H4), v("IDH"), v("AR"), False, True)
-        act(v("OHA"), n("P0", H4), bias=OFF - 4096.0)
-        if lastr:
+        aside()
+        for j, bw, bc in ((1, "P1", "P4"), (0, "P2", "P7")):
+            a, b, H2 = 128 * j, 128 * j + 128, slice(0, 2)
+            mm(n(bw, H2, A, slice(0, 6)), v("IDP"), n("WI", slice(8 * j, 8 * j + 8)), True, False)
+            for r in range(16):
+                mm(n(bw, H2, A, slice(1, 5)), usl("U", r), v("LW", 4 * a + r, 4 * b, 16), False, r == 15)
+            join(-16)
+            mm(v(bc, 0, 128), v("IDP"), v("PO", 0, 128), True, False)
+            ts(v("G6", 48 * j, 48 * j + 48), n(bw, H2, A, slice(0, 6)), 7.5, OP.is_lt)
             for h in range(4):
-                act(v("YQ", h, 256, 4), v(Qn, 64 * h, 64 * h + 64))
+                mm(n(bw, H2, h), v("IDP"), v(Q, 64 * h + 32 * j, 64 * h + 32 * j + 32), h == 0, False)
+            join(-4)
+            scan(v("SH", 48 * j, 48 * j + 48), v("DE", 48 * j, 48 * j + 48), v("G6", 48 * j, 48 * j + 48), 0.0, OP.add, OP.mult)
+            ts(v("AU2", 8 * j, 8 * j + 8), v("SH", 48 * j + 5, 48 * j + 48, 6), OFF, OP.add)
+            at_a = lambda win: ind(v(win, 0, 3072), v("AU2", 8 * j, 8 * j + 8))
+            add("SV"[j], v("AR", a, b), at_a("IDW"), -OFF)
+            mm(v(bc, 0, 128), v("IDH"), v("AR", a, b), False, False)
+            if not lastr: act(v("N1B", a, b), at_a("NXR"), scale=v("WA"))
+            act(v("XA", a, b), at_a("X"))
+            mm(n(bw, H2), v("IDP"), v("XA", a, b), False, True)
+            act(v("XS", a, b), n(bw, H2), scale=0.5, bias=0.25)
+            mm(n("P0", H2), v("ID4"), v("OH", a, b), True, False)
+            mm(n("P0", H2), v("IDH"), v("AR", a, b), False, True)
+            act(v("OHA", a, b), n("P0", H2), bias=OFF - 4096.0)
+            if lastr: places(t, j)
+            for p in range(8):
+                c, h = p // 4, p % 4
+                o, w, m, e = 64 * c, 16 * h + 16, 128 - 64 * c, 768 * j + 128 * p - 64 * c * h
+                ts(v("EA", e, e + m), v("AR", a + o, b), v("SH", 48 * j + 6 * p + 5, 48 * j + 6 * p + 6), OP.is_equal)
+                if c == 0: mm(v(bc, 64, 128), v("BB4"), v("EA", e + 64, e + m), False, False)
+                mm(v(bc, o, o + w), v("TR"), v("EA", e, e + w), False, p == 7)
+                if h < 3: mm(v(bc, o + w, o + 64), v("TRE"), v("EA", e + w, e + 64), False, False)
+                join(-(1 + (c == 0) + (h < 3)))
+            scan(v("CS", a, b), v("D0", a, b), v(bc, 0, 128), 0.0, OP.mult, OP.max)
+            tt(v("OFA", 8 * j, 8 * j + 8), v("CS", a + 15, b, 16), v("DUA", 8 * j, 8 * j + 8), OP.min)
+        cp(ind(v("X"), v("OFA", 8, 16)), v("XS", 128, 256))
+        scan(v("SR"), v("DR"), v("G6"), 0.0, OP.add, OP.mult)
+        ts(v(MW), v("SR", 5, 96, 6), OFF, OP.add)
+        remote("w", t, lambda h: v(Vn, 16 * h - 16, 16 * h), lambda h: v(MW))
+        if lastr:
+            dma(T.yu[:], v("ULF", 0, 1536))
+            for h in range(4):
+                gcp(v("YQ", h, 256, 4), v(Qn, 64 * h, 64 * h + 64))
             dma(T.yq[:], v("YQ"), "act")
-        e = 0
-        for p in range(16):
-            c, h = p // 4, p % 4
-            o, w = 64 * c, 16 * h + 16
-            ts(v("EA", e, e + 256 - o), v("AR", o, 256), v("SH", 6 * p + 5, 6 * p + 6), OP.is_equal)
-            if c < 3: mm(v("P7", o + 64, 256), v("BB4"), v("EA", e + 64, e + 256 - o), False, False)
-            mm(v("P7", o, o + w), v("TR"), v("EA", e, e + w), False, p == 15)
-            if h < 3: mm(v("P7", o + w, o + 64), v("TRE"), v("EA", e + w, e + 64), False, False)
-            e += 256 - o
-            if p == 1:
-                mm(n("P2", H4), v("IDP"), v("XA"), False, True)
-                act(v("XH"), n("P2", H4), scale=0.5, bias=1024.25)
-                act(v("XS"), v("XH"), bias=-1024.0)
-                if first:
-                    steps(5)
-                    for a in (3, 4, 10, 11): dma(rows("PW", a - 2), rows("W1", a))
-                if not lastr:
-                    diag(n("P1", 0, 0), "UA", "N1B")
-                    act(v("N1U"), n("P1", 0, 0))
-                    act(v("NNB"), ind(v("NXR", 0, 3072), v("N1U")))
-            if p == (4 if lastr else 15):
-                tt(ind(v("ULF"), VL if first else v("OFV")), v("DM"), v("OHA"), OP.max)
-                if lastr: dma(T.yu[:], v("ULF", 0, 1536))
-        scan(v("CS"), v("D0"), v("P7", 0, 256), 0.0, OP.mult, OP.max)
-        tt(v("OFA"), v("CS", 15, 256, 16), v("DUA"), OP.min)
-    run("X", "V")
+        if first and DEEP:
+            steps(*range(len(STEPS)))
+            for a in (3, 4, 10, 11): dma(rows("PW", a - 2), rows("W1", a))
+        if not lastr:
+            turn(n("TE"), v("N1B"))
+            unturn("P6", H4, [("", "TE", 6, 0, 1), ("", "TE", 7, 0, 1)])
+            act(v("N1U"), n("P6", H4, A, 0))
+            act(v("NNB"), ind(v("NXR", 0, 3072), v("N1U")))
+            cp(ind(v("NXR"), v("OFA", 8, 16)), v("NNB", 128, 256))
+            repeat([v(Qn if h else ZB, 64 * h, 64 * h + 64) for h in range(4)], ("QA", "QB")[1 - t % 2])
+    cp(ind(v("X"), v("OFA", 0, 8)), v("XS", 0, 128))
     dma(T.yx[:], v("X", 0, 3072))
-    act(v("YG"), ind(v("IDW"), v("VL%d" % NR, 4, 20)))
+    lay(NR, "S")
+    act(v("YG"), ind(v("IDW"), v("VC", 16 * NR, 16 * NR + 16)))
     for h in range(4):
         act(v("YR", h, 256, 4), v("YG", 64 * h, 64 * h + 64))
     dma(T.yv[:], rows("YR", 5, 0, 256), "act")

from concourse.bass import DstId, RemoteDMATransfer
from concourse.mybir import AluOpType, ActivationFunctionType

OP, AF = AluOpType, ActivationFunctionType
NR = 3
BIG = 131102.0
OFF = 1536.0
A = slice(None)
H4 = slice(0, 4)

START = {"V": "PW B1 B0 PI PW P16 G16 G15 U E16 NH TN NH TN PVL W1 NXL X1 DI TD X2",
         "S": "PW*3 B0N B1N C24 VC UC UM WA PO W1 X1 X2", "P": "P4<TN P3<TN",
         "G": "SHF IPI IP IN160 PW IV QD*6 IDM IDP PO*4 DB BB4*3 IDH WI*2 QJ*4 IDW*3 BHB BLB TR TRE D0 IDM4 ID4 I16 J16"}
QUICK = ()
DEEP = True
_V = "%sP3 P4 RI RI NF NF SL SL AU AU FB TF %sBLU LW LW G6 TH SH AU2 AR G6 EA SH EA AU2 SR EA*2 MW EA*4 CS %s"
_S = "C1 C1 DD SG JK NI FB ZC ZH ZB %sAU4 R4 DE OH DM %s"
_P = "%sP1<LW P3<OH P0<OH P2<LW P5<TH P4<AR P4<EA*8 P7<AR %sP7<EA*8"
_2 = ("AU FB TG ", "FB CV ") if not DEEP else ("", "CV ")
_W = ("TE EA*4 OFA EA*4 X CS NXR OFA", "N1B XA DR AR N1B XA XS N1U NNB XS OHA*2", "P6<TE*2 ")
CHAIN = [{"V": _V % ("W1 ", "AU FB TG ", _W[0]), "S": _S % ("FB ", _W[1]), "P": _P % ("", _W[2])},
         {"V": _V % ("EW*16 ", _2[0], _W[0]), "S": _S % (_2[1], _W[1]), "P": _P % ("P6<CV ", _W[2])},
         {"V": _V % ("EW*16 ", _2[0], "ULF EA ULF OFA EA*7 X CS OFA X"), "S": _S % (_2[1], "XA DR OHA AR OHA XA XS XS"),
          "P": _P % ("P6<CV ", "")}]
TESTS = {"V": "N0 X0 U1 U0 n1 y8-11 W i j y11-13 l0 l1 l2 l3 d0 r0 a0 a1 a2 a3 b0 b1 b2 b3",
         "S": "n0 y0-8 n2 y13-24 v g23 x0-24 g45 s2 s3 g67 s4 s5 s6 s7 c k",
         "P": "T0 T1 T2 J q2 q3 o D q4 q5 q6 m0 h2 Z0 h3 A0 p q7 A1 A2 h4 Z1 A3 h5 B0 h6 B1 Z2 h7 B2 Z3 C B3"}
FIRST = {"V": "l0 l1 l2 l3 d0 a0 L a1 a2 a3 b0 b1 b2 b3",
         "S": "g1 g2 s1 t0 g3 M g5 g4 s2 g7 s3 g6 s4 s5 s6 s7 c k",
         "P": "o D q1 q4 q2 h1 q3 h2 K q6 A0 Z0 A1 p h3 A2 q5 q7 h4 A3 h5 Z1 h6 B0 h7 B1 Z2 Z3 B2 C B3"}
SHARE = {"W1": 1536, "X1": 1536, "X2": 256}
WALK = 320
STEPS = (512,) + (128,) * 20
COST = dict(cycle=0.95, pe=0.48, gather=1.55, scatter=3.5, act=65, hop=120, dma=700, row=45, rate=18.0, issue=300, first=1500,
            remote=600, far=55, scale=100)
COSTS = [COST, dict(COST, cycle=0.9, gather=1.15, scatter=2.2, pe=0.55, hop=150, dma=1200, remote=900, scale=90),
         dict(COST, cycle=1.1, gather=1.95, scatter=5.0, hop=90, row=25, rate=30.0, far=30, first=800, scale=130)]
PASSES, TRIES, REACH, DEPTH, LEAN = 2, 4000, 40, 3, 0.2

SCRATCH = {}


def _buf(dtype, **names):
    for k, n in names.items():
        SCRATCH[k] = ("sbuf", [128] + (list(n) if isinstance(n, tuple) else [n]), dtype)


_buf("bfloat16", X=3328, X1=3072, X2=3072, NXR=3328, BHB=192, BLB=192, QA=1024, QB=1024, QD=(16, 4, 16), DF=1024,
     AB=4096, L1=4096, L2=4096, LW=1024, XG=4096, EA=1536, E16=16, SG=16, G6=96, WI=(16, 6), EW=(4, 4, 2, 4, 16))
_buf("int32", ULI=1536, PW=3072, W1=3072, NXN=192, PVN=192, P2N=192, IDW=3072, BHI=192, BLI=192, KI=16, RM=16, XS=256)
_buf("uint16", NXL=192, PVL=192, P2L=192, DL=256, BLU=64, VC=64)
_buf("float16", N1B=256, DI=256, FB=256, R4=256, XH=256, ZH=256, NH=384, TN=384, NI=8, VH=16, VR=256, AR=256, IDH=128,
     TD=(4, 2, 2, 16), TE=(4, 2, 2, 16), TH=(4, 2, 2, 16), TF=(4, 2, 2, 16), TG=(4, 2, 2, 16))
_buf("float32", ULF=1792, IN160=160, SHF=160, IG16=128, DE=96, DR=96, SH=96, SR=96)
for _t in range(NR + 1):
    SCRATCH["QJ%d" % _t] = ("sbuf", [128, 256], "bfloat16")
    SCRATCH["VL%d" % _t] = ("sbuf", [128, 48], "uint16")
    if _t < NR:
        SCRATCH["ZB%d" % _t] = ("sbuf", [128, 256], "bfloat16")
        SCRATCH["MW%d" % _t] = ("sbuf", [128, 16], "uint16")
for _k in range(8):
    SCRATCH["P%d" % _k] = ("psum", [128, 512] if _k in (3, 4, 7) else [128, 8, 4, 16], "float32")
_PACK, _WIDTH = {}, {}
for _w, _names, _dt, _n, _u in (
        ("sm", "IP P16 G16 G15 C24 WA W11 T1 T2 BC ZC", "float32", 8, 1),
        ("ci", "IPI PI", "int32", 8, 1),
        ("lu", "KU AU AU2 AU4 OFA OFV N1U", "uint16", 16, 16),
        ("lf", "DUA DUV I16 J16 IV VF D15 JK", "float32", 16, 16),
        ("mat", "U UM UC UA", "bfloat16", 144, 144),
        ("mh", "UR B0 B1 B0N B1N", "float16", 160, 160),
        ("sq", "BB4 TR TRE ONE CB C15 IDP IDM ID4 IDM4", "bfloat16", 128, 128),
        ("ff", "DB D0 K1 K0 DD SL RI CS DM OHA YG YR", "float32", 256, 256),
        ("bb", "K16 MK QM NNB ON MON PO C1 XA YQ OH NF CV", "bfloat16", 256, 256)):
    for _j, _nm in enumerate(_names.split()):
        _PACK[_nm] = (_w, _j * _n)
        _WIDTH[_nm] = _u
    SCRATCH[_w] = ("sbuf", [128, _n * len(_names.split())], _dt)

NDMA = 30
SEMAPHORES = ["qV", "qS", "qP", "qG", "sent"] + ["d%d" % _k for _k in range(NDMA)]
for _t in range(NR):
    SEMAPHORES += ["z%d" % _t, "w%d" % _t]
PLAN = []


def shift(t, h):
    return 1 + (t + h - 1) % 7


def weave(lists, needs, run):
    todo = {q: x.split() for q, x in lists.items()}
    every = [x for q in todo for x in todo[q]]
    done = set()
    while any(todo.values()):
        q = next(q for q in todo if todo[q] and all(y in done for y in every if needs(todo[q][0], y)))
        run(todo[q][0], q)
        done.add(todo[q].pop(0))


def is_bank(nm):
    return nm[0] == "P" and nm[1:].isdigit()


def apart(x, y):
    return (x[2] <= y[1] or y[2] <= x[1] or x[4] is not None and y[4] is not None and x[4] != y[4]
            or x[3] == y[3] > 1 and (x[1] - y[1]) % x[3] != 0)


def before(calls):
    log, bank, pred = {}, {}, []
    for k, (q, _t, lead, w, r, flags, _g, _n) in enumerate(calls):
        need = {}
        for keys, wr in ((w, True), (r, False)):
            for x in keys:
                nm = x[0]
                if is_bank(nm):
                    B = bank.setdefault(nm, {"start": None, "mid": [], "other": None, "wrote": None})
                    if q == "P":
                        ps = [B["start"], B["other"]] + (B["mid"] if flags[0] or flags[1] else [])
                        if flags[0]: B["start"], B["mid"] = k, []
                        else: B["mid"].append(k)
                    else:
                        ps = [B["start"], B["other"], B["wrote"]] + B["mid"]
                    for j in ps:
                        if j is not None and j != k:
                            free = calls[j][0] == q and (q == "P" or wr or j != B["wrote"])
                            need[j] = max(need.get(j, 0), 0 if free else 1)
                    if q != "P":
                        B["other"] = k
                        if any(y[0] == nm for y in w) and (not wr or all(y[0] != nm for y in r)): B["wrote"] = k
                    continue
                L = log.setdefault(nm, [])
                for y, wrote, j in L:
                    if j != k and (wrote or wr) and not apart(x, y): need[j] = 0 if calls[j][0] == q == "P" or x[0][0] == "_" else 1
                if wr and x[3] == 1 and x[4] is None: L[:] = [e for e in L if not (x[1] <= e[0][1] and e[0][2] <= x[2])]
                L.append((x, wr, k))
        pred.append(need)
    return pred


def named(calls):
    pairs = []
    for q in "VSPG":
        was = None
        for t in range(-1, NR * (q != "G")):
            left = [k for k, c in enumerate(calls) if c[0] == q and c[7][0] == t]
            for x in START[q].split() if t < 0 else (
                    [y + "*9" for y in (TESTS if t else FIRST)[q].split()[:5 * (t > 0) if q == "P" else None]] + CHAIN[t][q].split()):
                x, _s, m = x.partition("*")
                for k in [k for k in left if calls[k][7][1] == x][:int(m or 1)]:
                    if was is not None: pairs.append((was, k))
                    left.remove(k)
                    was = k
    return pairs


def place(calls, pred, seq, gaps=True):
    start, end, busy = {}, {}, {}
    for k in seq:
        q, d = calls[k][0], calls[k][1]
        t = max([end[j] + x for j, x in pred[k]], default=calls[k][2])
        B = busy.setdefault(q, [])
        i = len(B)
        if gaps:
            while i and B[i - 1][1] > t: i -= 1
            while i < len(B) and B[i][0] < t + d:
                t = max(t, B[i][1]); i += 1
        elif B: t = max(t, B[-1][1])
        B.insert(i, (t, t + d))
        start[k], end[k] = t, t + d
    return start, end


def replay(each, pred, seq):
    end, cause, last = [0.0] * len(each), [None] * len(each), {}
    for k in seq:
        q, d, t = each[k]
        why = last.get(q)
        if why is not None and end[why] > t: t = end[why]
        for j, x in pred[k]:
            if end[j] + x > t: t, why = end[j] + x, j
        end[k], cause[k], last[q] = t + d, why, k
    return end, cause


def arrange(calls):
    needs = before(calls)
    preds = [[[(j, d * C["hop"] + calls[k][2][m]) for j, d in need.items()] for k, need in enumerate(needs)] for m, C in enumerate(COSTS)]
    each = [[(c[0], c[1][m], c[2][m]) for c in calls] for m in range(len(COSTS))]

    def after(pred):
        succ = [[] for _ in calls]
        for k, ps in enumerate(pred):
            for j, x in ps: succ[j].append((k, x))
        return succ

    pred = [list(x) for x in preds[0]]
    for j, k in named(calls): pred[k].append((j, 0))
    succ, seq, done = after(pred), [], set()
    while len(seq) < len(calls):
        seq.append(next(k for k in range(len(calls)) if k not in done and all(j in done for j, _x in pred[k])))
        done.add(seq[-1])
    back = [c[:2] + (0,) for c in each[0]]
    start, end = place(each[0], pred, seq, False)
    for _ in range(PASSES):
        late = place(back, succ, sorted(start, key=lambda k: (-end[k], -start[k])))[1]
        start, end = place(each[0], pred, sorted(start, key=lambda k: (-late[k], start[k])))
    seq = sorted(start, key=lambda k: (start[k] - each[0][k][2], k))
    pred = preds[0]
    succ = after(pred)

    def worth(s):
        runs = [replay(e, p, s) for e, p in zip(each, preds)]
        return sum((max(x[0]) + LEAN * sum(x[0]) / len(s)) / C["scale"] for x, C in zip(runs, COSTS)), runs

    def moved(s, a, b, links):
        along, want = [], {s[b]}
        for i in range(b, a - 1, -1):
            if s[i] in want:
                along.append(s[i])
                want.update(j for j, _x in links[s[i]])
        return None if along[-1] == s[a] else s[:a] + along[::-1] + [k for k in s[a:b + 1] if k not in want] + s[b + 1:]

    best, runs = worth(seq)
    tries, better = 0, True
    while better and tries < TRIES:
        better = False
        for m in range(len(COSTS)):
            end, cause = runs[m]
            k, links = max(seq, key=lambda j: end[j]), []
            while cause[k] is not None:
                if calls[cause[k]][0] == calls[k][0] and all(j != cause[k] for j, _x in pred[k]): links.append((cause[k], k))
                k = cause[k]
            for j, k in links:
                a, b = seq.index(j), seq.index(k)
                if a > b: continue
                same = [i for i in range(max(0, a - REACH), min(len(seq), b + REACH)) if calls[seq[i]][0] == calls[k][0]]
                rev, z = seq[::-1], len(seq) - 1
                for s in ([moved(seq, i, b, pred) for i in same[::-1] if i <= a][:DEPTH]
                          + [(moved(rev, z - i, z - a, succ) or [])[::-1] for i in same if i >= b][:DEPTH]):
                    if not s: continue
                    tries += 1
                    w, r = worth(s)
                    if w < best - 1e-9:
                        best, runs, seq, better = w, r, s, True
                        break
    return seq


def rank_program(g, core, T, topo):
    me = T.rank_of(core)
    if me is None:
        return
    N = len(T.cores)
    ENG = {"V": g.vector, "S": g.scalar, "P": g.tensor, "G": g, "sync": g.sync, "act": g.scalar}
    cnt = {"V": 0, "S": 0, "P": 0, "G": 0}
    know = {"V": {}, "S": {}, "P": {}, "G": {}, "sync": {}}
    snap = {}
    unit = {"V": 1, "S": 1, "P": 1, "G": 1}
    total = {}
    log = {}
    nd = [0]
    sent = [0]

    def v(name, lo=0, hi=None, step=1):
        w, b = _PACK.get(name, (name, 0))
        if hi is None: hi = _WIDTH[name] if name in _PACK else T[w].shape[1]
        lo, hi = lo + b, hi + b
        ap = T[w][:, lo:hi:step] if step != 1 else T[w][:, lo:hi]
        return (ap, [(w, lo, hi, step, None)], [], len(range(lo, hi, step)), name.rstrip("012") if name[:2] in ("QJ", "ZB", "MW") else name)

    def n(name, *ix, key=None):
        f = ix[0] if ix else A
        lo, hi = (f, f + 1) if isinstance(f, int) else (f.start or 0, f.stop or 64)
        m = 1
        for k, d in enumerate(SCRATCH[name][1][1:]):
            if k >= len(ix) or isinstance(ix[k], slice): m *= len(range(d)[ix[k] if k < len(ix) else A])
        return (T[name][(A,) + ix], [(name,) + (key or (lo, hi, 1)) + (None,)], [], m, name)

    def ew(h, c, d, hs=A):
        return n("EW", h, c, d, hs, key=(4 * h + c, 4 * h + c + 1, 1) if isinstance(c, int) else (4 * h, 4 * h + 4, 1))

    def rows(name, f, lo=0, hi=3072):
        w, b = _PACK.get(name, (name, 0))
        return (T[w][f:128:16, lo + b:hi + b], [(w, lo + b, hi + b, 1, f)], [], hi - lo, name)

    def ind(win, off):
        return (win[0].indirect(off[0]), win[1], off[1], 16 * off[3], win[4])

    def width(x): return 4 if SCRATCH[x[1][0][0]][2] in ("float32", "int32") else 2

    def order(q, w, r):
        need = {}
        def dep(tok):
            if tok[0] == q == "P": return
            if know[q].get(tok[0], 0) < tok[1]: need[tok[0]] = max(need.get(tok[0], 0), tok[1])
        for keys, wr in ((w, True), (r, False)):
            for x in keys:
                for y, kind, tok in log.get(x[0], []):
                    if is_bank(x[0]):
                        if tok[0] != q or (kind == "w" and not wr): dep(tok)
                    elif (kind == "w" or wr) and not apart(x, y): dep(tok)
        for a in sorted(need):
            if any(b != a and snap.get((b, need[b]), {}).get(a, 0) >= need[a] for b in need): continue
            ENG[q].wait_ge(T.sem["q" + a if a in cnt else a], need[a] * unit[a])
        for a in need:
            for b, m in snap.get((a, need[a]), {}).items(): know[q][b] = max(know[q].get(b, 0), m)
            know[q][a] = max(know[q].get(a, 0), need[a])

    def note(tok, w, r):
        for keys, kind in ((w, "w"), (r, "r")):
            for x in keys:
                L = log.setdefault(x[0], [])
                if is_bank(x[0]):
                    L[:] = ([e for e in L if e[1] == "w"][-1:] if kind == "r" else []) + [(x, kind, tok)]
                else:
                    if kind == "w" and x[3] == 1 and x[4] is None: L[:] = [e for e in L if not (x[1] <= e[0][1] and e[0][2] <= x[2])]
                    L.append((x, kind, tok))

    none, at = [0] * len(COSTS), [0, None]
    calls = []

    def emit(q, fn, outs, ins, twice=False, flags=None, gp=None):
        w, r = [], []
        for o in outs: w += o[1]; r += o[2]
        for i in ins: r += i[1] + i[2]
        m = outs[0][3]

        def time(C):
            if q == "P": return C["pe"] * max(64, m)
            if q == "G": return gp + 2 * C["cycle"] * m
            if outs[0][2]: return 50 + C["scatter"] * C["cycle"] * m
            if ins and ins[0][2]: return {"V": 50, "S": 65}[q] + C["gather"] * C["cycle"] * m
            if q == "S": return C["act"] + C["cycle"] * m
            half = all(width(x) == 2 for x in outs + ins if x[3] == m)
            both = twice and not any(is_bank(x[1][0][0]) for x in ins)
            return C["cycle"] * max(64, m * (0.5 if half else 1) * (2 if both else 1))

        def go():
            order(q, w, r)
            cnt[q] += 1
            fn().then_inc(T.sem["q" + q], 1)
            now = dict(know[q]); now[q] = cnt[q]
            snap[(q, cnt[q])] = now
            note((q, cnt[q]), w, r)
        name = at[1] or (outs[0][4] + "<" + ins[1][4] if q == "P" else outs[0][4])
        calls.append((q, [time(C) for C in COSTS], none, w, r, flags, go, (at[0], name)))

    def join(k):
        part = calls[k:]
        calls[k:] = [("P", [sum(x) for x in zip(*[c[1] for c in part])], none, [x for c in part for x in c[3]],
                      [x for c in part for x in c[4]], (part[0][5][0], part[-1][5][1]), lambda: [c[6]() for c in part], part[0][7])]

    def dma(out, in_, q="sync"):
        qk = {"sync": "sync", "act": "S"}[q]
        w = out[1] if isinstance(out, tuple) else []
        r = in_[1] if isinstance(in_, tuple) else []
        sides = [x for x in (out, in_) if isinstance(x, tuple)]
        full = [x for x in sides if x[1][0][4] is None]
        x = (full or sides)[0]
        time = [8 * (C["row"] + x[3] * width(x) / C["rate"]) if full else C["row"] + x[3] * width(x) / 2 / C["rate"] for C in COSTS]

        def go():
            order(qk, w, r)
            nm = "d%d" % nd[0]; nd[0] += 1
            o = out[0] if isinstance(out, tuple) else out
            i = in_[0] if isinstance(in_, tuple) else in_
            ENG[q].dma_start(o, i).then_inc(T.sem[nm], 16)
            unit[nm] = 16; total[nm] = 1
            snap[(nm, 1)] = dict(know[qk])
            note((nm, 1), w, r)
        tok = [("_%d" % len(calls), 0, 1, 1, None)] if q == "act" else []
        if tok: calls.append(("S", [C["act"] for C in COSTS], none, tok + w, r, None, go, (at[0], "dma")))
        calls.append(("D", time, [C["dma"] for C in COSTS], w, r + tok, None, None if tok else go, (at[0], "dma")))

    def engines(src, dst, h):
        return topo.engines(src, dst)[{1: slice(0, 4), 2: slice(4, 8), 3: slice(0, 8)}[h]]

    def remote(kind, t, dst, src):
        nm = "%s%d" % (kind, t)
        src, dst = [None] + [src(h) for h in range(1, 4)], [None] + [dst(h) for h in range(1, 4)]
        w, r = [k for x in dst[1:] for k in x[1]], [k for x in src[1:] for k in x[1]]

        def go():
            order("G", [], r)
            for hs in ((1, 2), (3,)):
                trs = []
                for h in hs:
                    d = T.cores[(me + shift(t, h)) % N]
                    rid, pid, _s = topo.addr(d)
                    es = engines(core, d, h)
                    trs.append(RemoteDMATransfer(dst_ids=[DstId(rid=rid, pnc=pid)], dma_engine_mask=sum(1 << e for e in es),
                                                 remote_sem=T.sem[nm], src=src[h][0], dst=dst[h][0]))
                    sent[0] += len(es)
                g.remote_dma_fused(trs, local_sem=T.sem.sent)
            unit[nm] = sum(len(engines(T.cores[(me - shift(t, h)) % N], core, h)) for h in range(1, 4))
            total[nm] = 1
            snap[(nm, 1)] = {}
            note((nm, 1), w, [])
        tok = [("_" + nm, 0, 1, 1, None)]
        calls.append(("G", [2 * C["issue"] + C["first"] * (nm == "z0") for C in COSTS], none, tok + w, r, None, go, (t, nm)))
        calls.append(("R", [48 * (C["far"] + src[1][3] * 2 / C["rate"]) for C in COSTS], [C["remote"] for C in COSTS], w, tok, None,
                      None, (t, nm)))

    def cp(o, i): emit("V", lambda: g.vector.tensor_copy(o[0], i[0]), [o], [i])
    def tt(o, a, b, op): emit("V", lambda: g.vector.tensor_tensor(o[0], a[0], b[0], op), [o], [a, b], True)
    def ts(o, a, s1, op0, s2=None, op1=None):
        ex = [s for s in (s1, s2) if isinstance(s, tuple)]
        x1 = s1[0] if isinstance(s1, tuple) else s1
        x2 = s2[0] if isinstance(s2, tuple) else s2
        if op1 is None: emit("V", lambda: g.vector.tensor_scalar(o[0], a[0], x1, None, op0), [o], [a] + ex)
        else: emit("V", lambda: g.vector.tensor_scalar(o[0], a[0], x1, x2, op0, op1), [o], [a] + ex)
    def scan(o, d0, d1, init, op0, op1): emit("V", lambda: g.vector.tensor_tensor_scan(o[0], d0[0], d1[0], init, op0, op1), [o], [d0, d1])
    def turn(o, i): emit("V", lambda: g.vector.transpose(o[0], i[0]), [o], [i])
    def fill(o, c): emit("V", lambda: g.vector.memset(o[0], c), [o], [])
    def act(o, i, f=AF.Identity, bias=0.0, scale=1.0, acc=None):
        ex = [s for s in (bias, scale) if isinstance(s, tuple)]
        b = bias[0] if isinstance(bias, tuple) else bias
        s = scale[0] if isinstance(scale, tuple) else scale
        if acc is None: emit("S", lambda: g.scalar.activation(o[0], i[0], f, bias=b, scale=s), [o], [i] + ex)
        else: emit("S", lambda: g.scalar.activation(o[0], i[0], f, bias=b, scale=s, accum_out=acc[0]), [o, acc], [i] + ex)
    def mm(o, l, r, start, stop): emit("P", lambda: g.tensor.matmul(o[0], l[0], r[0], start, stop), [o], [l, r], flags=(start, stop))
    def iota(o, pat, base=0, cm=0, small=True):
        if small: emit("G", lambda: g.iota(o[0], pat, base, cm, allow_small_or_imprecise_dtypes=True), [o], [], gp=130)
        else: emit("G", lambda: g.iota(o[0], pat, base, cm), [o], [], gp=130)
    def keep(o, i, pat, op, base, cm, other=0.0): emit("G", lambda: g.affine_select(o[0], i[0], pat, op, other, base, cm), [o], [i], gp=170)
    def gcp(o, i): keep(o, i, [[0, o[3]]], OP.is_ge, 0, 0)
    def usl(name, r): return v(name, 15 - r, 143 - r)
    def sel(f, e, neg=""): return v("B%d%s" % (f, neg), 16 + 16 * (f - e), 144 + 16 * (f - e))

    def add(q, o, i, c):
        if q == "V": ts(o, i, c, OP.add)
        else: act(o, i, bias=c)

    def table(q, out, win, lst, lo, hi):
        (cp if q == "V" else act)(v(out, lo, hi), ind(v(win, 0, 3072), v(lst, lo // 16, hi // 16)))

    def diag(out, mat, src, start=True):
        for r in range(16):
            mm(out, usl(mat, r), v(src, r, 256, 16), start and r == 0, r == 15)
        join(-16)

    def unturn(bank, part, terms, stop=True, start=True):
        each = [(f, e, x) for x in terms for f in range(2) for e in range(2)]
        for k, (f, e, (neg, src, a, b, m)) in enumerate(each):
            mm(n(bank, part, slice(f, 4, 2), slice(b, b + m)), sel(f, e, neg), n(src, A, A, e, slice(a, a + m)),
               start and k == 0, stop and k == len(each) - 1)
            if k % 4 == 3: join(-4)

    def to_list(nat, bank, o=0):
        if nat:
            ts(v("NH", o, o + 192), v(nat), -OFF, OP.add)
            turn(v("TN", o, o + 192), v("NH", o, o + 192))
        for m in range(12 if bank else 0):
            for e in range(2):
                b = o + 32 * (m // 2) + 16 * e
                mm(v(bank, m, 192, 12), sel(m % 2, e), v("TN", b, b + 16), e == 0, e == 1)
        if bank: join(-24)

    def repeat(classes, out):
        for h in range(4): gcp(n("QD", slice(h, 16, 4), 0, key=(h, 16, 4)), classes[h])
        for k in (1, 2): gcp(n("QD", A, slice(k, 2 * k), key=(16 * k, 32 * k, 1)), n("QD", A, slice(0, k), key=(0, 16 * k, 1)))
        (cp if at[0] in QUICK else dma)(v(out), n("QD"))

    at[0] = -1
    dma(v("PVN"), T.pv[:])
    dma(v("NXN"), T.nx[:], "act")
    dma(v("QM"), T.mv[:])
    fill(v("PW", 0, 512), 1536)
    iota(v("SHF"), [[32, 5], [1016, 2], [1, 16]], -16, -1)
    ts(v("B1"), v("SHF"), 0.0, OP.is_equal)
    ts(v("B0"), v("SHF"), 1000.0, OP.is_equal)
    fill(v("PW", 512, 1024), 1536)
    iota(v("PW", 2688, 3072), [[0, 384]], 1536, 0, False)
    iota(v("IPI"), [[1, 1]], 0, 1, False)
    iota(v("IP"), [[1, 1]], 0, 1)
    iota(v("IN160"), [[1, 160]])
    iota(v("IV"), [[384, 4], [6, 4]])
    for a, b in ((1024, 1536), (1536, 2048), (2048, 2688)): act(v("PW", a, b), v("PW", 0, b - a))
    dma(rows("PW", 4), T.pv[:])
    dma(rows("PW", 11), T.rc[:], "act")
    dma(v("X", 0, 3072), T.xd[:])
    dma(v("ULI"), T.ul[:])

    def eye(name, c): keep(v(name), v("C15"), [[-1, 128]], OP.not_equal, 0, 1, c)
    to_list("PVN", "P4", 192)
    to_list("NXN", "P3")
    fill(v("C15"), 0.0)
    fill(v("ON"), 1.0)
    fill(v("MON"), -1.0)
    fill(v("CB"), -61440.0)
    ts(v("PI"), v("IPI"), 15, OP.bitwise_and)
    cp(v("P16"), v("PI"))
    tt(v("G16"), v("IP"), v("P16"), OP.subtract)
    ts(v("G15"), v("G16"), 15.0, OP.add)
    ts(v("U"), v("IN160", 0, 144), v("G15"), OP.is_equal)
    ts(v("E16"), v("IN160", 0, 16), v("P16"), OP.is_equal)
    act(v("C24"), v("P16"), scale=24.0)
    act(v("VC", 0, 16), v("IV"), bias=v("C24"))
    act(v("B0N"), v("B0"), scale=-1.0)
    act(v("B1N"), v("B1"), scale=-1.0)
    act(v("UC"), v("U"), scale=1048576.0)
    act(v("UM"), v("U"), scale=-1.0)
    act(v("WA"), v("E16", 7, 8), scale=64.0, bias=v("E16", 6, 7))
    act(v("UA"), v("U"), scale=v("WA"))
    act(v("PO", 0, 16), v("E16"), scale=4195840.0, bias=-4194304.0)
    iota(v("I16"), [[16, 16]], 1536)
    iota(v("J16"), [[16, 16]], 3072)
    act(v("DUV"), v("I16"), bias=v("P16"))
    act(v("DUA"), v("J16"), bias=v("P16"))
    ts(v("PVL"), v("P4", 0, 192), OFF, OP.add)
    repeat([v("QM", h, 256, 4) for h in range(4)], "QA")
    for out, win, lst in (("W1", "PW", "PVL"), ("X1", "X", "NXL"), ("X2", "X1", "NXL")):
        table("V", out, win, lst, 0, SHARE[out])
        table("S", out, win, lst, SHARE[out], 3072)
        if out == "W1": ts(v("NXL"), v("P3", 0, 192), OFF, OP.add)
    if DEEP: dma(v("P2N"), rows("W1", 4))
    dma(rows("PW", 3), rows("W1", 4))
    dma(rows("PW", 10), rows("W1", 11))
    for name, c in (("IDM", -1.0), ("IDP", 1.0), ("IDH", 1.0), ("IDM4", -4096.0), ("ID4", 4096.0)): eye(name, c)
    iota(v("BB4"), [[0, 128]], 4096)
    keep(v("BB4"), v("BB4"), [[-16, 8], [0, 16]], OP.is_ge, 0, 1)
    keep(v("BB4"), v("BB4"), [[16, 8], [0, 16]], OP.is_ge, 15, -1)
    keep(v("TR"), v("BB4"), [[1, 128]], OP.is_gt, 0, -1)
    keep(v("TRE"), v("BB4"), [[1, 128]], OP.is_ge, 0, -1)
    keep(v("D0"), v("ON"), [[0, 16], [1, 16]], OP.is_gt, 0, 0)
    keep(v("DB"), v("MON"), [[0, 16], [1, 16]], OP.is_gt, 0, 0, 524288.0)
    iota(n("WI"), [[0, 16], [-16, 6]], 16)
    keep(n("WI"), n("WI"), [[0, 16], [-1, 6]], OP.is_ge, 0, 0)
    for k in (16, 32, 64, 128): gcp(v("PO", k, 2 * k), v("PO", 0, k))
    for h in range(4):
        gcp(v("QJ0", 64 * h, 64 * h + 64), v("QM", h, 256, 4))
    ts(v("DI"), ind(v("ULI"), v("VC", 0, 16)), -OFF, OP.add)
    turn(n("TD"), v("DI"))
    unturn("P5", H4, [("", "TD", 0, 0, 16)])
    for k in range(3):
        iota(v("IDW", 1024 * k, 1024 * k + 1024), [[1, 1024]], 1024 * k, 0, False)
    dma(rows("PW", 5), rows("IDW", 5))
    dma(v("NXR", 0, 3072), v("X", 0, 3072))
    for k in range(3): gcp(v("ULF", 512 * k, 512 * k + 512), v("ULI", 512 * k, 512 * k + 512))
    ts(v("BHI"), v("NXN"), 6, OP.arith_shift_right)
    ts(v("BLI"), v("NXN"), 63, OP.bitwise_and)
    gcp(v("BHB"), v("BHI"))
    gcp(v("BLB"), v("BLI"))
    dma(rows("NXR", 7), v("BHB"))
    dma(rows("NXR", 6), v("BLB"))

    def steps(*ks):
        for k in ks:
            table("SV"[k < 5], "W1", "PW", "P2L", sum(STEPS[:k]), sum(STEPS[:k + 1]))

    def sums(bank, mat, src, q, last):
        for r in range(16):
            mm(n(bank, H4, A, slice(4 * q, 4 * q + 4)), usl(mat, r), v(src, 1024 * q + r, 1024 * q + 1024, 16), False, last and r == 15)
            if r % 8 == 7: join(-8)

    EIGHTH = ("P3", "P4", "P7", "P5", "P6")
    HALVES = ((0, 128, "P3"), (128, 256, "P4"))

    def places(t, j):
        a, b = HALVES[j][:2]
        if t: tt(ind(v("ULF"), v("OFV", a // 16, b // 16)), v("DM", a, b), v("OHA", a, b), OP.max)
        elif j == 0: tt(ind(v("ULF"), v("VC", 0, 16)), v("DM"), v("OHA"), OP.max)

    def lay(t, q):
        for h in range(4):
            at[1] = "W" if h and t < NR else None
            add(q if h else "S", v("VC", 16 * t + h, 16 * t + 16, 4) if t < NR else v("VC", 16 * t + 4 * h, 16 * t + 4 * h + 4),
                v("VL%d" % t, 17 * h - 16, 16 * h, 4) if h else v("MW%d" % (t - 1), 0, 16, 4), 0.0)

    for t in range(NR):
        Q, Qn, VL, Vn = "QJ%d" % t, "QJ%d" % (t + 1), v("VC", 16 * t, 16 * t + 16), "VL%d" % (t + 1)
        Q4, ZB, MW = ("QA", "QB")[t % 2], "ZB%d" % t, "MW%d" % t
        first, lastr = t == 0, t == NR - 1
        lists = FIRST if first else TESTS
        tens = lists["P"].split()
        m0 = 512 * min(int(y[1]) for y in lists["S"].split() if y[0] == "g")

        def test(x, out, q, op, m=1024):
            tt(v(out, 1024 * q, 1024 * q + m), ind(v(x, 0, 3072), v("DL", 64 * q, 64 * q + m // 16)), v(Q4, 0, m), op)

        def needs(x, y):
            k, j = x[0], int(x[1]) if x[1:2].isdigit() else 0
            if k in "xy":
                lo, hi = [int(u) for u in x[1:].split("-")]
                return y[0] == "y" if k == "x" else y[0] == "X" or y in ["n%d" % u for u in range(lo // 8, (hi + 7) // 8)]
            if y[0] in {"a": "yQ", "b": "xQ", "d": "XQ", "g": "X", "q": "Q", "c": "A", "k": "Z", "m": "o", "Z": "o", "A": "o", "B": "p",
                        "C": "pc", "i": "WU", "v": "W", "j": "i", "J": "j", "l": "J", "T": "N", "w": "v", "D": "j", "p": "D", "K": "L",
                        "M": "K"}.get(k, ""): return True
            if k == "h" and y[0] == "g": return x[1] in y
            return y in {"n": ["T%d" % j], "d": ["l0"], "g": ["l%d" % (j // 2)], "a": ["l%d" % j], "b": ["l%d" % j],
                         "t": ["d0"], "r": ["d0"], "m": ["d0"], "s": ["h%d" % j], "A": ["a%d" % j], "B": ["b%d" % j],
                         "q": ["s%d" % (j - 5)] + (["l0", "l1", "l2", "l3"] if j == 4 else ["n%d" % (7 - j)] + ["M"] * (j == 5)),
                         "h": ["q%d" % j], "Z": ["t%d" % j, "r%d" % j, "m%d" % j, "s%d" % (2 * j), "s%d" % (2 * j + 1)]}.get(k, [])

        def run(x, q):
            at[1] = x
            k, j = x[0], int(x[1]) if x[1:2].isdigit() else 0
            last = lambda kinds: x == [y for y in tens if y[0] in kinds][-1]
            bank = EIGHTH[(7 - j) % 5]
            if k in "XN":
                a, b = HALVES[j][:2]
                cp(ind(v({"X": "X", "N": "NXR"}[k]), v("OFA", a // 16, b // 16)), v({"X": "XS", "N": "NNB"}[k], a, b))
            if k == "U": places(t - 1, j)
            if k == "W": lay(t, q)
            if k == "i": add(q, v("DI"), ind(v("ULF", 0, 1536), VL), -OFF)
            if k == "L" and DEEP: to_list("P2N", None)
            if k == "K" and DEEP: to_list(None, "P7")
            if k == "M" and DEEP: add(q, v("P2L"), v("P7", 0, 192), OFF)
            if k == "j": turn(n("TD"), v("DI"))
            if k == "J": unturn("P5", H4, [("", "TD", 0, 0, 16)])
            if k == "l": add(q, v("DL", 64 * j, 64 * j + 64), n("P5", H4, A, slice(4 * j, 4 * j + 4)), OFF)
            if k == "T":
                for r in range(16):
                    mm(v(EIGHTH[j], 0, 64), usl("UA", r), v("NXR", 1024 * j + r, 1024 * j + 1024, 16), r == 0, r == 15)
                join(-16)
            if k == "n": add(q, v("NXL", 64 * j, 64 * j + 64), v(EIGHTH[j], 0, 64), 0.0)
            if k in "xy":
                lo, hi = [128 * int(u) for u in x[1:].split("-")]
                table(q, *(("X2", "X1") if k == "x" else ("X1", "X")), "NXL", lo, hi)
            if k == "v":
                act(v("VR"), ind(v("IDW"), VL))
                act(v("VF"), VL)
                gcp(v("VH", 0, 16), v("VF"))
            if k == "d": test("X", "DF", 0, OP.subtract, m0)
            if k == "t": act(v("AB", 0, m0), v("DF", 0, m0), AF.Abs)
            if k == "r": ts(v("AB", 0, m0), v("DF", 0, m0), 0.0, OP.max, 2.0, OP.mult)
            if k == "a": test("X1", "L1", j, OP.is_lt)
            if k == "b": test("X2", "L2", j, OP.is_lt)
            if k == "g":
                u = j + len(x) - 1
                act(v("XG", 512 * j, 512 * u), ind(v("X", 0, 3072), v("DL", 32 * j, 32 * u)))
            if k == "s": act(v("AB", 512 * j, 512 * j + 512), n(bank), AF.Abs)
            if k == "c": act(v("C1"), n("P1", H4), AF.Relu, scale=32.0)
            if k == "k":
                for a, b, key in HALVES: act(v(key, 0, 128), n("P0", slice(a // 64, b // 64)), scale=-16.0, bias=65536.0)
            if k == "o": mm(n("P0", H4), v("C15"), v("ON"), True, False)
            if k in "op": mm(n("P1" if k == "o" else "P2", H4), v("CB"), v("ON"), True, False)
            if k == "D": unturn("P2", slice(4, 8), [("N", "TD", 0, 0, 16), ("", "TD", 0, 1, 15)])
            if k == "w": equal(j)
            if k == "q": mm(n(bank), v("IDM"), v(Q4, 512 * (j % 2), 512 * (j % 2) + 512), True, False)
            if k == "h": mm(n(bank), v("IDP"), v("XG", 512 * j, 512 * j + 512), False, True)
            if k == "m": sums("P0", "UM", "DF", 0, False)
            if k == "Z": sums("P0", "U", "AB", j, last("Z"))
            if k == "A": sums("P1", "UC", "L1", j, last("A"))
            if k == "B": sums("P2", "UC", "L2", j, last("BC"))
            if k == "C": mm(n("P2", H4), v("IDP"), v("C1"), False, last("BC"))
            at[1] = None

        pairs = [] if first else [(h, c) for h in range(4) for c in range(4)]

        def equal(m):
            for h, c in pairs[:m]:
                ts(ew(h, c, slice(0, 2 - c % 2)), v("VR", 64 * c, 128 * (c // 2 + 1)), v("VF", 4 * c + h, 4 * c + h + 1), OP.is_equal)
            del pairs[:m]

        def count(*hs):
            for h in hs:
                if h == 0: mm(n("P1", H4), v("IDP"), v("PO"), True, False)
                mm(n("P1", H4, slice(0, h + 1)), v("TR"), ew(h, A, 0, slice(0, h + 1)), False, False)
                if h < 3: mm(n("P1", H4, slice(h + 1, 4)), v("TRE"), ew(h, A, 0, slice(h + 1, 4)), False, False)
                mm(n("P1", slice(1, 4, 2)), v("BB4"), ew(h, slice(0, 4, 2), 1), False, h == 3)

        def aside():
            act(v("RM"), v("RI", 15, 256, 16), bias=131087.0)
            ts(v("KI"), v("RM"), 15, OP.bitwise_and)
            act(v("KU"), v("KI"))
            act(v("OH"), ind(v("E16"), v("KU")))
            mm(v("P3", 0, 256), v("IDM4"), v("OH"), False, True)
            act(v("DM"), v("P3", 0, 256), bias=OFF)
            gcp(v(Qn, 0, 64), v(ZB, 0, 64))
            if not first:
                act(v("CV"), n("P1", H4), AF.Relu, bias=-OFF)
                mm(n("P6", 0, 0), v("IDH"), v("VH", 0, 16), True, False)
                diag(n("P6", 0, 0), "U", "CV", False)
                tt(v("OFV"), n("P6", 0, 0), v("DUV"), OP.min)

        at[0] = t
        weave(lists, needs, run)
        cp(v("D15"), v("DL", 195, 256, 4))
        equal(16)
        for a, b, key in HALVES: act(v("C1", a, b), n("P2", slice(a // 64, b // 64)), AF.Sign)
        act(v("DD"), n("P2", slice(4, 8)))
        for a, b, key in HALVES: tt(v(key, 0, 128), v(key, 0, 128), v("C1", a, b), OP.mult)
        for a, b, key in HALVES: scan(v("RI", a, b), v("DB", a, b), v(key, 0, 128), 1000000.0, OP.add, OP.min)
        if not first: count(0, 1, 2, 3)
        act(v("SG"), v("RI", 15, 256, 16), AF.Sign)
        for a, b, key in HALVES: tt(v("NF", a, b), v(key, 0, 128), v("RI", a, b), OP.not_equal)
        mm(v("P4", 0, 16), v("ON", 0, 128), v("SG"), True, True)
        for a, b, key in HALVES: scan(v("SL", a, b), v("DD", a, b), v("NF", a, b), 0.0, OP.add, OP.mult)
        act(v("JK"), v("P4", 0, 16), scale=0.25, bias=198655.75 / 16, acc=v("BC"))
        for a, b, key in HALVES: tt(v("AU", a // 16, b // 16), v("SL", a + 15, b, 16), v("D15", a // 16, b // 16), OP.add)
        mm(v("P3", 0, 256), v("IDH"), v("DI"), True, False)
        act(v("NI", 0, 1), v("BC"), scale=1.0 / 128, bias=-12.49609375)
        for q, (a, b, key) in zip("SV", HALVES): add(q, v("FB", a, b), ind(v("PW"), v("AU", a // 16, b // 16)), -OFF)
        act(v("ZC"), v("NI", 0, 1), scale=-128.0, bias=v("BC"))
        act(v("ZH"), v(Q), scale=0.5, bias=v("ZC"))
        act(v(ZB), v("ZH"), bias=-OFF)
        remote("z", t, lambda h: v(Qn, 64 * h, 64 * h + 64), lambda h: v(ZB, 64 * h, 64 * h + 64))
        turn(n("TF"), v("FB"))
        dons, recs = [("", "TF", 0, 0, 6), ("N", "TF", 1, 0, 5)], [("", "TF", 6, 0, 6), ("N", "TF", 7, 0, 5)]
        if first or not DEEP:
            unturn("P5", H4, [("", "TF", 3, 0, 1)])
            ts(v("AU"), n("P5", H4, A, 0), OFF, OP.add)
            for q, (a, b, key) in zip("SV", HALVES): add(q, v("FB", a, b), ind(v("PW"), v("AU", a // 16, b // 16)), -OFF)
            turn(n("TG"), v("FB"))
            unturn("P6", H4, [("", "TF", 3, 2, 2), ("", "TG", 3, 0, 2)])
            dons += [("", "TG", 3, 1, 2), ("N", "TG", 4, 1, 1)]
            recs += [("", "TG", 10, 2, 2), ("N", "TG", 10, 1, 2)]
        else: unturn("P6", H4, [("", "TF", 1, 0, 4)])
        unturn("P0", H4, dons)
        unturn("P5", H4, recs, False)
        ts(v("BLU"), n("P6", H4, A, H4), OFF, OP.add)
        for a, b in ((512, 1024), (0, 512)):
            tt(v("LW", a, b), ind(v("X", 0, 3072), v("BLU", a // 16, b // 16)), v(Q4, a, b), OP.is_lt)
        act(v("AU4"), v("BLU", 0, 64, 4))
        act(v("R4"), ind(v("PW"), v("AU4")), bias=-OFF)
        act(v("DE"), n("P0", H4, A, slice(0, 6)))
        turn(n("TH"), v("R4"))
        unturn("P5", H4, [("", "TH", 11, 1, 1)], True, False)
        act(v("DR"), n("P5", H4, A, slice(0, 6)))
        aside()
        for j, bw, bc in ((1, "P1", "P4"), (0, "P2", "P7")):
            a, b, H2 = 128 * j, 128 * j + 128, slice(0, 2)
            mm(n(bw, H2, A, slice(0, 6)), v("IDP"), n("WI", slice(8 * j, 8 * j + 8)), True, False)
            for r in range(16):
                mm(n(bw, H2, A, slice(1, 5)), usl("U", r), v("LW", 4 * a + r, 4 * b, 16), False, r == 15)
            join(-16)
            mm(v(bc, 0, 128), v("IDP"), v("PO", 0, 128), True, False)
            ts(v("G6", 48 * j, 48 * j + 48), n(bw, H2, A, slice(0, 6)), 7.5, OP.is_lt)
            for h in range(4):
                mm(n(bw, H2, h), v("IDP"), v(Q, 64 * h + 32 * j, 64 * h + 32 * j + 32), h == 0, False)
            join(-4)
            scan(v("SH", 48 * j, 48 * j + 48), v("DE", 48 * j, 48 * j + 48), v("G6", 48 * j, 48 * j + 48), 0.0, OP.add, OP.mult)
            ts(v("AU2", 8 * j, 8 * j + 8), v("SH", 48 * j + 5, 48 * j + 48, 6), OFF, OP.add)
            at_a = lambda win: ind(v(win, 0, 3072), v("AU2", 8 * j, 8 * j + 8))
            add("SV"[j], v("AR", a, b), at_a("IDW"), -OFF)
            mm(v(bc, 0, 128), v("IDH"), v("AR", a, b), False, False)
            if not lastr: act(v("N1B", a, b), at_a("NXR"), scale=v("WA"))
            act(v("XA", a, b), at_a("X"))
            mm(n(bw, H2), v("IDP"), v("XA", a, b), False, True)
            act(v("XS", a, b), n(bw, H2), scale=0.5, bias=0.25)
            mm(n("P0", H2), v("ID4"), v("OH", a, b), True, False)
            mm(n("P0", H2), v("IDH"), v("AR", a, b), False, True)
            act(v("OHA", a, b), n("P0", H2), bias=OFF - 4096.0)
            if lastr: places(t, j)
            for p in range(8):
                c, h = p // 4, p % 4
                o, w, m, e = 64 * c, 16 * h + 16, 128 - 64 * c, 768 * j + 128 * p - 64 * c * h
                ts(v("EA", e, e + m), v("AR", a + o, b), v("SH", 48 * j + 6 * p + 5, 48 * j + 6 * p + 6), OP.is_equal)
                if c == 0: mm(v(bc, 64, 128), v("BB4"), v("EA", e + 64, e + m), False, False)
                mm(v(bc, o, o + w), v("TR"), v("EA", e, e + w), False, p == 7)
                if h < 3: mm(v(bc, o + w, o + 64), v("TRE"), v("EA", e + w, e + 64), False, False)
                join(-(1 + (c == 0) + (h < 3)))
            scan(v("CS", a, b), v("D0", a, b), v(bc, 0, 128), 0.0, OP.mult, OP.max)
            tt(v("OFA", 8 * j, 8 * j + 8), v("CS", a + 15, b, 16), v("DUA", 8 * j, 8 * j + 8), OP.min)
        cp(ind(v("X"), v("OFA", 8, 16)), v("XS", 128, 256))
        scan(v("SR"), v("DR"), v("G6"), 0.0, OP.add, OP.mult)
        ts(v(MW), v("SR", 5, 96, 6), OFF, OP.add)
        remote("w", t, lambda h: v(Vn, 16 * h - 16, 16 * h), lambda h: v(MW))
        if lastr:
            dma(T.yu[:], v("ULF", 0, 1536))
            for h in range(4):
                gcp(v("YQ", h, 256, 4), v(Qn, 64 * h, 64 * h + 64))
            dma(T.yq[:], v("YQ"), "act")
        if first and DEEP:
            steps(*range(len(STEPS)))
            for a in (3, 4, 10, 11): dma(rows("PW", a - 2), rows("W1", a))
        if not lastr:
            turn(n("TE"), v("N1B"))
            unturn("P6", H4, [("", "TE", 6, 0, 1), ("", "TE", 7, 0, 1)])
            act(v("N1U"), n("P6", H4, A, 0))
            act(v("NNB"), ind(v("NXR", 0, 3072), v("N1U")))
            cp(ind(v("NXR"), v("OFA", 8, 16)), v("NNB", 128, 256))
            repeat([v(Qn if h else ZB, 64 * h, 64 * h + 64) for h in range(4)], ("QA", "QB")[1 - t % 2])
    cp(ind(v("X"), v("OFA", 0, 8)), v("XS", 0, 128))
    dma(T.yx[:], v("X", 0, 3072))
    lay(NR, "S")
    act(v("YG"), ind(v("IDW"), v("VC", 16 * NR, 16 * NR + 16)))
    for h in range(4):
        act(v("YR", h, 256, 4), v("YG", 64 * h, 64 * h + 64))
    dma(T.yv[:], rows("YR", 5, 0, 256), "act")
    if not PLAN: PLAN.extend(arrange(calls))
    for k in PLAN:
        if calls[k][6]: calls[k][6]()
    for q in ("V", "S", "P", "G"):
        g.wait_ge(T.sem["q" + q], cnt[q])
    for nm in sorted(total):
        g.wait_ge(T.sem[nm], unit[nm])
    g.wait_ge(T.sem.sent, sent[0])
